import numpy as np
import ml_dtypes


def mxq(x, axis, fmt="e4m3"):
    dtype, down = {"e4m3": (ml_dtypes.float8_e4m3fn, 7), "e5m2": (ml_dtypes.float8_e5m2, 14)}[fmt]
    v = np.moveaxis(np.asarray(x, np.float32).astype(ml_dtypes.bfloat16).astype(np.float64), axis, -1)
    blocks = v.reshape(v.shape[:-1] + (-1, 32))
    amax = np.abs(blocks).max(-1, keepdims=True)
    byte = np.maximum(np.where(amax > 0, np.frexp(amax)[1] - 1 + 127, 0) - down, 1)
    scale = np.exp2(byte - 127.0)
    codes = (blocks / scale).astype(np.float32).astype(dtype).astype(np.float64)
    return np.moveaxis((codes * scale).reshape(v.shape), -1, axis)


WIDE = False


def mx_kscale(k):
    if not WIDE:
        return np.ones(k)
    levels = np.array([10, -10, 5, -5, 0])
    if k % 512:
        return np.exp2(np.random.permutation(np.resize(levels, k // 32))).repeat(32)
    a = np.empty((k // 512, 16))
    for p in range(k // 512):
        a[p, :8] = np.random.permutation(np.resize(levels, 8))
        for g in range(8):
            far = levels[np.abs(levels - a[p, g]) >= 10]
            a[p, g + 8] = far[np.random.randint(len(far))]
    return np.exp2(a.ravel()).repeat(32)


BF16 = ml_dtypes.bfloat16


def bf(x):
    return np.asarray(x, np.float32).astype(BF16)


def f64(x):
    return np.asarray(x).astype(np.float64)


E2M1 = np.array([0.0, 0.5, 1.0, 1.5, 2.0, 3.0, 4.0, 6.0, -0.0, -0.5, -1.0, -1.5, -2.0, -3.0, -4.0, -6.0])


def pack_weight(w, fmt):
    k, n = w.shape
    w = f64(bf(w)).reshape(k // 32, 32, n)
    amax = np.abs(w).max(1)
    if fmt == "e4m3":
        byte = np.frexp(amax)[1] - 1 + 127 - 7
    else:
        mant, ex = np.frexp(amax / 6.0)
        byte = np.where(mant > 0.5, ex, ex - 1) + 127
    byte = np.clip(np.where(amax > 0, byte, 1), 1, 254)
    scaled = (w * np.exp2(127.0 - byte)[:, None, :]).reshape(k, n).astype(np.float32)
    by_word = np.ascontiguousarray(scaled.reshape(k // 512, 128, 4, n).transpose(0, 1, 3, 2))
    if fmt == "e4m3":
        words = by_word.astype(ml_dtypes.float8_e4m3fn).view(np.uint8)
    else:
        c = by_word.astype(ml_dtypes.float4_e2m1fn).view(np.uint8) & 0xF
        words = c[..., 0::2] | (c[..., 1::2] << 4)
    return np.ascontiguousarray(words), np.ascontiguousarray(byte.astype(np.uint8).reshape(k // 512, 16, n))


def unpack_weight(words, scales, fmt):
    g, p, n, _ = words.shape
    if fmt == "e4m3":
        vals = np.ascontiguousarray(words).view(ml_dtypes.float8_e4m3fn).astype(np.float64)
    else:
        nib = np.empty((g, p, n, 4), np.uint8)
        nib[..., 0::2] = words & 0xF
        nib[..., 1::2] = words >> 4
        vals = E2M1[nib]
    vals = vals * np.repeat(np.exp2(scales.astype(np.float64) - 127.0), 8, axis=1)[..., None]
    return vals.transpose(0, 1, 3, 2).reshape(g * 512, n)
def pack4(w):
    words, scales = pack_weight(w, "e2m1")
    return words.reshape(words.shape[0], 128, -1), scales


def unpack4(words, scales):
    return unpack_weight(words.reshape(words.shape[0], 128, -1, 2), scales, "e2m1")


M, K, N, G = 1024, 2048, 512, 64


def setup_inputs():
    s, v, m = mx_kscale(K), mx_kscale(K), mx_kscale(M)
    ga = np.kron(np.exp(0.8 * np.random.standard_normal((M // G, K // G))), np.ones((G, G)))
    gx = np.kron(np.exp(0.8 * np.random.standard_normal((K // G, N // G))), np.ones((G, G)))
    xt = gx * np.random.standard_normal((K, N))
    err = ga * np.random.standard_normal((M, K)) * 0.05 / np.sqrt(K)
    mag = ga * np.abs(np.random.standard_normal((M, K))) * np.exp(1.2 * np.random.standard_normal((M, K))) * 6.0 / K
    u_words, u_scales = pack4(np.ascontiguousarray((mag * v * m[:, None]).T))
    v_words, v_scales = pack4(np.abs(xt) / v[:, None])
    return {"e": bf(err * s * m[:, None]),
            "x": bf(xt / s[:, None]),
            "u_words": u_words, "u_scales": u_scales,
            "v_words": v_words, "v_scales": v_scales,
            "b_abs": bf(3.0 * np.abs(np.random.standard_normal((M, N))) * m[:, None])}


def reference(e, x, u_words, u_scales, v_words, v_scales, b_abs):
    r = np.abs(mxq(f64(e), 1, "e4m3") @ mxq(f64(x), 0, "e4m3"))
    d = (unpack4(u_words, u_scales).T @ unpack4(v_words, v_scales)) + f64(b_abs)
    w = 1.0 / d
    return mxq(r, 0, "e4m3").T @ mxq(w, 0, "e4m3")

@@ -1,0 +1,253 @@
+from contextlib import ExitStack
+
+import concourse.mybir as mybir
+from concourse.masks import make_identity
+
+M, K, N = 1024, 2048, 512
+FLOPS = 2 * (2 * M * K * N) + 2 * M * N * N
+
+F32 = mybir.dt.float32
+BF16 = mybir.dt.bfloat16
+I32 = mybir.dt.int32
+U32 = mybir.dt.uint32
+U8 = mybir.dt.uint8
+FP8X4 = mybir.dt.float8_e4m3fn_x4
+FP4X4 = mybir.dt.float4_e2m1fn_x4
+ACT = mybir.ActivationFunctionType
+ALU = mybir.AluOpType
+
+P = 128
+
+LOADS = "dE00 dE01 dE02 dE03 dU0a dVa dU0b dVb db0 dX0 dU1 dE10 dE11 dX1 dX2 dX3 dE12 dE13 db1".split()
+STEPS = "T00a:0 T00b:1 c00a:A T01a:2 c00b:A T01b:3 c01a:A T02a:4 qE00:V T02b:5 pS0:V c01b:V T03a:6 c02b:A T03b:7 pU0a:V c03a:A pS1:V A0:0 c03b:A pU0b:V c02a:V D00:0 A1:1 a00:V D01:1 r00:A A2:2 a01:V D02:2 r01:A pU1:V A3:3 iX0:A a02:V qE01:V D03:3 qE02:V T10a:4 a03:V T10b:5 qE03:V c10a:A T11a:6 c10b:A qX0:V T11b:7 c11a:A iX1:V D10:0 iX2:A D11:1 iX3:V D12:2 qX1:V r02:A qX2:V r03:A T12a:3 qE10:V T12b:4 c11b:A qX3:V T13a:5 c12a:A a10:V T13b:6 s00:A a11:V D13:7 r10:A a12:V c12b:A c13a:V R00:0 c13b:A a13:V s03:A qE11:V R01:1 r11:A qE12:V b00:A s01:V R02:2 b01:A qR00:V qE13:V r12:A R03:3 qR01:V s02:V b02:A r13:A qR02:V R10:4 qW0:V b03:A s11:V s10:A R11:5 s13:V s12:A qR03:V b10:A R12:6 qW1:V b11:A qR10:V S00:7 qR11:V b12:A S10:7 R13:0 o0:V qR12:V S01:1 b13:A S11:1 S02:2 dO0:S o1:A S12:2 qR13:V S03:3 o2:V S13:3 o3:A dO1:S dO2:S dO3:S".split()
+
+
+def tile_cross_backward_error_s12_kernel(tc, e, x, u_words, u_scales, v_words, v_scales, b_abs, out):
+    nc = tc.nc
+    with ExitStack() as ctx:
+        keep = ctx.enter_context(tc.tile_pool(name="keep", bufs=1))
+        psum = ctx.enter_context(tc.psum_pool(name="psum", bufs=1))
+
+        def sb(name, shape, dtype):
+            return keep.tile(shape, dtype, name=name, align_bytes=64)
+
+        def grid(name, a, b, shape, dtype):
+            return [[sb("%s%d%d" % (name, i, j), shape, dtype) for j in range(b)] for i in range(a)]
+
+        def row(name, a, shape, dtype):
+            return [sb("%s%d" % (name, i), shape, dtype) for i in range(a)]
+
+        ident = sb("ident", [P, P], F32)
+        perm = sb("perm", [P, P], F32)
+        warm = sb("warm", [P, 2], F32)
+        e_raw = grid("e_raw", 2, 4, [P, 4, 512], BF16)
+        e_grp = grid("e_grp", 2, 4, [P, 2048], BF16)
+        e_codes = grid("e_codes", 2, 4, [P, 512], U32)
+        e_sc = grid("e_sc", 2, 4, [P, 512], U8)
+        x_raw = row("x_raw", 4, [P, 4, 512], BF16)
+        x_grp = row("x_grp", 4, [P, 512, 4], BF16)
+        x_codes = row("x_codes", 4, [P, 512], U32)
+        x_sc = row("x_sc", 4, [P, 512], U8)
+        u_raw = grid("u_raw", 2, 2, [P, 2, 1024], U8)
+        u_w = grid("u_w", 2, 2, [P, 2, 1024], U8)
+        us_raw = sb("us_raw", [P, 4, 1024], U8)
+        us = row("us", 2, [P, 4, 512], U8)
+        v_w = row("v_w", 2, [P, 2, 1024], U8)
+        vs = sb("vs", [P, 4, 512], U8)
+        b_sb = row("b_sb", 2, [P, 4, 512], BF16)
+        d_sb = row("d_sb", 2, [P, 4, 512], F32)
+        w_bf = row("w_bf", 2, [P, 512, 4], BF16)
+        w_codes = row("w_codes", 2, [P, 512], U32)
+        w_sc = row("w_sc", 2, [P, 512], U8)
+        r_bf = grid("r_bf", 2, 4, [P, P, 4], BF16)
+        r_codes = grid("r_codes", 2, 4, [P, P], U32)
+        r_sc = grid("r_sc", 2, 4, [P, P], U8)
+        o_sb = row("o_sb", 4, [P, 512], F32)
+
+        ctx.enter_context(tc.manual_schedule())
+
+        nc.vector.memset(us_raw[:].rearrange("p g n -> p (g n)").bitcast(I32), 0)
+        nc.vector.memset(vs[:].rearrange("p g n -> p (g n)").bitcast(I32), 0)
+        nc.vector.memset(warm[:], 1.0)
+        make_identity(nc, ident[:])
+
+        def load(name):
+            if name[1] == "E":
+                h, g = int(name[2]), int(name[3])
+                src = e[512 * h : 512 * (h + 1), 512 * g : 512 * (g + 1)]
+                nc.sync.dma_start(out=e_raw[h][g][:], in_=src.rearrange("(j p) k -> p j k", p=P))
+            elif name[1] == "X":
+                g = int(name[2])
+                nc.sync.dma_start(out=x_raw[g][:], in_=x[512 * g : 512 * (g + 1), :].rearrange("(p j) n -> p j n", j=4))
+            elif name[1] == "V":
+                a = "ab".index(name[2])
+                src = v_words[2 * a : 2 * a + 2].rearrange("g p n -> p g n")
+                nc.sync.dma_start(out=v_w[a][:].bitcast(I32), in_=src.bitcast(I32))
+            elif name[1] == "U":
+                h = int(name[2])
+                for a in ["ab".index(name[3])] if len(name) > 3 else [0, 1]:
+                    src = u_words[2 * a : 2 * a + 2, :, 1024 * h : 1024 * (h + 1)].rearrange("g p n -> p g n")
+                    nc.sync.dma_start(out=u_raw[h][a][:].bitcast(I32), in_=src.bitcast(I32))
+            else:
+                h = int(name[2])
+                rows = b_abs[512 * h : 512 * (h + 1), :].rearrange("(q t s) n -> s q t n", t=4, s=4)
+                for s in range(4):
+                    nc.sync.dma_start(out=b_sb[h][s:P:4], in_=rows[s])
+
+        for name in LOADS[:4]:
+            load(name)
+        for r in range(4):
+            src = u_scales[:, r:16:4, :].rearrange("g q n -> q g n")
+            nc.gpsimd.dma_start(out=us_raw[r:P:32].bitcast(I32), in_=src.bitcast(I32))
+        for r in range(4):
+            src = v_scales[:, r:16:4, :].rearrange("g q n -> q g n")
+            nc.scalar.dma_start(out=vs[r:P:32].bitcast(I32), in_=src.bitcast(I32))
+        for name in LOADS[4:]:
+            load(name)
+
+        nc.scalar.activation(out=warm[:, 1:2], in_=warm[:, 0:1], func=ACT.Abs_reciprocal_sqrt)
+        nc.vector.tensor_copy(
+            out=perm[:].rearrange("p (t q s) -> p t q s", t=4, s=4),
+            in_=ident[:].rearrange("p (q t s) -> p t q s", t=4, s=4),
+        )
+
+        banks = {}
+
+        def new_bank(key, bank):
+            banks[key] = psum.tile([P, 512], F32, name="ps_" + key, tag="bank%d" % bank)
+            return banks[key]
+
+        def copy(eng, dst, src):
+            if eng == "V":
+                nc.vector.tensor_copy(out=dst, in_=src)
+            else:
+                nc.scalar.copy(out=dst, in_=src)
+
+        def d_passes(acc, h, t, passes):
+            for g in passes:
+                nc.tensor.matmul_mx(
+                    out=acc[:],
+                    lhsT=u_w[h][g // 2][:, g % 2, 256 * t : 256 * (t + 1)].bitcast(FP4X4),
+                    lhsT_scale=us[h][:, g, P * t : P * (t + 1)],
+                    rhs=v_w[g // 2][:, g % 2, :].bitcast(FP4X4),
+                    rhs_scale=vs[:, g, :],
+                    start=(g == 0),
+                    stop=(g == 3),
+                )
+
+        def permute_u(h, a):
+            nc.vector.tensor_copy(
+                out=u_w[h][a][:].bitcast(I32).rearrange("p g (t q s) -> p g t q s", t=4, s=2),
+                in_=u_raw[h][a][:].bitcast(I32).rearrange("p g (q t s) -> p g t q s", t=4, s=2),
+            )
+
+        def step(name, arg):
+            kind = name[0]
+            if kind == "T":
+                h, g, pair = int(name[1]), int(name[2]), "ab".index(name[3])
+                bank = new_bank(name, int(arg))
+                words = e_raw[h][g][:].rearrange("p j k -> p (j k)").bitcast(F32)
+                for jj in range(2):
+                    j = 2 * pair + jj
+                    for u in range(2):
+                        o = P * (2 * jj + u)
+                        nc.tensor.transpose(bank[:, o : o + P], words[:, 256 * j + u : 256 * (j + 1) : 2], perm[:])
+            elif kind == "c":
+                h, g, pair = int(name[1]), int(name[2]), "ab".index(name[3])
+                dst = e_grp[h][g][:].bitcast(F32).rearrange("p (t j c u) -> p j t c u", t=4, j=4, u=2)
+                src = banks["T" + name[1:]][:].rearrange("p (j u t c) -> p j t c u", j=2, u=2, t=4)
+                copy(arg, dst[:, 2 * pair : 2 * pair + 2], src)
+            elif kind == "A":
+                t = int(name[1])
+                d_passes(new_bank("D0%d" % t, int(arg)), 0, t, (0, 1))
+            elif kind == "D":
+                h, t = int(name[1]), int(name[2])
+                if h == 0:
+                    d_passes(banks[name], 0, t, (2, 3))
+                else:
+                    d_passes(new_bank(name, int(arg)), 1, t, (0, 1, 2, 3))
+            elif kind == "R":
+                h, c = int(name[1]), int(name[2])
+                bank = new_bank(name, int(arg))
+                cols = slice(P * c, P * (c + 1))
+                for t in range(4):
+                    rows = slice(P * t, P * (t + 1))
+                    for g in range(4):
+                        nc.tensor.matmul_mx(
+                            out=bank[:, rows],
+                            lhsT=e_codes[h][g][:, rows].bitcast(FP8X4),
+                            lhsT_scale=e_sc[h][g][:, rows],
+                            rhs=x_codes[g][:, cols].bitcast(FP8X4),
+                            rhs_scale=x_sc[g][:, cols],
+                            start=(g == 0),
+                            stop=(g == 3),
+                        )
+            elif kind == "S":
+                h, c = int(name[1]), int(name[2])
+                acc = new_bank("S%d" % c, int(arg)) if h == 0 else banks["S%d" % c]
+                nc.tensor.matmul_mx(
+                    out=acc[:],
+                    lhsT=r_codes[h][c][:].bitcast(FP8X4),
+                    lhsT_scale=r_sc[h][c][:],
+                    rhs=w_codes[h][:].bitcast(FP8X4),
+                    rhs_scale=w_sc[h][:],
+                    start=(h == 0),
+                    stop=(h == 1),
+                )
+            elif name[:2] == "pU":
+                h = int(name[2])
+                for a in ["ab".index(name[3])] if len(name) > 3 else [0, 1]:
+                    permute_u(h, a)
+            elif name[:2] == "pS":
+                h = int(name[2])
+                nc.vector.tensor_copy(
+                    out=us[h][:].bitcast(I32).rearrange("p g (t q) -> p g t q", t=4),
+                    in_=us_raw[:, :, 512 * h : 512 * (h + 1)].bitcast(I32).rearrange("p g (q t) -> p g t q", t=4),
+                )
+            elif name[:2] == "iX":
+                g = int(name[2])
+                copy(
+                    arg,
+                    x_grp[g][:].rearrange("p (c i) t -> p c t i", i=4),
+                    x_raw[g][:].rearrange("p t (c i) -> p c t i", i=4),
+                )
+            elif name[:2] == "qX":
+                g = int(name[2])
+                nc.vector.quantize_mx(out=x_codes[g][:].bitcast(FP8X4), scales=x_sc[g][:], in_=x_grp[g][:].rearrange("p n t -> p (n t)"))
+            elif name[:2] == "qE":
+                h, g = int(name[2]), int(name[3])
+                nc.vector.quantize_mx(out=e_codes[h][g][:].bitcast(FP8X4), scales=e_sc[h][g][:], in_=e_grp[h][g][:])
+            elif name[:2] == "qR":
+                h, c = int(name[2]), int(name[3])
+                nc.vector.quantize_mx(out=r_codes[h][c][:].bitcast(FP8X4), scales=r_sc[h][c][:], in_=r_bf[h][c][:].rearrange("p n t -> p (n t)"))
+            elif name[:2] == "qW":
+                h = int(name[2])
+                nc.vector.quantize_mx(out=w_codes[h][:].bitcast(FP8X4), scales=w_sc[h][:], in_=w_bf[h][:].rearrange("p n t -> p (n t)"))
+            elif kind == "a":
+                h, t = int(name[1]), int(name[2])
+                nc.vector.tensor_tensor(out=d_sb[h][:, t, :], in0=banks["D" + name[1:]][:], in1=b_sb[h][:, t, :], op=ALU.add)
+            elif kind == "r":
+                h, t = int(name[1]), int(name[2])
+                nc.scalar.activation(out=d_sb[h][:, t, :], in_=d_sb[h][:, t, :], func=ACT.Abs_reciprocal_sqrt)
+            elif kind == "s":
+                h, c = int(name[1]), int(name[2])
+                src = d_sb[h][:, :, P * c : P * (c + 1)].rearrange("p t n -> p n t")
+                dst = w_bf[h][:, P * c : P * (c + 1), :]
+                if arg == "V":
+                    nc.vector.tensor_tensor(out=dst, in0=src, in1=src, op=ALU.mult)
+                else:
+                    nc.scalar.activation(out=dst, in_=src, func=ACT.Square)
+            elif kind == "b":
+                h, c = int(name[1]), int(name[2])
+                src = banks["R" + name[1:]][:].rearrange("p (t n) -> p n t", t=4)
+                nc.scalar.activation(out=r_bf[h][c][:], in_=src, func=ACT.Abs)
+            elif kind == "o":
+                c = int(name[1])
+                copy(arg, o_sb[c][:], banks["S%d" % c][:])
+            else:
+                c = int(name[2])
+                nc.sync.dma_start(out=out[P * c : P * (c + 1), :], in_=o_sb[c][:])
+
+        for item in STEPS:
+            name, arg = item.split(":")
+            step(name, arg)

@@ -18,8 +18,8 @@ ALU = mybir.AluOpType
 
 P = 128
 
-LOADS = "dE00 dE01 dE02 dE03 dU0a dVa dU0b dVb db0 dX0 dU1 dE10 dE11 dX1 dX2 dX3 dE12 dE13 db1".split()
-STEPS = "T00a:0 T00b:1 c00a:A T01a:2 c00b:A T01b:3 c01a:A T02a:4 qE00:V T02b:5 pS0:V c01b:V T03a:6 c02b:A T03b:7 pU0a:V c03a:A pS1:V A0:0 c03b:A pU0b:V c02a:V D00:0 A1:1 a00:V D01:1 r00:A A2:2 a01:V D02:2 r01:A pU1:V A3:3 iX0:A a02:V qE01:V D03:3 qE02:V T10a:4 a03:V T10b:5 qE03:V c10a:A T11a:6 c10b:A qX0:V T11b:7 c11a:A iX1:V D10:0 iX2:A D11:1 iX3:V D12:2 qX1:V r02:A qX2:V r03:A T12a:3 qE10:V T12b:4 c11b:A qX3:V T13a:5 c12a:A a10:V T13b:6 s00:A a11:V D13:7 r10:A a12:V c12b:A c13a:V R00:0 c13b:A a13:V s03:A qE11:V R01:1 r11:A qE12:V b00:A s01:V R02:2 b01:A qR00:V qE13:V r12:A R03:3 qR01:V s02:V b02:A r13:A qR02:V R10:4 qW0:V b03:A s11:V s10:A R11:5 s13:V s12:A qR03:V b10:A R12:6 qW1:V b11:A qR10:V S00:7 qR11:V b12:A S10:7 R13:0 o0:V qR12:V S01:1 b13:A S11:1 S02:2 dO0:S o1:A S12:2 qR13:V S03:3 o2:V S13:3 o3:A dO1:S dO2:S dO3:S".split()
+LOADS = "dE00 du00 du01 du02 du03 dE01 dE02 dE03 dU0a dv0 dv1 dv2 dv3 dVa dU0b dVb db00 db01 db02 db03 dX0 dE10 dU1 dE11 du10 du11 du12 du13 dX1 dX2 dE12 dX3 dE13 db10 db11 db12 db13".split()
+STEPS = "T00a:0 T00b:1 c00a:A c00b:A T01a:2 T01b:3 c01a:A T02a:4 c01b:A T02b:5 c02a:V T03a:6 c02b:V T03b:7 c03a:A pU0a:V pS0:V qE00:V A0:0 pU0b:V c03b:V A1:1 qE01:V qE02:V D00:0 A2:2 a00:V D01:1 iX0:V r00:A D02:2 A3:3 a01:V D03:3 a02:V r01:A T10a:4 a03:V T10b:5 r02:A pU1:V T11a:6 c10a:A pS1:V T11b:7 c10b:A qX0:V c11a:A D10:0 iX1:V r03:A D11:1 iX2:A qE03:V c11b:V D12:2 qX1:V T12a:3 iX3:V s00:A T12b:4 c12a:A T13a:5 qX2:V c12b:A T13b:6 qX3:V s01:A D13:7 a10:V c13a:A a11:V r10:A R00:0 qE10:V c13b:A a12:V s02:A R01:1 qE11:V r11:A a13:V r12:A R02:2 s03:V r13:A qE12:V b00:A R03:3 qE13:V b01:A s10:V s12:A R10:4 qR00:V s13:A s11:V R11:5 b02:A qW0:V b03:A qR01:V qR02:V b10:A R12:6 qR03:V qW1:V b11:A qR10:V R13:7 qR11:V b12:A qR12:V S00:0 b13:A S10:0 S01:1 o0:A S11:1 qR13:V S02:2 o1:A S12:2 S03:3 o2:V S13:3 dO0:S o3:A dO1:S dO2:S dO3:S".split()
 
 
 def tile_cross_backward_error_s12_kernel(tc, e, x, u_words, u_scales, v_words, v_scales, b_abs, out):
@@ -40,16 +40,16 @@ def tile_cross_backward_error_s12_kernel(tc, e, x, u_words, u_scales, v_words, v
         ident = sb("ident", [P, P], F32)
         perm = sb("perm", [P, P], F32)
         warm = sb("warm", [P, 2], F32)
-        e_raw = grid("e_raw", 2, 4, [P, 4, 512], BF16)
-        e_grp = grid("e_grp", 2, 4, [P, 2048], BF16)
+        e_raw = grid("e_raw", 2, 4, [P, 2048], BF16)
+        e_grp = grid("e_grp", 2, 2, [P, 2, 2048], BF16)
         e_codes = grid("e_codes", 2, 4, [P, 512], U32)
         e_sc = grid("e_sc", 2, 4, [P, 512], U8)
         x_raw = row("x_raw", 4, [P, 4, 512], BF16)
         x_grp = row("x_grp", 4, [P, 512, 4], BF16)
         x_codes = row("x_codes", 4, [P, 512], U32)
         x_sc = row("x_sc", 4, [P, 512], U8)
-        u_raw = grid("u_raw", 2, 2, [P, 2, 1024], U8)
-        u_w = grid("u_w", 2, 2, [P, 2, 1024], U8)
+        u_raw = row("u_raw", 2, [P, 4, 1024], U8)
+        u_w = row("u_w", 2, [P, 4, 1024], U8)
         us_raw = sb("us_raw", [P, 4, 1024], U8)
         us = row("us", 2, [P, 4, 512], U8)
         v_w = row("v_w", 2, [P, 2, 1024], U8)
@@ -71,11 +71,23 @@ def tile_cross_backward_error_s12_kernel(tc, e, x, u_words, u_scales, v_words, v
         nc.vector.memset(warm[:], 1.0)
         make_identity(nc, ident[:])
 
+        def passes_of(name):
+            return {"a": slice(0, 2), "b": slice(2, 4)}.get(name[-1], slice(0, 4))
+
         def load(name):
             if name[1] == "E":
-                h, g = int(name[2]), int(name[3])
-                src = e[512 * h : 512 * (h + 1), 512 * g : 512 * (g + 1)]
-                nc.sync.dma_start(out=e_raw[h][g][:], in_=src.rearrange("(j p) k -> p j k", p=P))
+                h, j = int(name[2]), int(name[3])
+                m0 = 512 * h + P * j
+                nc.sync.dma_start(out=e_raw[h][j][:], in_=e[m0 : m0 + P, :])
+            elif name[1] == "u":
+                r = int(name[3])
+                cols = slice(512 * int(name[2]), 512 * (int(name[2]) + 1)) if "du10" in LOADS else slice(0, 1024)
+                src = u_scales[:, r:16:4, cols].rearrange("g q n -> q g n")
+                nc.sync.dma_start(out=us_raw[r:P:32, :, cols].bitcast(I32), in_=src.bitcast(I32))
+            elif name[1] == "v":
+                r = int(name[2])
+                src = v_scales[:, r:16:4, :].rearrange("g q n -> q g n")
+                nc.sync.dma_start(out=vs[r:P:32].bitcast(I32), in_=src.bitcast(I32))
             elif name[1] == "X":
                 g = int(name[2])
                 nc.sync.dma_start(out=x_raw[g][:], in_=x[512 * g : 512 * (g + 1), :].rearrange("(p j) n -> p j n", j=4))
@@ -85,24 +97,16 @@ def tile_cross_backward_error_s12_kernel(tc, e, x, u_words, u_scales, v_words, v
                 nc.sync.dma_start(out=v_w[a][:].bitcast(I32), in_=src.bitcast(I32))
             elif name[1] == "U":
                 h = int(name[2])
-                for a in ["ab".index(name[3])] if len(name) > 3 else [0, 1]:
-                    src = u_words[2 * a : 2 * a + 2, :, 1024 * h : 1024 * (h + 1)].rearrange("g p n -> p g n")
-                    nc.sync.dma_start(out=u_raw[h][a][:].bitcast(I32), in_=src.bitcast(I32))
+                gs = passes_of(name)
+                src = u_words[gs, :, 1024 * h : 1024 * (h + 1)].rearrange("g p n -> p g n")
+                nc.sync.dma_start(out=u_raw[h][:, gs].bitcast(I32), in_=src.bitcast(I32))
             else:
                 h = int(name[2])
                 rows = b_abs[512 * h : 512 * (h + 1), :].rearrange("(q t s) n -> s q t n", t=4, s=4)
-                for s in range(4):
-                    nc.sync.dma_start(out=b_sb[h][s:P:4], in_=rows[s])
+                s = int(name[3])
+                nc.sync.dma_start(out=b_sb[h][s:P:4], in_=rows[s])
 
-        for name in LOADS[:4]:
-            load(name)
-        for r in range(4):
-            src = u_scales[:, r:16:4, :].rearrange("g q n -> q g n")
-            nc.gpsimd.dma_start(out=us_raw[r:P:32].bitcast(I32), in_=src.bitcast(I32))
-        for r in range(4):
-            src = v_scales[:, r:16:4, :].rearrange("g q n -> q g n")
-            nc.scalar.dma_start(out=vs[r:P:32].bitcast(I32), in_=src.bitcast(I32))
-        for name in LOADS[4:]:
+        for name in LOADS:
             load(name)
 
         nc.scalar.activation(out=warm[:, 1:2], in_=warm[:, 0:1], func=ACT.Abs_reciprocal_sqrt)
@@ -127,7 +131,7 @@ def tile_cross_backward_error_s12_kernel(tc, e, x, u_words, u_scales, v_words, v
             for g in passes:
                 nc.tensor.matmul_mx(
                     out=acc[:],
-                    lhsT=u_w[h][g // 2][:, g % 2, 256 * t : 256 * (t + 1)].bitcast(FP4X4),
+                    lhsT=u_w[h][:, g, 256 * t : 256 * (t + 1)].bitcast(FP4X4),
                     lhsT_scale=us[h][:, g, P * t : P * (t + 1)],
                     rhs=v_w[g // 2][:, g % 2, :].bitcast(FP4X4),
                     rhs_scale=vs[:, g, :],
@@ -135,28 +139,28 @@ def tile_cross_backward_error_s12_kernel(tc, e, x, u_words, u_scales, v_words, v
                     stop=(g == 3),
                 )
 
-        def permute_u(h, a):
+        def permute_u(h, gs):
             nc.vector.tensor_copy(
-                out=u_w[h][a][:].bitcast(I32).rearrange("p g (t q s) -> p g t q s", t=4, s=2),
-                in_=u_raw[h][a][:].bitcast(I32).rearrange("p g (q t s) -> p g t q s", t=4, s=2),
+                out=u_w[h][:, gs].bitcast(I32).rearrange("p g (t q s) -> p g t q s", t=4, s=2),
+                in_=u_raw[h][:, gs].bitcast(I32).rearrange("p g (q t s) -> p g t q s", t=4, s=2),
             )
 
         def step(name, arg):
             kind = name[0]
             if kind == "T":
-                h, g, pair = int(name[1]), int(name[2]), "ab".index(name[3])
+                h, j, pair = int(name[1]), int(name[2]), "ab".index(name[3])
                 bank = new_bank(name, int(arg))
-                words = e_raw[h][g][:].rearrange("p j k -> p (j k)").bitcast(F32)
-                for jj in range(2):
-                    j = 2 * pair + jj
+                words = e_raw[h][j][:].bitcast(F32)
+                for gg in range(2):
+                    g = 2 * pair + gg
                     for u in range(2):
-                        o = P * (2 * jj + u)
-                        nc.tensor.transpose(bank[:, o : o + P], words[:, 256 * j + u : 256 * (j + 1) : 2], perm[:])
+                        o = P * (2 * gg + u)
+                        nc.tensor.transpose(bank[:, o : o + P], words[:, 256 * g + u : 256 * (g + 1) : 2], perm[:])
             elif kind == "c":
-                h, g, pair = int(name[1]), int(name[2]), "ab".index(name[3])
-                dst = e_grp[h][g][:].bitcast(F32).rearrange("p (t j c u) -> p j t c u", t=4, j=4, u=2)
-                src = banks["T" + name[1:]][:].rearrange("p (j u t c) -> p j t c u", j=2, u=2, t=4)
-                copy(arg, dst[:, 2 * pair : 2 * pair + 2], src)
+                h, j, pair = int(name[1]), int(name[2]), "ab".index(name[3])
+                dst = e_grp[h][pair][:].bitcast(F32).rearrange("p g (t j c u) -> p j g t c u", t=4, j=4, u=2)
+                src = banks["T" + name[1:]][:].rearrange("p (g u t c) -> p g t c u", g=2, u=2, t=4)
+                copy(arg, dst[:, j], src)
             elif kind == "A":
                 t = int(name[1])
                 d_passes(new_bank("D0%d" % t, int(arg)), 0, t, (0, 1))
@@ -195,9 +199,7 @@ def tile_cross_backward_error_s12_kernel(tc, e, x, u_words, u_scales, v_words, v
                     stop=(h == 1),
                 )
             elif name[:2] == "pU":
-                h = int(name[2])
-                for a in ["ab".index(name[3])] if len(name) > 3 else [0, 1]:
-                    permute_u(h, a)
+                permute_u(int(name[2]), passes_of(name))
             elif name[:2] == "pS":
                 h = int(name[2])
                 nc.vector.tensor_copy(
@@ -216,7 +218,7 @@ def tile_cross_backward_error_s12_kernel(tc, e, x, u_words, u_scales, v_words, v
                 nc.vector.quantize_mx(out=x_codes[g][:].bitcast(FP8X4), scales=x_sc[g][:], in_=x_grp[g][:].rearrange("p n t -> p (n t)"))
             elif name[:2] == "qE":
                 h, g = int(name[2]), int(name[3])
-                nc.vector.quantize_mx(out=e_codes[h][g][:].bitcast(FP8X4), scales=e_sc[h][g][:], in_=e_grp[h][g][:])
+                nc.vector.quantize_mx(out=e_codes[h][g][:].bitcast(FP8X4), scales=e_sc[h][g][:], in_=e_grp[h][g // 2][:, g % 2, :])
             elif name[:2] == "qR":
                 h, c = int(name[2]), int(name[3])
                 nc.vector.quantize_mx(out=r_codes[h][c][:].bitcast(FP8X4), scales=r_sc[h][c][:], in_=r_bf[h][c][:].rearrange("p n t -> p (n t)"))

@@ -17,9 +17,10 @@ ACT = mybir.ActivationFunctionType
 ALU = mybir.AluOpType
 
 P = 128
+WARM_PASSES = 26
 
-LOADS = "dE00 du00 du01 du02 du03 dE01 dE02 dE03 dU0a dv0 dv1 dv2 dv3 dVa dU0b dVb db00 db01 db02 db03 dX0 dE10 dU1 dE11 du10 du11 du12 du13 dX1 dX2 dE12 dX3 dE13 db10 db11 db12 db13".split()
-STEPS = "T00a:0 T00b:1 c00a:A c00b:A T01a:2 T01b:3 c01a:A T02a:4 c01b:A T02b:5 c02a:V T03a:6 c02b:V T03b:7 c03a:A pU0a:V pS0:V qE00:V A0:0 pU0b:V c03b:V A1:1 qE01:V qE02:V D00:0 A2:2 a00:V D01:1 iX0:V r00:A D02:2 A3:3 a01:V D03:3 a02:V r01:A T10a:4 a03:V T10b:5 r02:A pU1:V T11a:6 c10a:A pS1:V T11b:7 c10b:A qX0:V c11a:A D10:0 iX1:V r03:A D11:1 iX2:A qE03:V c11b:V D12:2 qX1:V T12a:3 iX3:V s00:A T12b:4 c12a:A T13a:5 qX2:V c12b:A T13b:6 qX3:V s01:A D13:7 a10:V c13a:A a11:V r10:A R00:0 qE10:V c13b:A a12:V s02:A R01:1 qE11:V r11:A a13:V r12:A R02:2 s03:V r13:A qE12:V b00:A R03:3 qE13:V b01:A s10:V s12:A R10:4 qR00:V s13:A s11:V R11:5 b02:A qW0:V b03:A qR01:V qR02:V b10:A R12:6 qR03:V qW1:V b11:A qR10:V R13:7 qR11:V b12:A qR12:V S00:0 b13:A S10:0 S01:1 o0:A S11:1 qR13:V S02:2 o1:A S12:2 S03:3 o2:V S13:3 dO0:S o3:A dO1:S dO2:S dO3:S".split()
+LOADS = "dU0a dVa du00 du01 du02 du03 dv0 dv1 dv2 dv3 dU0b dVb db00 db01 db02 db03 dE00 du10 du11 du12 du13 dU1 dX0 dE01 dX1 dE02 dE03 dX2 dE10 dE11 dX3 dE12 dE13 db10 db11 db12 db13".split()
+STEPS = "pU0a:V pS0:V A0:0 A1:1 pU0b:V A2:2 A3:3 D00:0 D01:1 a00:V D02:2 a01:V T00a:4 pS1:V T01a:5 c00a:A a02:V D03:3 c01a:A pU1:V a03:V D10:6 iX0:V r00:A T02a:7 qX0:V T03a:0 c02a:A iX1:V D11:1 r01:A c03a:V T00b:4 T01b:5 c00b:A qE00:V T02b:2 c01b:A qX1:V T03b:7 c02b:A qE01:V D12:0 c03b:A iX2:V s00:A T10a:4 T11a:3 qX2:V c10a:A T12a:5 c11a:A T13a:2 iX3:V c12a:A D13:7 s01:A qE02:V T10b:4 qX3:V c13a:A T11b:3 qE03:V c10b:A T12b:5 qE10:V c11b:A T13b:2 c12b:A a10:V R00:4 c13b:A qE11:V a11:V R01:3 b00:A a12:V a13:V R02:5 b01:A qE12:V r10:A R03:6 qE13:V qW0:V r11:A R10:2 s10:V R11:4 b02:A s11:V b03:A R12:3 b10:A qR00:V b11:A qR10:V R13:5 qW1:V b12:A qR11:V qR12:V S00:6 b13:A S10:6 S01:2 o0:A S11:2 qR13:V S02:4 S12:4 o1:A S03:1 o2:V S13:1 o3:A dO0:S dO1:S dO2:S dO3:S".split()
 
 
 def tile_cross_backward_error_s12_kernel(tc, e, x, u_words, u_scales, v_words, v_scales, b_abs, out):
@@ -39,8 +40,12 @@ def tile_cross_backward_error_s12_kernel(tc, e, x, u_words, u_scales, v_words, v
 
         ident = sb("ident", [P, P], F32)
         perm = sb("perm", [P, P], F32)
-        warm = sb("warm", [P, 2], F32)
-        e_raw = grid("e_raw", 2, 4, [P, 2048], BF16)
+        warm = sb("warm", [P, 512], BF16)
+        warm_out = sb("warm_out", [P, 1], F32)
+        warm_codes = sb("warm_codes", [P, P], U32)
+        warm_sc = sb("warm_sc", [P, P], U8)
+        y_sb = row("y_sb", 2, [P, 512, 4], F32)
+        e_raw = grid("e_raw", 2, 4, [P, 2, 1024], BF16)
         e_grp = grid("e_grp", 2, 2, [P, 2, 2048], BF16)
         e_codes = grid("e_codes", 2, 4, [P, 512], U32)
         e_sc = grid("e_sc", 2, 4, [P, 512], U8)
@@ -59,16 +64,17 @@ def tile_cross_backward_error_s12_kernel(tc, e, x, u_words, u_scales, v_words, v
         w_bf = row("w_bf", 2, [P, 512, 4], BF16)
         w_codes = row("w_codes", 2, [P, 512], U32)
         w_sc = row("w_sc", 2, [P, 512], U8)
-        r_bf = grid("r_bf", 2, 4, [P, P, 4], BF16)
-        r_codes = grid("r_codes", 2, 4, [P, P], U32)
-        r_sc = grid("r_sc", 2, 4, [P, P], U8)
+        r_bf = row("r_bf", 2, [P, 512, 4], BF16)
+        r_codes = row("r_codes", 2, [P, 512], U32)
+        r_sc = row("r_sc", 2, [P, 512], U8)
         o_sb = row("o_sb", 4, [P, 512], F32)
 
         ctx.enter_context(tc.manual_schedule())
 
+        nc.gpsimd.memset(warm[:], 1.0)
         nc.vector.memset(us_raw[:].rearrange("p g n -> p (g n)").bitcast(I32), 0)
+        nc.vector.quantize_mx(out=warm_codes[:].bitcast(FP8X4), scales=warm_sc[:], in_=warm[:])
         nc.vector.memset(vs[:].rearrange("p g n -> p (g n)").bitcast(I32), 0)
-        nc.vector.memset(warm[:], 1.0)
         make_identity(nc, ident[:])
 
         def passes_of(name):
@@ -76,9 +82,10 @@ def tile_cross_backward_error_s12_kernel(tc, e, x, u_words, u_scales, v_words, v
 
         def load(name):
             if name[1] == "E":
-                h, j = int(name[2]), int(name[3])
-                m0 = 512 * h + P * j
-                nc.sync.dma_start(out=e_raw[h][j][:], in_=e[m0 : m0 + P, :])
+                h, i = int(name[2]), int(name[3])
+                m0, k0 = 512 * h + 256 * (i % 2), 1024 * (i // 2)
+                src = e[m0 : m0 + 256, k0 : k0 + 1024].rearrange("(j p) k -> p j k", p=P)
+                nc.sync.dma_start(out=e_raw[h][i][:], in_=src)
             elif name[1] == "u":
                 r = int(name[3])
                 cols = slice(512 * int(name[2]), 512 * (int(name[2]) + 1)) if "du10" in LOADS else slice(0, 1024)
@@ -109,11 +116,23 @@ def tile_cross_backward_error_s12_kernel(tc, e, x, u_words, u_scales, v_words, v
         for name in LOADS:
             load(name)
 
-        nc.scalar.activation(out=warm[:, 1:2], in_=warm[:, 0:1], func=ACT.Abs_reciprocal_sqrt)
+        nc.scalar.activation(out=warm_out[:], in_=warm[:, 0:1], func=ACT.Abs_reciprocal_sqrt)
         nc.vector.tensor_copy(
             out=perm[:].rearrange("p (t q s) -> p t q s", t=4, s=4),
             in_=ident[:].rearrange("p (q t s) -> p t q s", t=4, s=4),
         )
+
+        warm_ps = psum.tile([P, 512], F32, name="ps_warm", tag="bank7")
+        for i in range(WARM_PASSES):
+            nc.tensor.matmul_mx(
+                out=warm_ps[:, P * (i % 4) : P * (i % 4 + 1)],
+                lhsT=warm_codes[:].bitcast(FP8X4),
+                lhsT_scale=warm_sc[:],
+                rhs=warm_codes[:].bitcast(FP8X4),
+                rhs_scale=warm_sc[:],
+                start=True,
+                stop=True,
+            )
 
         banks = {}
 
@@ -150,12 +169,11 @@ def tile_cross_backward_error_s12_kernel(tc, e, x, u_words, u_scales, v_words, v
             if kind == "T":
                 h, j, pair = int(name[1]), int(name[2]), "ab".index(name[3])
                 bank = new_bank(name, int(arg))
-                words = e_raw[h][j][:].bitcast(F32)
+                words = e_raw[h][2 * pair + j // 2][:, j % 2, :].bitcast(F32)
                 for gg in range(2):
-                    g = 2 * pair + gg
                     for u in range(2):
                         o = P * (2 * gg + u)
-                        nc.tensor.transpose(bank[:, o : o + P], words[:, 256 * g + u : 256 * (g + 1) : 2], perm[:])
+                        nc.tensor.transpose(bank[:, o : o + P], words[:, 256 * gg + u : 256 * (gg + 1) : 2], perm[:])
             elif kind == "c":
                 h, j, pair = int(name[1]), int(name[2]), "ab".index(name[3])
                 dst = e_grp[h][pair][:].bitcast(F32).rearrange("p g (t j c u) -> p j g t c u", t=4, j=4, u=2)
@@ -191,8 +209,8 @@ def tile_cross_backward_error_s12_kernel(tc, e, x, u_words, u_scales, v_words, v
                 acc = new_bank("S%d" % c, int(arg)) if h == 0 else banks["S%d" % c]
                 nc.tensor.matmul_mx(
                     out=acc[:],
-                    lhsT=r_codes[h][c][:].bitcast(FP8X4),
-                    lhsT_scale=r_sc[h][c][:],
+                    lhsT=r_codes[h][:, P * c : P * (c + 1)].bitcast(FP8X4),
+                    lhsT_scale=r_sc[h][:, P * c : P * (c + 1)],
                     rhs=w_codes[h][:].bitcast(FP8X4),
                     rhs_scale=w_sc[h][:],
                     start=(h == 0),
@@ -221,7 +239,8 @@ def tile_cross_backward_error_s12_kernel(tc, e, x, u_words, u_scales, v_words, v
                 nc.vector.quantize_mx(out=e_codes[h][g][:].bitcast(FP8X4), scales=e_sc[h][g][:], in_=e_grp[h][g // 2][:, g % 2, :])
             elif name[:2] == "qR":
                 h, c = int(name[2]), int(name[3])
-                nc.vector.quantize_mx(out=r_codes[h][c][:].bitcast(FP8X4), scales=r_sc[h][c][:], in_=r_bf[h][c][:].rearrange("p n t -> p (n t)"))
+                cols = slice(0, 512) if h == 0 else slice(P * c, P * (c + 1))
+                nc.vector.quantize_mx(out=r_codes[h][:, cols].bitcast(FP8X4), scales=r_sc[h][:, cols], in_=r_bf[h][:, cols, :].rearrange("p n t -> p (n t)"))
             elif name[:2] == "qW":
                 h = int(name[2])
                 nc.vector.quantize_mx(out=w_codes[h][:].bitcast(FP8X4), scales=w_sc[h][:], in_=w_bf[h][:].rearrange("p n t -> p (n t)"))
@@ -229,12 +248,13 @@ def tile_cross_backward_error_s12_kernel(tc, e, x, u_words, u_scales, v_words, v
                 h, t = int(name[1]), int(name[2])
                 nc.vector.tensor_tensor(out=d_sb[h][:, t, :], in0=banks["D" + name[1:]][:], in1=b_sb[h][:, t, :], op=ALU.add)
             elif kind == "r":
-                h, t = int(name[1]), int(name[2])
-                nc.scalar.activation(out=d_sb[h][:, t, :], in_=d_sb[h][:, t, :], func=ACT.Abs_reciprocal_sqrt)
+                h, c = int(name[1]), int(name[2])
+                cols = slice(256 * c, 256 * (c + 1))
+                nc.scalar.activation(out=y_sb[h][:, cols, :], in_=d_sb[h][:, :, cols].rearrange("p t n -> p n t"), func=ACT.Abs_reciprocal_sqrt)
             elif kind == "s":
                 h, c = int(name[1]), int(name[2])
-                src = d_sb[h][:, :, P * c : P * (c + 1)].rearrange("p t n -> p n t")
-                dst = w_bf[h][:, P * c : P * (c + 1), :]
+                src = y_sb[h][:, 256 * c : 256 * (c + 1), :]
+                dst = w_bf[h][:, 256 * c : 256 * (c + 1), :]
                 if arg == "V":
                     nc.vector.tensor_tensor(out=dst, in0=src, in1=src, op=ALU.mult)
                 else:
@@ -242,7 +262,7 @@ def tile_cross_backward_error_s12_kernel(tc, e, x, u_words, u_scales, v_words, v
             elif kind == "b":
                 h, c = int(name[1]), int(name[2])
                 src = banks["R" + name[1:]][:].rearrange("p (t n) -> p n t", t=4)
-                nc.scalar.activation(out=r_bf[h][c][:], in_=src, func=ACT.Abs)
+                nc.scalar.activation(out=r_bf[h][:, P * c : P * (c + 1), :], in_=src, func=ACT.Abs)
             elif kind == "o":
                 c = int(name[1])
                 copy(arg, o_sb[c][:], banks["S%d" % c][:])

@@ -13,14 +13,26 @@ U32 = mybir.dt.uint32
 U8 = mybir.dt.uint8
 FP8X4 = mybir.dt.float8_e4m3fn_x4
 FP4X4 = mybir.dt.float4_e2m1fn_x4
-ACT = mybir.ActivationFunctionType
+FUNC = mybir.ActivationFunctionType
 ALU = mybir.AluOpType
 
 P = 128
-WARM_PASSES = 26
+PACK = 4
+PASS = P * PACK
+K_PASSES = K // PASS
+HALVES = M // PASS
+ROW_TILES = PASS // P
+CHUNKS = N // P
+W_PIECE = N // 2
+BANK = 512
+UPPER_BANKS = 4
+WARM_PASSES = 36
 
-LOADS = "dU0a dVa du00 du01 du02 du03 dv0 dv1 dv2 dv3 dU0b dVb db00 db01 db02 db03 dE00 du10 du11 du12 du13 dU1 dX0 dE01 dX1 dE02 dE03 dX2 dE10 dE11 dX3 dE12 dE13 db10 db11 db12 db13".split()
-STEPS = "pU0a:V pS0:V A0:0 A1:1 pU0b:V A2:2 A3:3 D00:0 D01:1 a00:V D02:2 a01:V T00a:4 pS1:V T01a:5 c00a:A a02:V D03:3 c01a:A pU1:V a03:V D10:6 iX0:V r00:A T02a:7 qX0:V T03a:0 c02a:A iX1:V D11:1 r01:A c03a:V T00b:4 T01b:5 c00b:A qE00:V T02b:2 c01b:A qX1:V T03b:7 c02b:A qE01:V D12:0 c03b:A iX2:V s00:A T10a:4 T11a:3 qX2:V c10a:A T12a:5 c11a:A T13a:2 iX3:V c12a:A D13:7 s01:A qE02:V T10b:4 qX3:V c13a:A T11b:3 qE03:V c10b:A T12b:5 qE10:V c11b:A T13b:2 c12b:A a10:V R00:4 c13b:A qE11:V a11:V R01:3 b00:A a12:V a13:V R02:5 b01:A qE12:V r10:A R03:6 qE13:V qW0:V r11:A R10:2 s10:V R11:4 b02:A s11:V b03:A R12:3 b10:A qR00:V b11:A qR10:V R13:5 qW1:V b12:A qR11:V qR12:V S00:6 b13:A S10:6 S01:2 o0:A S11:2 qR13:V S02:4 S12:4 o1:A S03:1 o2:V S13:1 o3:A dO0:S dO1:S dO2:S dO3:S".split()
+FIRST_PAIR, SECOND_PAIR, ALL_PASSES = slice(0, 2), slice(2, 4), slice(0, 4)
+
+
+def block(i, width=P):
+    return slice(width * i, width * (i + 1))
 
 
 def tile_cross_backward_error_s12_kernel(tc, e, x, u_words, u_scales, v_words, v_scales, b_abs, out):
@@ -29,247 +41,299 @@ def tile_cross_backward_error_s12_kernel(tc, e, x, u_words, u_scales, v_words, v
         keep = ctx.enter_context(tc.tile_pool(name="keep", bufs=1))
         psum = ctx.enter_context(tc.psum_pool(name="psum", bufs=1))
 
-        def sb(name, shape, dtype):
+        def sbuf(name, shape, dtype):
             return keep.tile(shape, dtype, name=name, align_bytes=64)
 
-        def grid(name, a, b, shape, dtype):
-            return [[sb("%s%d%d" % (name, i, j), shape, dtype) for j in range(b)] for i in range(a)]
+        def sbufs(name, count, shape, dtype):
+            return [sbuf("%s%d" % (name, i), shape, dtype) for i in range(count)]
 
-        def row(name, a, shape, dtype):
-            return [sb("%s%d" % (name, i), shape, dtype) for i in range(a)]
+        def sbufs_by_half(name, count, shape, dtype):
+            return [sbufs("%s%d_" % (name, h), count, shape, dtype) for h in range(HALVES)]
 
-        ident = sb("ident", [P, P], F32)
-        perm = sb("perm", [P, P], F32)
-        warm = sb("warm", [P, 512], BF16)
-        warm_out = sb("warm_out", [P, 1], F32)
-        warm_codes = sb("warm_codes", [P, P], U32)
-        warm_sc = sb("warm_sc", [P, P], U8)
-        y_sb = row("y_sb", 2, [P, 512, 4], F32)
-        e_raw = grid("e_raw", 2, 4, [P, 2, 1024], BF16)
-        e_grp = grid("e_grp", 2, 2, [P, 2, 2048], BF16)
-        e_codes = grid("e_codes", 2, 4, [P, 512], U32)
-        e_sc = grid("e_sc", 2, 4, [P, 512], U8)
-        x_raw = row("x_raw", 4, [P, 4, 512], BF16)
-        x_grp = row("x_grp", 4, [P, 512, 4], BF16)
-        x_codes = row("x_codes", 4, [P, 512], U32)
-        x_sc = row("x_sc", 4, [P, 512], U8)
-        u_raw = row("u_raw", 2, [P, 4, 1024], U8)
-        u_w = row("u_w", 2, [P, 4, 1024], U8)
-        us_raw = sb("us_raw", [P, 4, 1024], U8)
-        us = row("us", 2, [P, 4, 512], U8)
-        v_w = row("v_w", 2, [P, 2, 1024], U8)
-        vs = sb("vs", [P, 4, 512], U8)
-        b_sb = row("b_sb", 2, [P, 4, 512], BF16)
-        d_sb = row("d_sb", 2, [P, 4, 512], F32)
-        w_bf = row("w_bf", 2, [P, 512, 4], BF16)
-        w_codes = row("w_codes", 2, [P, 512], U32)
-        w_sc = row("w_sc", 2, [P, 512], U8)
-        r_bf = row("r_bf", 2, [P, 512, 4], BF16)
-        r_codes = row("r_codes", 2, [P, 512], U32)
-        r_sc = row("r_sc", 2, [P, 512], U8)
-        o_sb = row("o_sb", 4, [P, 512], F32)
+        ident = sbuf("ident", [P, P], F32)
+        to_slots = sbuf("to_slots", [P, P], F32)
+        warm = sbuf("warm", [P, PASS], BF16)
+        warm_codes = sbuf("warm_codes", [P, P], U32)
+        warm_scale = sbuf("warm_scale", [P, P], U8)
+        e_rows = sbufs_by_half("e_rows", ROW_TILES, [P, K], BF16)
+        e_packed = sbufs_by_half("e_packed", K_PASSES // 2, [P, 2, PASS * PACK], BF16)
+        e_codes = sbufs_by_half("e_codes", K_PASSES, [P, PASS], U32)
+        e_scale = sbufs_by_half("e_scale", K_PASSES, [P, PASS], U8)
+        x_rows = sbufs("x_rows", K_PASSES, [P, PACK, N], BF16)
+        x_packed = sbufs("x_packed", K_PASSES, [P, N, PACK], BF16)
+        x_codes = sbufs("x_codes", K_PASSES, [P, N], U32)
+        x_scale = sbufs("x_scale", K_PASSES, [P, N], U8)
+        u_codes_in = sbuf("u_codes_in", [P, K_PASSES, 2 * M], U8)
+        u_scale_in = sbuf("u_scale_in", [P, K_PASSES, M], U8)
+        u_codes = sbufs("u_codes", HALVES, [P, K_PASSES, 2 * PASS], U8)
+        u_scale = sbufs("u_scale", HALVES, [P, K_PASSES, PASS], U8)
+        v_codes = sbufs("v_codes", K_PASSES // 2, [P, 2, 2 * N], U8)
+        v_scale = sbuf("v_scale", [P, K_PASSES, N], U8)
+        b_slots = sbufs("b_slots", HALVES, [P, PACK, N], BF16)
+        d_slots = sbufs("d_slots", HALVES, [P, PACK, N], F32)
+        d_rsqrt = sbufs("d_rsqrt", HALVES, [P, N, PACK], F32)
+        w_packed = sbufs("w_packed", HALVES, [P, N, PACK], BF16)
+        w_codes = sbufs("w_codes", HALVES, [P, N], U32)
+        w_scale = sbufs("w_scale", HALVES, [P, N], U8)
+        r_packed = sbufs("r_packed", HALVES, [P, N, PACK], BF16)
+        r_codes = sbufs("r_codes", HALVES, [P, N], U32)
+        r_scale = sbufs("r_scale", HALVES, [P, N], U8)
+        out_rows = sbufs("out_rows", CHUNKS, [P, N], F32)
+
+        def psum_bank(name, index):
+            return psum.tile([P, BANK], F32, name=name, tag="bank%d" % index)
+
+        def quantize(codes, scale, packed):
+            nc.vector.quantize_mx(out=codes.bitcast(FP8X4), scales=scale, in_=packed)
+
+        def load_u_codes(passes):
+            src = u_words[passes].rearrange("g p n -> p g n")
+            nc.sync.dma_start(out=u_codes_in[:, passes].bitcast(I32), in_=src.bitcast(I32))
+
+        def load_v_codes(pair):
+            src = v_words[block(pair, 2)].rearrange("g p n -> p g n")
+            nc.sync.dma_start(out=v_codes[pair][:].bitcast(I32), in_=src.bitcast(I32))
+
+        def load_scale_rows(tile, rows):
+            for r in range(4):
+                src = rows[:, r:16:4, :].rearrange("g b n -> b g n")
+                nc.sync.dma_start(out=tile[r:P:32].bitcast(I32), in_=src.bitcast(I32))
+
+        def load_b(h):
+            rows = b_abs[block(h, PASS), :].rearrange("(q t s) n -> s q t n", t=PACK, s=4)
+            for s in range(4):
+                nc.sync.dma_start(out=b_slots[h][s:P:4], in_=rows[s])
+
+        def load_e(h, j):
+            nc.sync.dma_start(out=e_rows[h][j][:], in_=e[block(ROW_TILES * h + j), :])
+
+        def load_x(g):
+            nc.sync.dma_start(out=x_rows[g][:], in_=x[block(g, PASS), :].rearrange("(p i) n -> p i n", i=PACK))
+
+        def order_u_codes(h, passes):
+            src = u_codes_in[:, passes, block(h, 2 * PASS)].bitcast(I32)
+            nc.vector.tensor_copy(
+                out=u_codes[h][:, passes].bitcast(I32).rearrange("p g (t q a) -> p g t q a", t=PACK, a=2),
+                in_=src.rearrange("p g (q t a) -> p g t q a", t=PACK, a=2),
+            )
+
+        def order_u_scale(h):
+            nc.vector.tensor_copy(
+                out=u_scale[h][:].bitcast(I32).rearrange("p g (t q) -> p g t q", t=PACK),
+                in_=u_scale_in[:, :, block(h, PASS)].bitcast(I32).rearrange("p g (q t) -> p g t q", t=PACK),
+            )
+
+        d_psum = {}
+
+        def d_matmul(h, t, passes):
+            if passes.start == 0:
+                d_psum[h, t] = psum_bank("d%d%d" % (h, t), t)
+            for g in range(passes.start, passes.stop):
+                nc.tensor.matmul_mx(
+                    out=d_psum[h, t][:],
+                    lhsT=u_codes[h][:, g, block(t, 2 * P)].bitcast(FP4X4),
+                    lhsT_scale=u_scale[h][:, g, block(t)],
+                    rhs=v_codes[g // 2][:, g % 2, :].bitcast(FP4X4),
+                    rhs_scale=v_scale[:, g, :],
+                    start=(g == 0),
+                    stop=(g == K_PASSES - 1),
+                )
+
+        def add_b(h, t):
+            nc.vector.tensor_tensor(out=d_slots[h][:, t, :], in0=d_psum[h, t][:], in1=b_slots[h][:, t, :], op=ALU.add)
+
+        def rsqrt_d(h, piece):
+            cols = block(piece, W_PIECE)
+            src = d_slots[h][:, :, cols].rearrange("p t n -> p n t")
+            nc.scalar.activation(out=d_rsqrt[h][:, cols, :], in_=src, func=FUNC.Abs_reciprocal_sqrt)
+
+        def square_on_vector(h, piece):
+            src = d_rsqrt[h][:, block(piece, W_PIECE), :]
+            nc.vector.tensor_tensor(out=w_packed[h][:, block(piece, W_PIECE), :], in0=src, in1=src, op=ALU.mult)
+
+        def square_on_scalar(h, piece):
+            src = d_rsqrt[h][:, block(piece, W_PIECE), :]
+            nc.scalar.activation(out=w_packed[h][:, block(piece, W_PIECE), :], in_=src, func=FUNC.Square)
+
+        def quantize_w(h):
+            quantize(w_codes[h][:], w_scale[h][:], w_packed[h][:].rearrange("p n t -> p (n t)"))
+
+        e_psum = {}
+
+        def transpose_e(h, j):
+            words = e_rows[h][j][:].bitcast(F32)
+            for pair in range(K_PASSES // 2):
+                bank = psum_bank("e%d%d%d" % (h, j, pair), UPPER_BANKS + 2 * (j % 2) + pair)
+                e_psum[h, j, pair] = bank
+                for gg in range(2):
+                    first_word = (2 * pair + gg) * PASS // 2
+                    for u in range(2):
+                        src = words[:, first_word + u : first_word + PASS // 2 : 2]
+                        nc.tensor.transpose(bank[:, block(2 * gg + u)], src, to_slots[:])
+
+        def pack_e(h, j):
+            for pair in range(K_PASSES // 2):
+                dst = e_packed[h][pair][:].bitcast(F32).rearrange("p g (t j c u) -> p j g t c u", t=PACK, j=ROW_TILES, u=2)
+                src = e_psum[h, j, pair][:].rearrange("p (g u t c) -> p g t c u", g=2, u=2, t=PACK)
+                nc.scalar.copy(out=dst[:, j], in_=src)
+
+        def quantize_e(h, g):
+            quantize(e_codes[h][g][:], e_scale[h][g][:], e_packed[h][g // 2][:, g % 2, :])
+
+        def pack_x(g):
+            nc.vector.tensor_copy(
+                out=x_packed[g][:].rearrange("p (c a) i -> p c i a", a=4),
+                in_=x_rows[g][:].rearrange("p i (c a) -> p c i a", a=4),
+            )
+
+        def quantize_x(g):
+            quantize(x_codes[g][:], x_scale[g][:], x_packed[g][:].rearrange("p n i -> p (n i)"))
+
+        def r_chunk(h, c):
+            bank = psum_bank("r%d%d" % (h, c), c + (UPPER_BANKS if h == 0 else 0))
+            for t in range(PACK):
+                for g in range(K_PASSES):
+                    nc.tensor.matmul_mx(
+                        out=bank[:, block(t)],
+                        lhsT=e_codes[h][g][:, block(t)].bitcast(FP8X4),
+                        lhsT_scale=e_scale[h][g][:, block(t)],
+                        rhs=x_codes[g][:, block(c)].bitcast(FP8X4),
+                        rhs_scale=x_scale[g][:, block(c)],
+                        start=(g == 0),
+                        stop=(g == K_PASSES - 1),
+                    )
+            src = bank[:].rearrange("p (t n) -> p n t", t=PACK)
+            nc.scalar.activation(out=r_packed[h][:, block(c), :], in_=src, func=FUNC.Abs)
+
+        def quantize_r(h, cols):
+            quantize(r_codes[h][:, cols], r_scale[h][:, cols], r_packed[h][:, cols, :].rearrange("p n t -> p (n t)"))
+
+        def out_chunk(c):
+            bank = psum_bank("out%d" % c, UPPER_BANKS + c)
+            for h in range(HALVES):
+                nc.tensor.matmul_mx(
+                    out=bank[:],
+                    lhsT=r_codes[h][:, block(c)].bitcast(FP8X4),
+                    lhsT_scale=r_scale[h][:, block(c)],
+                    rhs=w_codes[h][:].bitcast(FP8X4),
+                    rhs_scale=w_scale[h][:],
+                    start=(h == 0),
+                    stop=(h == HALVES - 1),
+                )
+            if c % 2 == 0:
+                nc.scalar.copy(out=out_rows[c][:], in_=bank[:])
+            else:
+                nc.vector.tensor_copy(out=out_rows[c][:], in_=bank[:])
+            nc.sync.dma_start(out=out[block(c), :], in_=out_rows[c][:])
 
         ctx.enter_context(tc.manual_schedule())
 
         nc.gpsimd.memset(warm[:], 1.0)
-        nc.vector.memset(us_raw[:].rearrange("p g n -> p (g n)").bitcast(I32), 0)
-        nc.vector.quantize_mx(out=warm_codes[:].bitcast(FP8X4), scales=warm_sc[:], in_=warm[:])
-        nc.vector.memset(vs[:].rearrange("p g n -> p (g n)").bitcast(I32), 0)
+        nc.vector.memset(u_scale_in[:].rearrange("p g n -> p (g n)").bitcast(I32), 0)
+        quantize(warm_codes[:], warm_scale[:], warm[:])
+        nc.vector.memset(v_scale[:].rearrange("p g n -> p (g n)").bitcast(I32), 0)
         make_identity(nc, ident[:])
 
-        def passes_of(name):
-            return {"a": slice(0, 2), "b": slice(2, 4)}.get(name[-1], slice(0, 4))
+        load_u_codes(FIRST_PAIR)
+        load_scale_rows(u_scale_in, u_scales)
+        load_v_codes(0)
+        load_scale_rows(v_scale, v_scales)
+        load_u_codes(SECOND_PAIR)
+        load_v_codes(1)
+        load_b(0)
+        load_e(0, 0)
+        load_x(0)
+        load_e(0, 1)
+        load_x(1)
+        load_e(0, 2)
+        load_e(0, 3)
+        load_x(2)
+        load_e(1, 0)
+        load_e(1, 1)
+        load_x(3)
+        load_e(1, 2)
+        load_e(1, 3)
+        load_b(1)
 
-        def load(name):
-            if name[1] == "E":
-                h, i = int(name[2]), int(name[3])
-                m0, k0 = 512 * h + 256 * (i % 2), 1024 * (i // 2)
-                src = e[m0 : m0 + 256, k0 : k0 + 1024].rearrange("(j p) k -> p j k", p=P)
-                nc.sync.dma_start(out=e_raw[h][i][:], in_=src)
-            elif name[1] == "u":
-                r = int(name[3])
-                cols = slice(512 * int(name[2]), 512 * (int(name[2]) + 1)) if "du10" in LOADS else slice(0, 1024)
-                src = u_scales[:, r:16:4, cols].rearrange("g q n -> q g n")
-                nc.sync.dma_start(out=us_raw[r:P:32, :, cols].bitcast(I32), in_=src.bitcast(I32))
-            elif name[1] == "v":
-                r = int(name[2])
-                src = v_scales[:, r:16:4, :].rearrange("g q n -> q g n")
-                nc.sync.dma_start(out=vs[r:P:32].bitcast(I32), in_=src.bitcast(I32))
-            elif name[1] == "X":
-                g = int(name[2])
-                nc.sync.dma_start(out=x_raw[g][:], in_=x[512 * g : 512 * (g + 1), :].rearrange("(p j) n -> p j n", j=4))
-            elif name[1] == "V":
-                a = "ab".index(name[2])
-                src = v_words[2 * a : 2 * a + 2].rearrange("g p n -> p g n")
-                nc.sync.dma_start(out=v_w[a][:].bitcast(I32), in_=src.bitcast(I32))
-            elif name[1] == "U":
-                h = int(name[2])
-                gs = passes_of(name)
-                src = u_words[gs, :, 1024 * h : 1024 * (h + 1)].rearrange("g p n -> p g n")
-                nc.sync.dma_start(out=u_raw[h][:, gs].bitcast(I32), in_=src.bitcast(I32))
-            else:
-                h = int(name[2])
-                rows = b_abs[512 * h : 512 * (h + 1), :].rearrange("(q t s) n -> s q t n", t=4, s=4)
-                s = int(name[3])
-                nc.sync.dma_start(out=b_sb[h][s:P:4], in_=rows[s])
-
-        for name in LOADS:
-            load(name)
-
-        nc.scalar.activation(out=warm_out[:], in_=warm[:, 0:1], func=ACT.Abs_reciprocal_sqrt)
         nc.vector.tensor_copy(
-            out=perm[:].rearrange("p (t q s) -> p t q s", t=4, s=4),
-            in_=ident[:].rearrange("p (q t s) -> p t q s", t=4, s=4),
+            out=to_slots[:].rearrange("p (t q s) -> p t q s", t=PACK, s=4),
+            in_=ident[:].rearrange("p (q t s) -> p t q s", t=PACK, s=4),
         )
-
-        warm_ps = psum.tile([P, 512], F32, name="ps_warm", tag="bank7")
+        warm_psum = psum_bank("warm_psum", 2 * UPPER_BANKS - 1)
         for i in range(WARM_PASSES):
             nc.tensor.matmul_mx(
-                out=warm_ps[:, P * (i % 4) : P * (i % 4 + 1)],
+                out=warm_psum[:, block(i % PACK)],
                 lhsT=warm_codes[:].bitcast(FP8X4),
-                lhsT_scale=warm_sc[:],
+                lhsT_scale=warm_scale[:],
                 rhs=warm_codes[:].bitcast(FP8X4),
-                rhs_scale=warm_sc[:],
+                rhs_scale=warm_scale[:],
                 start=True,
                 stop=True,
             )
 
-        banks = {}
+        order_u_codes(0, FIRST_PAIR)
+        order_u_scale(0)
+        order_u_scale(1)
+        order_u_codes(0, SECOND_PAIR)
+        order_u_codes(1, ALL_PASSES)
+        for t in range(PACK):
+            d_matmul(0, t, FIRST_PAIR)
+        for t in range(PACK):
+            d_matmul(0, t, SECOND_PAIR)
+            add_b(0, t)
 
-        def new_bank(key, bank):
-            banks[key] = psum.tile([P, 512], F32, name="ps_" + key, tag="bank%d" % bank)
-            return banks[key]
+        transpose_e(0, 0)
+        d_matmul(1, 0, ALL_PASSES)
+        rsqrt_d(0, 0)
+        pack_e(0, 0)
+        transpose_e(0, 1)
+        d_matmul(1, 1, ALL_PASSES)
+        pack_e(0, 1)
+        pack_x(0)
+        pack_x(1)
+        quantize_x(0)
+        square_on_vector(0, 0)
+        quantize_x(1)
+        for j in (2, 3):
+            transpose_e(0, j)
+            pack_e(0, j)
+        d_matmul(1, 2, ALL_PASSES)
+        rsqrt_d(0, 1)
+        pack_x(2)
+        quantize_e(0, 0)
+        quantize_x(2)
+        quantize_e(0, 1)
+        pack_x(3)
+        quantize_e(0, 2)
+        quantize_e(0, 3)
+        quantize_x(3)
+        for j in (0, 1):
+            transpose_e(1, j)
+            pack_e(1, j)
+        d_matmul(1, 3, ALL_PASSES)
+        for j in (2, 3):
+            transpose_e(1, j)
+            pack_e(1, j)
+        square_on_scalar(0, 1)
 
-        def copy(eng, dst, src):
-            if eng == "V":
-                nc.vector.tensor_copy(out=dst, in_=src)
-            else:
-                nc.scalar.copy(out=dst, in_=src)
+        for t in range(PACK):
+            add_b(1, t)
+        for g in range(K_PASSES):
+            quantize_e(1, g)
+        r_chunk(0, 0)
+        r_chunk(0, 1)
+        rsqrt_d(1, 0)
+        rsqrt_d(1, 1)
+        r_chunk(0, 2)
+        r_chunk(0, 3)
+        quantize_w(0)
+        square_on_vector(1, 0)
+        square_on_vector(1, 1)
+        quantize_r(0, slice(0, N))
+        quantize_w(1)
 
-        def d_passes(acc, h, t, passes):
-            for g in passes:
-                nc.tensor.matmul_mx(
-                    out=acc[:],
-                    lhsT=u_w[h][:, g, 256 * t : 256 * (t + 1)].bitcast(FP4X4),
-                    lhsT_scale=us[h][:, g, P * t : P * (t + 1)],
-                    rhs=v_w[g // 2][:, g % 2, :].bitcast(FP4X4),
-                    rhs_scale=vs[:, g, :],
-                    start=(g == 0),
-                    stop=(g == 3),
-                )
-
-        def permute_u(h, gs):
-            nc.vector.tensor_copy(
-                out=u_w[h][:, gs].bitcast(I32).rearrange("p g (t q s) -> p g t q s", t=4, s=2),
-                in_=u_raw[h][:, gs].bitcast(I32).rearrange("p g (q t s) -> p g t q s", t=4, s=2),
-            )
-
-        def step(name, arg):
-            kind = name[0]
-            if kind == "T":
-                h, j, pair = int(name[1]), int(name[2]), "ab".index(name[3])
-                bank = new_bank(name, int(arg))
-                words = e_raw[h][2 * pair + j // 2][:, j % 2, :].bitcast(F32)
-                for gg in range(2):
-                    for u in range(2):
-                        o = P * (2 * gg + u)
-                        nc.tensor.transpose(bank[:, o : o + P], words[:, 256 * gg + u : 256 * (gg + 1) : 2], perm[:])
-            elif kind == "c":
-                h, j, pair = int(name[1]), int(name[2]), "ab".index(name[3])
-                dst = e_grp[h][pair][:].bitcast(F32).rearrange("p g (t j c u) -> p j g t c u", t=4, j=4, u=2)
-                src = banks["T" + name[1:]][:].rearrange("p (g u t c) -> p g t c u", g=2, u=2, t=4)
-                copy(arg, dst[:, j], src)
-            elif kind == "A":
-                t = int(name[1])
-                d_passes(new_bank("D0%d" % t, int(arg)), 0, t, (0, 1))
-            elif kind == "D":
-                h, t = int(name[1]), int(name[2])
-                if h == 0:
-                    d_passes(banks[name], 0, t, (2, 3))
-                else:
-                    d_passes(new_bank(name, int(arg)), 1, t, (0, 1, 2, 3))
-            elif kind == "R":
-                h, c = int(name[1]), int(name[2])
-                bank = new_bank(name, int(arg))
-                cols = slice(P * c, P * (c + 1))
-                for t in range(4):
-                    rows = slice(P * t, P * (t + 1))
-                    for g in range(4):
-                        nc.tensor.matmul_mx(
-                            out=bank[:, rows],
-                            lhsT=e_codes[h][g][:, rows].bitcast(FP8X4),
-                            lhsT_scale=e_sc[h][g][:, rows],
-                            rhs=x_codes[g][:, cols].bitcast(FP8X4),
-                            rhs_scale=x_sc[g][:, cols],
-                            start=(g == 0),
-                            stop=(g == 3),
-                        )
-            elif kind == "S":
-                h, c = int(name[1]), int(name[2])
-                acc = new_bank("S%d" % c, int(arg)) if h == 0 else banks["S%d" % c]
-                nc.tensor.matmul_mx(
-                    out=acc[:],
-                    lhsT=r_codes[h][:, P * c : P * (c + 1)].bitcast(FP8X4),
-                    lhsT_scale=r_sc[h][:, P * c : P * (c + 1)],
-                    rhs=w_codes[h][:].bitcast(FP8X4),
-                    rhs_scale=w_sc[h][:],
-                    start=(h == 0),
-                    stop=(h == 1),
-                )
-            elif name[:2] == "pU":
-                permute_u(int(name[2]), passes_of(name))
-            elif name[:2] == "pS":
-                h = int(name[2])
-                nc.vector.tensor_copy(
-                    out=us[h][:].bitcast(I32).rearrange("p g (t q) -> p g t q", t=4),
-                    in_=us_raw[:, :, 512 * h : 512 * (h + 1)].bitcast(I32).rearrange("p g (q t) -> p g t q", t=4),
-                )
-            elif name[:2] == "iX":
-                g = int(name[2])
-                copy(
-                    arg,
-                    x_grp[g][:].rearrange("p (c i) t -> p c t i", i=4),
-                    x_raw[g][:].rearrange("p t (c i) -> p c t i", i=4),
-                )
-            elif name[:2] == "qX":
-                g = int(name[2])
-                nc.vector.quantize_mx(out=x_codes[g][:].bitcast(FP8X4), scales=x_sc[g][:], in_=x_grp[g][:].rearrange("p n t -> p (n t)"))
-            elif name[:2] == "qE":
-                h, g = int(name[2]), int(name[3])
-                nc.vector.quantize_mx(out=e_codes[h][g][:].bitcast(FP8X4), scales=e_sc[h][g][:], in_=e_grp[h][g // 2][:, g % 2, :])
-            elif name[:2] == "qR":
-                h, c = int(name[2]), int(name[3])
-                cols = slice(0, 512) if h == 0 else slice(P * c, P * (c + 1))
-                nc.vector.quantize_mx(out=r_codes[h][:, cols].bitcast(FP8X4), scales=r_sc[h][:, cols], in_=r_bf[h][:, cols, :].rearrange("p n t -> p (n t)"))
-            elif name[:2] == "qW":
-                h = int(name[2])
-                nc.vector.quantize_mx(out=w_codes[h][:].bitcast(FP8X4), scales=w_sc[h][:], in_=w_bf[h][:].rearrange("p n t -> p (n t)"))
-            elif kind == "a":
-                h, t = int(name[1]), int(name[2])
-                nc.vector.tensor_tensor(out=d_sb[h][:, t, :], in0=banks["D" + name[1:]][:], in1=b_sb[h][:, t, :], op=ALU.add)
-            elif kind == "r":
-                h, c = int(name[1]), int(name[2])
-                cols = slice(256 * c, 256 * (c + 1))
-                nc.scalar.activation(out=y_sb[h][:, cols, :], in_=d_sb[h][:, :, cols].rearrange("p t n -> p n t"), func=ACT.Abs_reciprocal_sqrt)
-            elif kind == "s":
-                h, c = int(name[1]), int(name[2])
-                src = y_sb[h][:, 256 * c : 256 * (c + 1), :]
-                dst = w_bf[h][:, 256 * c : 256 * (c + 1), :]
-                if arg == "V":
-                    nc.vector.tensor_tensor(out=dst, in0=src, in1=src, op=ALU.mult)
-                else:
-                    nc.scalar.activation(out=dst, in_=src, func=ACT.Square)
-            elif kind == "b":
-                h, c = int(name[1]), int(name[2])
-                src = banks["R" + name[1:]][:].rearrange("p (t n) -> p n t", t=4)
-                nc.scalar.activation(out=r_bf[h][:, P * c : P * (c + 1), :], in_=src, func=ACT.Abs)
-            elif kind == "o":
-                c = int(name[1])
-                copy(arg, o_sb[c][:], banks["S%d" % c][:])
-            else:
-                c = int(name[2])
-                nc.sync.dma_start(out=out[P * c : P * (c + 1), :], in_=o_sb[c][:])
-
-        for item in STEPS:
-            name, arg = item.split(":")
-            step(name, arg)
+        for c in range(CHUNKS):
+            r_chunk(1, c)
+            quantize_r(1, block(c))
+        for c in range(CHUNKS):
+            out_chunk(c)

@@ -26,7 +26,6 @@ CHUNKS = N // P
 W_PIECE = N // 2
 BANK = 512
 UPPER_BANKS = 4
-WARM_PASSES = 36
 
 FIRST_PAIR, SECOND_PAIR, ALL_PASSES = slice(0, 2), slice(2, 4), slice(0, 4)
 
@@ -52,9 +51,6 @@ def tile_cross_backward_error_s12_kernel(tc, e, x, u_words, u_scales, v_words, v
 
         ident = sbuf("ident", [P, P], F32)
         to_slots = sbuf("to_slots", [P, P], F32)
-        warm = sbuf("warm", [P, PASS], BF16)
-        warm_codes = sbuf("warm_codes", [P, P], U32)
-        warm_scale = sbuf("warm_scale", [P, P], U8)
         e_rows = sbufs_by_half("e_rows", ROW_TILES, [P, K], BF16)
         e_packed = sbufs_by_half("e_packed", K_PASSES // 2, [P, 2, PASS * PACK], BF16)
         e_codes = sbufs_by_half("e_codes", K_PASSES, [P, PASS], U32)
@@ -228,9 +224,7 @@ def tile_cross_backward_error_s12_kernel(tc, e, x, u_words, u_scales, v_words, v
 
         ctx.enter_context(tc.manual_schedule())
 
-        nc.gpsimd.memset(warm[:], 1.0)
         nc.vector.memset(u_scale_in[:].rearrange("p g n -> p (g n)").bitcast(I32), 0)
-        quantize(warm_codes[:], warm_scale[:], warm[:])
         nc.vector.memset(v_scale[:].rearrange("p g n -> p (g n)").bitcast(I32), 0)
         make_identity(nc, ident[:])
 
@@ -259,17 +253,6 @@ def tile_cross_backward_error_s12_kernel(tc, e, x, u_words, u_scales, v_words, v
             out=to_slots[:].rearrange("p (t q s) -> p t q s", t=PACK, s=4),
             in_=ident[:].rearrange("p (q t s) -> p t q s", t=PACK, s=4),
         )
-        warm_psum = psum_bank("warm_psum", 2 * UPPER_BANKS - 1)
-        for i in range(WARM_PASSES):
-            nc.tensor.matmul_mx(
-                out=warm_psum[:, block(i % PACK)],
-                lhsT=warm_codes[:].bitcast(FP8X4),
-                lhsT_scale=warm_scale[:],
-                rhs=warm_codes[:].bitcast(FP8X4),
-                rhs_scale=warm_scale[:],
-                start=True,
-                stop=True,
-            )
 
         order_u_codes(0, FIRST_PAIR)
         order_u_scale(0)

@@ -21,13 +21,17 @@ PACK = 4
 PASS = P * PACK
 K_PASSES = K // PASS
 HALVES = M // PASS
-ROW_TILES = PASS // P
+SLOTS = HALVES * PACK
+RUN = 8
 CHUNKS = N // P
 W_PIECE = N // 2
 BANK = 512
-UPPER_BANKS = 4
+STAGE_BUFS = 3
 
 FIRST_PAIR, SECOND_PAIR, ALL_PASSES = slice(0, 2), slice(2, 4), slice(0, 4)
+
+R_BANKS = ((2, 3, 4, 5), (6, 7, 4, 5))
+OUT_BANKS = (0, 1, 2, 3)
 
 
 def block(i, width=P):
@@ -46,28 +50,25 @@ def tile_cross_backward_error_s12_kernel(tc, e, x, u_words, u_scales, v_words, v
         def sbufs(name, count, shape, dtype):
             return [sbuf("%s%d" % (name, i), shape, dtype) for i in range(count)]
 
-        def sbufs_by_half(name, count, shape, dtype):
-            return [sbufs("%s%d_" % (name, h), count, shape, dtype) for h in range(HALVES)]
-
         ident = sbuf("ident", [P, P], F32)
-        to_slots = sbuf("to_slots", [P, P], F32)
-        e_rows = sbufs_by_half("e_rows", ROW_TILES, [P, K], BF16)
-        e_packed = sbufs_by_half("e_packed", K_PASSES // 2, [P, 2, PASS * PACK], BF16)
-        e_codes = sbufs_by_half("e_codes", K_PASSES, [P, PASS], U32)
-        e_scale = sbufs_by_half("e_scale", K_PASSES, [P, PASS], U8)
+        e_rows = sbufs("e_rows", SLOTS, [P, K], BF16)
+        e_split = sbufs("e_split", STAGE_BUFS, [P, K // 2], F32)
+        e_packed = sbufs("e_packed", STAGE_BUFS, [P, K], BF16)
+        e_codes = sbufs("e_codes", SLOTS, [P, K_PASSES * P], U32)
+        e_scale = sbufs("e_scale", SLOTS, [P, K_PASSES * P], U8)
         x_rows = sbufs("x_rows", K_PASSES, [P, PACK, N], BF16)
         x_packed = sbufs("x_packed", K_PASSES, [P, N, PACK], BF16)
         x_codes = sbufs("x_codes", K_PASSES, [P, N], U32)
         x_scale = sbufs("x_scale", K_PASSES, [P, N], U8)
-        u_codes_in = sbuf("u_codes_in", [P, K_PASSES, 2 * M], U8)
-        u_scale_in = sbuf("u_scale_in", [P, K_PASSES, M], U8)
-        u_codes = sbufs("u_codes", HALVES, [P, K_PASSES, 2 * PASS], U8)
+        u_codes_in = sbufs("u_codes_in", HALVES, [P, K_PASSES * 2 * PASS], U8)
+        u_scale_in = sbufs("u_scale_in", HALVES, [P, K_PASSES, PASS], U8)
+        u_codes = sbufs("u_codes", HALVES, [P, K_PASSES * 2 * PASS], U8)
         u_scale = sbufs("u_scale", HALVES, [P, K_PASSES, PASS], U8)
-        v_codes = sbufs("v_codes", K_PASSES // 2, [P, 2, 2 * N], U8)
+        v_codes = sbuf("v_codes", [P, K_PASSES * 2 * N], U8)
         v_scale = sbuf("v_scale", [P, K_PASSES, N], U8)
-        b_slots = sbufs("b_slots", HALVES, [P, PACK, N], BF16)
+        b_slots = sbufs("b_slots", SLOTS, [P, N], BF16)
         d_slots = sbufs("d_slots", HALVES, [P, PACK, N], F32)
-        d_rsqrt = sbufs("d_rsqrt", HALVES, [P, N, PACK], F32)
+        d_rsqrt = sbufs("d_rsqrt", HALVES, [P, PACK, N], F32)
         w_packed = sbufs("w_packed", HALVES, [P, N, PACK], BF16)
         w_codes = sbufs("w_codes", HALVES, [P, N], U32)
         w_scale = sbufs("w_scale", HALVES, [P, N], U8)
@@ -82,99 +83,127 @@ def tile_cross_backward_error_s12_kernel(tc, e, x, u_words, u_scales, v_words, v
         def quantize(codes, scale, packed):
             nc.vector.quantize_mx(out=codes.bitcast(FP8X4), scales=scale, in_=packed)
 
-        def load_u_codes(passes):
-            src = u_words[passes].rearrange("g p n -> p g n")
-            nc.sync.dma_start(out=u_codes_in[:, passes].bitcast(I32), in_=src.bitcast(I32))
+        def copy_on(engine, dst, src):
+            if engine == "scalar":
+                nc.scalar.copy(out=dst, in_=src)
+            else:
+                nc.vector.tensor_copy(out=dst, in_=src)
 
-        def load_v_codes(pair):
-            src = v_words[block(pair, 2)].rearrange("g p n -> p g n")
-            nc.sync.dma_start(out=v_codes[pair][:].bitcast(I32), in_=src.bitcast(I32))
+        def pass_range(tile, passes):
+            cols = slice(passes.start * 2 * PASS, passes.stop * 2 * PASS)
+            return tile[:, cols].bitcast(I32).rearrange("p (g w) -> p g w", w=PASS // 2)
+
+        def load_u_codes(h, passes):
+            src = u_words[passes, :, block(h, 2 * PASS)].rearrange("g p n -> p g n")
+            nc.sync.dma_start(out=pass_range(u_codes_in[h], passes), in_=src.bitcast(I32))
+
+        def load_v_codes(passes):
+            src = v_words[passes].rearrange("g p n -> p g n")
+            nc.sync.dma_start(out=pass_range(v_codes, passes), in_=src.bitcast(I32))
 
         def load_scale_rows(tile, rows):
             for r in range(4):
                 src = rows[:, r:16:4, :].rearrange("g b n -> b g n")
                 nc.sync.dma_start(out=tile[r:P:32].bitcast(I32), in_=src.bitcast(I32))
 
-        def load_b(h):
-            rows = b_abs[block(h, PASS), :].rearrange("(q t s) n -> s q t n", t=PACK, s=4)
-            for s in range(4):
-                nc.sync.dma_start(out=b_slots[h][s:P:4], in_=rows[s])
+        def slot_rows(matrix, j):
+            h, t = divmod(j, PACK)
+            return matrix[block(h, PASS), :].rearrange("(b t r) n -> t b r n", t=PACK, r=RUN)[t]
 
-        def load_e(h, j):
-            nc.sync.dma_start(out=e_rows[h][j][:], in_=e[block(ROW_TILES * h + j), :])
+        def load_b(j):
+            nc.sync.dma_start(out=b_slots[j][:], in_=slot_rows(b_abs, j))
+
+        def load_e(j):
+            nc.sync.dma_start(out=e_rows[j][:], in_=slot_rows(e, j))
 
         def load_x(g):
             nc.sync.dma_start(out=x_rows[g][:], in_=x[block(g, PASS), :].rearrange("(p i) n -> p i n", i=PACK))
 
+        def zero(tile):
+            nc.vector.memset(tile[:].rearrange("p g n -> p (g n)").bitcast(I32), 0)
+
         def order_u_codes(h, passes):
-            src = u_codes_in[:, passes, block(h, 2 * PASS)].bitcast(I32)
             nc.vector.tensor_copy(
-                out=u_codes[h][:, passes].bitcast(I32).rearrange("p g (t q a) -> p g t q a", t=PACK, a=2),
-                in_=src.rearrange("p g (q t a) -> p g t q a", t=PACK, a=2),
+                out=pass_range(u_codes[h], passes).rearrange("p g (t b a) -> p g t b a", t=PACK, a=RUN // 2),
+                in_=pass_range(u_codes_in[h], passes).rearrange("p g (b t a) -> p g t b a", t=PACK, a=RUN // 2),
             )
 
         def order_u_scale(h):
             nc.vector.tensor_copy(
-                out=u_scale[h][:].bitcast(I32).rearrange("p g (t q) -> p g t q", t=PACK),
-                in_=u_scale_in[:, :, block(h, PASS)].bitcast(I32).rearrange("p g (q t) -> p g t q", t=PACK),
+                out=u_scale[h][:].bitcast(I32).rearrange("p g (t b a) -> p g t b a", t=PACK, a=RUN // 4),
+                in_=u_scale_in[h][:].bitcast(I32).rearrange("p g (b t a) -> p g t b a", t=PACK, a=RUN // 4),
             )
 
         d_psum = {}
 
-        def d_matmul(h, t, passes):
+        def d_matmul(j, passes, bank):
+            h, t = divmod(j, PACK)
             if passes.start == 0:
-                d_psum[h, t] = psum_bank("d%d%d" % (h, t), t)
+                d_psum[j] = psum_bank("d%d" % j, bank)
             for g in range(passes.start, passes.stop):
                 nc.tensor.matmul_mx(
-                    out=d_psum[h, t][:],
-                    lhsT=u_codes[h][:, g, block(t, 2 * P)].bitcast(FP4X4),
+                    out=d_psum[j][:],
+                    lhsT=u_codes[h][:, block(PACK * g + t, 2 * P)].bitcast(FP4X4),
                     lhsT_scale=u_scale[h][:, g, block(t)],
-                    rhs=v_codes[g // 2][:, g % 2, :].bitcast(FP4X4),
+                    rhs=v_codes[:, block(g, 2 * N)].bitcast(FP4X4),
                     rhs_scale=v_scale[:, g, :],
                     start=(g == 0),
                     stop=(g == K_PASSES - 1),
                 )
 
-        def add_b(h, t):
-            nc.vector.tensor_tensor(out=d_slots[h][:, t, :], in0=d_psum[h, t][:], in1=b_slots[h][:, t, :], op=ALU.add)
+        def add_b(j):
+            h, t = divmod(j, PACK)
+            nc.vector.tensor_tensor(out=d_slots[h][:, t, :], in0=d_psum[j][:], in1=b_slots[j][:], op=ALU.add)
 
-        def rsqrt_d(h, piece):
-            cols = block(piece, W_PIECE)
-            src = d_slots[h][:, :, cols].rearrange("p t n -> p n t")
-            nc.scalar.activation(out=d_rsqrt[h][:, cols, :], in_=src, func=FUNC.Abs_reciprocal_sqrt)
+        def empty_d(j):
+            h, t = divmod(j, PACK)
+            nc.scalar.copy(out=d_slots[h][:, t, :], in_=d_psum[j][:])
 
-        def square_on_vector(h, piece):
-            src = d_rsqrt[h][:, block(piece, W_PIECE), :]
-            nc.vector.tensor_tensor(out=w_packed[h][:, block(piece, W_PIECE), :], in0=src, in1=src, op=ALU.mult)
+        def add_b_sbuf(j):
+            h, t = divmod(j, PACK)
+            nc.vector.tensor_tensor(out=d_slots[h][:, t, :], in0=d_slots[h][:, t, :], in1=b_slots[j][:], op=ALU.add)
 
-        def square_on_scalar(h, piece):
-            src = d_rsqrt[h][:, block(piece, W_PIECE), :]
-            nc.scalar.activation(out=w_packed[h][:, block(piece, W_PIECE), :], in_=src, func=FUNC.Square)
+        def rsqrt_d(h, slots):
+            nc.scalar.activation(out=d_rsqrt[h][:, slots, :], in_=d_slots[h][:, slots, :], func=FUNC.Abs_reciprocal_sqrt)
+
+        def square(engine, h, cols):
+            src = d_rsqrt[h][:, :, cols].rearrange("p t (c i) -> p c t i", i=2)
+            dst = w_packed[h][:, cols, :].rearrange("p (c i) t -> p c t i", i=2)
+            if engine == "scalar":
+                nc.scalar.activation(out=dst, in_=src, func=FUNC.Square)
+            else:
+                nc.vector.tensor_tensor(out=dst, in0=src, in1=src, op=ALU.mult)
 
         def quantize_w(h):
             quantize(w_codes[h][:], w_scale[h][:], w_packed[h][:].rearrange("p n t -> p (n t)"))
 
         e_psum = {}
 
-        def transpose_e(h, j):
-            words = e_rows[h][j][:].bitcast(F32)
+        def split_e(engine, j):
+            copy_on(
+                engine,
+                e_split[j % STAGE_BUFS][:].rearrange("p (g u w) -> p g u w", g=K_PASSES, u=2),
+                e_rows[j][:].bitcast(F32).rearrange("p (g w u) -> p g u w", g=K_PASSES, u=2),
+            )
+
+        def transpose_e(j, banks, split):
+            if split:
+                words = e_split[j % STAGE_BUFS][:].rearrange("p (g u w) -> p g u w", g=K_PASSES, u=2)
+            else:
+                words = e_rows[j][:].bitcast(F32).rearrange("p (g w u) -> p g u w", g=K_PASSES, u=2)
             for pair in range(K_PASSES // 2):
-                bank = psum_bank("e%d%d%d" % (h, j, pair), UPPER_BANKS + 2 * (j % 2) + pair)
-                e_psum[h, j, pair] = bank
+                bank = psum_bank("e%d%d" % (j, pair), banks[pair])
+                e_psum[j, pair] = bank
                 for gg in range(2):
-                    first_word = (2 * pair + gg) * PASS // 2
                     for u in range(2):
-                        src = words[:, first_word + u : first_word + PASS // 2 : 2]
-                        nc.tensor.transpose(bank[:, block(2 * gg + u)], src, to_slots[:])
+                        nc.tensor.transpose(bank[:, block(2 * gg + u)], words[:, 2 * pair + gg, u, :], ident[:])
 
-        def pack_e(h, j):
-            for pair in range(K_PASSES // 2):
-                dst = e_packed[h][pair][:].bitcast(F32).rearrange("p g (t j c u) -> p j g t c u", t=PACK, j=ROW_TILES, u=2)
-                src = e_psum[h, j, pair][:].rearrange("p (g u t c) -> p g t c u", g=2, u=2, t=PACK)
-                nc.scalar.copy(out=dst[:, j], in_=src)
+        def pack_e(engine, j, pair):
+            dst = e_packed[j % STAGE_BUFS][:, block(pair, K // 2)].bitcast(F32).rearrange("p (g r u) -> p g r u", g=2, u=2)
+            copy_on(engine, dst, e_psum[j, pair][:].rearrange("p (g u r) -> p g r u", g=2, u=2))
 
-        def quantize_e(h, g):
-            quantize(e_codes[h][g][:], e_scale[h][g][:], e_packed[h][g // 2][:, g % 2, :])
+        def quantize_e(j):
+            quantize(e_codes[j][:], e_scale[j][:], e_packed[j % STAGE_BUFS][:])
 
         def pack_x(g):
             nc.vector.tensor_copy(
@@ -185,138 +214,218 @@ def tile_cross_backward_error_s12_kernel(tc, e, x, u_words, u_scales, v_words, v
         def quantize_x(g):
             quantize(x_codes[g][:], x_scale[g][:], x_packed[g][:].rearrange("p n i -> p (n i)"))
 
-        def r_chunk(h, c):
-            bank = psum_bank("r%d%d" % (h, c), c + (UPPER_BANKS if h == 0 else 0))
-            for t in range(PACK):
-                for g in range(K_PASSES):
-                    nc.tensor.matmul_mx(
-                        out=bank[:, block(t)],
-                        lhsT=e_codes[h][g][:, block(t)].bitcast(FP8X4),
-                        lhsT_scale=e_scale[h][g][:, block(t)],
-                        rhs=x_codes[g][:, block(c)].bitcast(FP8X4),
-                        rhs_scale=x_scale[g][:, block(c)],
-                        start=(g == 0),
-                        stop=(g == K_PASSES - 1),
-                    )
-            src = bank[:].rearrange("p (t n) -> p n t", t=PACK)
+        r_psum = {}
+        r_count = {}
+
+        def r_matmul(j, g, c, bank):
+            h, t = divmod(j, PACK)
+            if (h, c) not in r_psum:
+                r_psum[h, c] = psum_bank("r%d%d" % (h, c), bank)
+            done = r_count.get((h, c), 0)
+            r_count[h, c] = done + 1
+            nc.tensor.matmul_mx(
+                out=r_psum[h, c][:, block(t)],
+                lhsT=e_codes[j][:, block(g)].bitcast(FP8X4),
+                lhsT_scale=e_scale[j][:, block(g)],
+                rhs=x_codes[g][:, block(c)].bitcast(FP8X4),
+                rhs_scale=x_scale[g][:, block(c)],
+                start=(done == 0),
+                stop=(done == PACK * K_PASSES - 1),
+            )
+
+        def r_slot(j, passes, chunks=range(CHUNKS)):
+            for g in passes:
+                for c in chunks:
+                    r_matmul(j, g, c, R_BANKS[j // PACK][c])
+
+        def abs_r(h, c):
+            src = r_psum[h, c][:].rearrange("p (t n) -> p n t", t=PACK)
             nc.scalar.activation(out=r_packed[h][:, block(c), :], in_=src, func=FUNC.Abs)
 
         def quantize_r(h, cols):
             quantize(r_codes[h][:, cols], r_scale[h][:, cols], r_packed[h][:, cols, :].rearrange("p n t -> p (n t)"))
 
-        def out_chunk(c):
-            bank = psum_bank("out%d" % c, UPPER_BANKS + c)
-            for h in range(HALVES):
-                nc.tensor.matmul_mx(
-                    out=bank[:],
-                    lhsT=r_codes[h][:, block(c)].bitcast(FP8X4),
-                    lhsT_scale=r_scale[h][:, block(c)],
-                    rhs=w_codes[h][:].bitcast(FP8X4),
-                    rhs_scale=w_scale[h][:],
-                    start=(h == 0),
-                    stop=(h == HALVES - 1),
-                )
-            if c % 2 == 0:
-                nc.scalar.copy(out=out_rows[c][:], in_=bank[:])
-            else:
-                nc.vector.tensor_copy(out=out_rows[c][:], in_=bank[:])
+        out_psum = {}
+
+        def out_matmul(h, c):
+            if h == 0:
+                out_psum[c] = psum_bank("out%d" % c, OUT_BANKS[c])
+            nc.tensor.matmul_mx(
+                out=out_psum[c][:],
+                lhsT=r_codes[h][:, block(c)].bitcast(FP8X4),
+                lhsT_scale=r_scale[h][:, block(c)],
+                rhs=w_codes[h][:].bitcast(FP8X4),
+                rhs_scale=w_scale[h][:],
+                start=(h == 0),
+                stop=(h == HALVES - 1),
+            )
+
+        def store(engine, c):
+            copy_on(engine, out_rows[c][:], out_psum[c][:])
             nc.sync.dma_start(out=out[block(c), :], in_=out_rows[c][:])
 
         ctx.enter_context(tc.manual_schedule())
 
-        nc.vector.memset(u_scale_in[:].rearrange("p g n -> p (g n)").bitcast(I32), 0)
-        nc.vector.memset(v_scale[:].rearrange("p g n -> p (g n)").bitcast(I32), 0)
+        zero(u_scale_in[0])
+        zero(v_scale)
+        zero(u_scale_in[1])
         make_identity(nc, ident[:])
-
-        load_u_codes(FIRST_PAIR)
-        load_scale_rows(u_scale_in, u_scales)
-        load_v_codes(0)
+        load_u_codes(0, slice(0, 2))
+        load_v_codes(slice(0, 2))
+        load_scale_rows(u_scale_in[0], u_scales[:, :, block(0, PASS)])
         load_scale_rows(v_scale, v_scales)
-        load_u_codes(SECOND_PAIR)
-        load_v_codes(1)
-        load_b(0)
-        load_e(0, 0)
+        load_u_codes(0, slice(2, 4))
+        load_v_codes(slice(2, 4))
+        load_e(0)
         load_x(0)
-        load_e(0, 1)
-        load_x(1)
-        load_e(0, 2)
-        load_e(0, 3)
-        load_x(2)
-        load_e(1, 0)
-        load_e(1, 1)
-        load_x(3)
-        load_e(1, 2)
-        load_e(1, 3)
+        load_b(0)
         load_b(1)
-
-        nc.vector.tensor_copy(
-            out=to_slots[:].rearrange("p (t q s) -> p t q s", t=PACK, s=4),
-            in_=ident[:].rearrange("p (q t s) -> p t q s", t=PACK, s=4),
-        )
-
-        order_u_codes(0, FIRST_PAIR)
+        load_scale_rows(u_scale_in[1], u_scales[:, :, block(1, PASS)])
+        load_u_codes(1, slice(0, 2))
+        load_e(1)
+        load_b(2)
+        load_b(3)
+        load_u_codes(1, slice(2, 4))
+        load_x(1)
+        load_e(2)
+        load_b(4)
+        load_b(5)
+        load_x(2)
+        load_e(3)
+        load_x(3)
+        load_e(4)
+        load_b(6)
+        load_b(7)
+        load_e(5)
+        load_e(6)
+        load_e(7)
+        order_u_codes(0, slice(0, 2))
         order_u_scale(0)
-        order_u_scale(1)
-        order_u_codes(0, SECOND_PAIR)
-        order_u_codes(1, ALL_PASSES)
-        for t in range(PACK):
-            d_matmul(0, t, FIRST_PAIR)
-        for t in range(PACK):
-            d_matmul(0, t, SECOND_PAIR)
-            add_b(0, t)
-
-        transpose_e(0, 0)
-        d_matmul(1, 0, ALL_PASSES)
-        rsqrt_d(0, 0)
-        pack_e(0, 0)
-        transpose_e(0, 1)
-        d_matmul(1, 1, ALL_PASSES)
-        pack_e(0, 1)
+        order_u_codes(0, slice(2, 4))
         pack_x(0)
-        pack_x(1)
+        d_matmul(0, slice(0, 2), 0)
+        d_matmul(1, slice(0, 2), 1)
+        d_matmul(0, slice(2, 4), 0)
+        d_matmul(1, slice(2, 4), 1)
+        transpose_e(0, (6, 7), False)
+        d_matmul(2, slice(0, 4), 2)
+        d_matmul(3, slice(0, 4), 3)
+        add_b(0)
+        order_u_scale(1)
+        order_u_codes(1, slice(0, 2))
+        add_b(1)
         quantize_x(0)
-        square_on_vector(0, 0)
+        pack_e("scalar", 0, 0)
+        pack_e("scalar", 0, 1)
+        rsqrt_d(0, slice(0, 2))
+        d_matmul(4, slice(0, 2), 4)
+        d_matmul(5, slice(0, 2), 5)
+        transpose_e(1, (6, 7), False)
+        quantize_e(0)
+        add_b(2)
+        order_u_codes(1, slice(2, 4))
+        add_b(3)
+        pack_x(1)
+        pack_e("scalar", 1, 0)
+        pack_e("scalar", 1, 1)
+        rsqrt_d(0, slice(2, 4))
+        square("scalar", 0, slice(0, 256))
+        d_matmul(4, slice(2, 4), 4)
+        d_matmul(5, slice(2, 4), 5)
+        d_matmul(6, slice(0, 4), 0)
+        transpose_e(2, (6, 7), False)
+        d_matmul(7, slice(0, 4), 1)
+        quantize_e(1)
         quantize_x(1)
-        for j in (2, 3):
-            transpose_e(0, j)
-            pack_e(0, j)
-        d_matmul(1, 2, ALL_PASSES)
-        rsqrt_d(0, 1)
+        add_b(4)
+        add_b(5)
         pack_x(2)
-        quantize_e(0, 0)
+        pack_e("scalar", 2, 0)
+        pack_e("scalar", 2, 1)
+        split_e("scalar", 3)
+        square("scalar", 0, slice(256, 512))
+        r_slot(0, range(0, 2), range(0, 4))
+        r_slot(1, range(0, 2), range(0, 4))
+        transpose_e(3, (6, 7), True)
+        quantize_e(2)
         quantize_x(2)
-        quantize_e(0, 1)
         pack_x(3)
-        quantize_e(0, 2)
-        quantize_e(0, 3)
+        split_e("vector", 4)
         quantize_x(3)
-        for j in (0, 1):
-            transpose_e(1, j)
-            pack_e(1, j)
-        d_matmul(1, 3, ALL_PASSES)
-        for j in (2, 3):
-            transpose_e(1, j)
-            pack_e(1, j)
-        square_on_scalar(0, 1)
-
-        for t in range(PACK):
-            add_b(1, t)
-        for g in range(K_PASSES):
-            quantize_e(1, g)
-        r_chunk(0, 0)
-        r_chunk(0, 1)
-        rsqrt_d(1, 0)
-        rsqrt_d(1, 1)
-        r_chunk(0, 2)
-        r_chunk(0, 3)
+        pack_e("scalar", 3, 0)
+        pack_e("scalar", 3, 1)
+        rsqrt_d(1, slice(0, 2))
+        r_slot(2, range(0, 2), range(0, 4))
+        r_slot(0, range(2, 3), range(0, 4))
+        r_slot(1, range(2, 3), range(0, 4))
+        r_slot(2, range(2, 3), range(0, 4))
+        transpose_e(4, (6, 7), True)
+        r_slot(0, range(3, 4), range(0, 4))
+        r_slot(1, range(3, 4), range(0, 4))
+        r_slot(2, range(3, 4), range(0, 4))
+        quantize_e(3)
+        split_e("vector", 5)
+        add_b(6)
+        add_b(7)
+        split_e("vector", 6)
+        pack_e("scalar", 4, 0)
+        pack_e("scalar", 4, 1)
+        rsqrt_d(1, slice(2, 3))
+        r_slot(3, range(0, 4), range(0, 2))
+        transpose_e(5, (6, 7), True)
+        r_slot(3, range(0, 4), range(2, 4))
+        transpose_e(6, (0, 1), True)
+        quantize_e(4)
+        split_e("vector", 7)
+        pack_e("vector", 5, 1)
         quantize_w(0)
-        square_on_vector(1, 0)
-        square_on_vector(1, 1)
-        quantize_r(0, slice(0, N))
+        abs_r(0, 0)
+        abs_r(0, 1)
+        pack_e("scalar", 5, 0)
+        abs_r(0, 2)
+        pack_e("scalar", 6, 0)
+        abs_r(0, 3)
+        transpose_e(7, (2, 3), True)
+        r_slot(4, range(0, 4), range(0, 2))
+        quantize_e(5)
+        pack_e("vector", 6, 1)
+        pack_e("vector", 7, 1)
+        quantize_e(6)
+        pack_e("scalar", 7, 0)
+        rsqrt_d(1, slice(3, 4))
+        square("scalar", 1, slice(256, 512))
+        r_slot(5, range(0, 4), range(0, 2))
+        r_slot(4, range(0, 4), range(2, 4))
+        r_slot(5, range(0, 4), range(2, 4))
+        r_slot(6, range(0, 4), range(0, 1))
+        quantize_e(7)
+        square("vector", 1, slice(0, 256))
+        quantize_r(0, slice(0, 512))
         quantize_w(1)
-
-        for c in range(CHUNKS):
-            r_chunk(1, c)
-            quantize_r(1, block(c))
-        for c in range(CHUNKS):
-            out_chunk(c)
+        r_slot(7, range(0, 4), range(0, 1))
+        r_slot(6, range(0, 4), range(1, 2))
+        r_slot(7, range(0, 4), range(1, 2))
+        r_slot(6, range(0, 4), range(2, 3))
+        r_slot(7, range(0, 4), range(2, 3))
+        r_slot(6, range(0, 4), range(3, 4))
+        r_slot(7, range(0, 4), range(3, 4))
+        out_matmul(0, 0)
+        abs_r(1, 0)
+        abs_r(1, 1)
+        abs_r(1, 2)
+        abs_r(1, 3)
+        quantize_r(1, slice(0, 128))
+        quantize_r(1, slice(128, 256))
+        quantize_r(1, slice(256, 384))
+        quantize_r(1, slice(384, 512))
+        out_matmul(1, 0)
+        out_matmul(0, 1)
+        out_matmul(1, 1)
+        out_matmul(0, 2)
+        out_matmul(1, 2)
+        out_matmul(0, 3)
+        out_matmul(1, 3)
+        store("scalar", 0)
+        store("vector", 1)
+        store("scalar", 2)
+        store("vector", 3)

@@ -10,6 +10,7 @@ F32 = mybir.dt.float32
 BF16 = mybir.dt.bfloat16
 I32 = mybir.dt.int32
 U32 = mybir.dt.uint32
+U16 = mybir.dt.uint16
 U8 = mybir.dt.uint8
 FP8X4 = mybir.dt.float8_e4m3fn_x4
 FP4X4 = mybir.dt.float4_e2m1fn_x4
@@ -22,7 +23,6 @@ PASS = P * PACK
 K_PASSES = K // PASS
 HALVES = M // PASS
 SLOTS = HALVES * PACK
-RUN = 8
 CHUNKS = N // P
 W_PIECE = N // 2
 BANK = 512
@@ -60,13 +60,13 @@ def tile_cross_backward_error_s12_kernel(tc, e, x, u_words, u_scales, v_words, v
         x_packed = sbufs("x_packed", K_PASSES, [P, N, PACK], BF16)
         x_codes = sbufs("x_codes", K_PASSES, [P, N], U32)
         x_scale = sbufs("x_scale", K_PASSES, [P, N], U8)
-        u_codes_in = sbufs("u_codes_in", HALVES, [P, K_PASSES * 2 * PASS], U8)
-        u_scale_in = sbufs("u_scale_in", HALVES, [P, K_PASSES, PASS], U8)
-        u_codes = sbufs("u_codes", HALVES, [P, K_PASSES * 2 * PASS], U8)
-        u_scale = sbufs("u_scale", HALVES, [P, K_PASSES, PASS], U8)
+        u_codes_in = sbuf("u_codes_in", [P, K_PASSES * 2 * M], U8)
+        u_scale_in = sbuf("u_scale_in", [P, K_PASSES, M], U8)
+        u_codes = sbuf("u_codes", [P, K_PASSES * 2 * M], U8)
+        u_scale = sbuf("u_scale", [P, K_PASSES * M], U8)
         v_codes = sbuf("v_codes", [P, K_PASSES * 2 * N], U8)
         v_scale = sbuf("v_scale", [P, K_PASSES, N], U8)
-        b_slots = sbufs("b_slots", SLOTS, [P, N], BF16)
+        b_slots = sbufs("b_slots", HALVES, [P, PACK * N], BF16)
         d_slots = sbufs("d_slots", HALVES, [P, PACK, N], F32)
         d_rsqrt = sbufs("d_rsqrt", HALVES, [P, PACK, N], F32)
         w_packed = sbufs("w_packed", HALVES, [P, N, PACK], BF16)
@@ -89,32 +89,25 @@ def tile_cross_backward_error_s12_kernel(tc, e, x, u_words, u_scales, v_words, v
             else:
                 nc.vector.tensor_copy(out=dst, in_=src)
 
-        def pass_range(tile, passes):
-            cols = slice(passes.start * 2 * PASS, passes.stop * 2 * PASS)
-            return tile[:, cols].bitcast(I32).rearrange("p (g w) -> p g w", w=PASS // 2)
-
-        def load_u_codes(h, passes):
-            src = u_words[passes, :, block(h, 2 * PASS)].rearrange("g p n -> p g n")
-            nc.sync.dma_start(out=pass_range(u_codes_in[h], passes), in_=src.bitcast(I32))
-
-        def load_v_codes(passes):
-            src = v_words[passes].rearrange("g p n -> p g n")
-            nc.sync.dma_start(out=pass_range(v_codes, passes), in_=src.bitcast(I32))
+        def load_codes(tile, words, passes):
+            width = words.shape[2]
+            dst = tile[:, passes.start * width : passes.stop * width].bitcast(I32)
+            src = words[passes].rearrange("g p n -> p g n").bitcast(I32)
+            nc.sync.dma_start(out=dst.rearrange("p (g w) -> p g w", w=width // 4), in_=src)
 
         def load_scale_rows(tile, rows):
             for r in range(4):
                 src = rows[:, r:16:4, :].rearrange("g b n -> b g n")
                 nc.sync.dma_start(out=tile[r:P:32].bitcast(I32), in_=src.bitcast(I32))
 
-        def slot_rows(matrix, j):
-            h, t = divmod(j, PACK)
-            return matrix[block(h, PASS), :].rearrange("(b t r) n -> t b r n", t=PACK, r=RUN)[t]
-
-        def load_b(j):
-            nc.sync.dma_start(out=b_slots[j][:], in_=slot_rows(b_abs, j))
+        def load_b(h, slots):
+            rows = b_abs[block(h, PASS), :].rearrange("(p t) n -> p (t n)", t=PACK)
+            cols = slice(slots.start * N, slots.stop * N)
+            nc.sync.dma_start(out=b_slots[h][:, cols], in_=rows[:, cols])
 
         def load_e(j):
-            nc.sync.dma_start(out=e_rows[j][:], in_=slot_rows(e, j))
+            h, t = divmod(j, PACK)
+            nc.sync.dma_start(out=e_rows[j][:], in_=e[h * PASS + t : (h + 1) * PASS : PACK, :])
 
         def load_x(g):
             nc.sync.dma_start(out=x_rows[g][:], in_=x[block(g, PASS), :].rearrange("(p i) n -> p i n", i=PACK))
@@ -122,29 +115,30 @@ def tile_cross_backward_error_s12_kernel(tc, e, x, u_words, u_scales, v_words, v
         def zero(tile):
             nc.vector.memset(tile[:].rearrange("p g n -> p (g n)").bitcast(I32), 0)
 
-        def order_u_codes(h, passes):
+        def by_slot(dst, src):
             nc.vector.tensor_copy(
-                out=pass_range(u_codes[h], passes).rearrange("p g (t b a) -> p g t b a", t=PACK, a=RUN // 2),
-                in_=pass_range(u_codes_in[h], passes).rearrange("p g (b t a) -> p g t b a", t=PACK, a=RUN // 2),
+                out=dst.rearrange("p (a t m) -> p a t m", t=PACK, m=P),
+                in_=src.rearrange("p (a m t) -> p a t m", t=PACK, m=P),
             )
 
-        def order_u_scale(h):
-            nc.vector.tensor_copy(
-                out=u_scale[h][:].bitcast(I32).rearrange("p g (t b a) -> p g t b a", t=PACK, a=RUN // 4),
-                in_=u_scale_in[h][:].bitcast(I32).rearrange("p g (b t a) -> p g t b a", t=PACK, a=RUN // 4),
-            )
+        def order_u_codes(passes):
+            cols = slice(passes.start * 2 * M, passes.stop * 2 * M)
+            by_slot(u_codes[:, cols].bitcast(U16), u_codes_in[:, cols].bitcast(U16))
+
+        def order_u_scale(passes):
+            cols = slice(passes.start * M, passes.stop * M)
+            by_slot(u_scale[:, cols], u_scale_in[:].rearrange("p g n -> p (g n)")[:, cols])
 
         d_psum = {}
 
         def d_matmul(j, passes, bank):
-            h, t = divmod(j, PACK)
             if passes.start == 0:
                 d_psum[j] = psum_bank("d%d" % j, bank)
             for g in range(passes.start, passes.stop):
                 nc.tensor.matmul_mx(
                     out=d_psum[j][:],
-                    lhsT=u_codes[h][:, block(PACK * g + t, 2 * P)].bitcast(FP4X4),
-                    lhsT_scale=u_scale[h][:, g, block(t)],
+                    lhsT=u_codes[:, block(SLOTS * g + j, 2 * P)].bitcast(FP4X4),
+                    lhsT_scale=u_scale[:, block(SLOTS * g + j)],
                     rhs=v_codes[:, block(g, 2 * N)].bitcast(FP4X4),
                     rhs_scale=v_scale[:, g, :],
                     start=(g == 0),
@@ -153,7 +147,7 @@ def tile_cross_backward_error_s12_kernel(tc, e, x, u_words, u_scales, v_words, v
 
         def add_b(j):
             h, t = divmod(j, PACK)
-            nc.vector.tensor_tensor(out=d_slots[h][:, t, :], in0=d_psum[j][:], in1=b_slots[j][:], op=ALU.add)
+            nc.vector.tensor_tensor(out=d_slots[h][:, t, :], in0=d_psum[j][:], in1=b_slots[h][:, block(t, N)], op=ALU.add)
 
         def empty_d(j):
             h, t = divmod(j, PACK)
@@ -161,7 +155,7 @@ def tile_cross_backward_error_s12_kernel(tc, e, x, u_words, u_scales, v_words, v
 
         def add_b_sbuf(j):
             h, t = divmod(j, PACK)
-            nc.vector.tensor_tensor(out=d_slots[h][:, t, :], in0=d_slots[h][:, t, :], in1=b_slots[j][:], op=ALU.add)
+            nc.vector.tensor_tensor(out=d_slots[h][:, t, :], in0=d_slots[h][:, t, :], in1=b_slots[h][:, block(t, N)], op=ALU.add)
 
         def rsqrt_d(h, slots):
             nc.scalar.activation(out=d_rsqrt[h][:, slots, :], in_=d_slots[h][:, slots, :], func=FUNC.Abs_reciprocal_sqrt)
@@ -205,10 +199,11 @@ def tile_cross_backward_error_s12_kernel(tc, e, x, u_words, u_scales, v_words, v
         def quantize_e(j):
             quantize(e_codes[j][:], e_scale[j][:], e_packed[j % STAGE_BUFS][:])
 
-        def pack_x(g):
-            nc.vector.tensor_copy(
-                out=x_packed[g][:].rearrange("p (c a) i -> p c i a", a=4),
-                in_=x_rows[g][:].rearrange("p i (c a) -> p c i a", a=4),
+        def pack_x(engine, g):
+            copy_on(
+                engine,
+                x_packed[g][:].rearrange("p (c a) i -> p c i a", a=4),
+                x_rows[g][:].rearrange("p i (c a) -> p c i a", a=4),
             )
 
         def quantize_x(g):
@@ -266,114 +261,122 @@ def tile_cross_backward_error_s12_kernel(tc, e, x, u_words, u_scales, v_words, v
 
         ctx.enter_context(tc.manual_schedule())
 
-        zero(u_scale_in[0])
+        zero(u_scale_in)
         zero(v_scale)
-        zero(u_scale_in[1])
         make_identity(nc, ident[:])
-        load_u_codes(0, slice(0, 2))
-        load_v_codes(slice(0, 2))
-        load_scale_rows(u_scale_in[0], u_scales[:, :, block(0, PASS)])
+        load_codes(u_codes_in, u_words, slice(0, 1))
+        load_scale_rows(u_scale_in, u_scales)
+        load_codes(v_codes, v_words, slice(0, 1))
         load_scale_rows(v_scale, v_scales)
-        load_u_codes(0, slice(2, 4))
-        load_v_codes(slice(2, 4))
         load_e(0)
+        load_codes(u_codes_in, u_words, slice(1, 2))
+        load_codes(v_codes, v_words, slice(1, 2))
+        load_codes(u_codes_in, u_words, slice(2, 4))
+        load_codes(v_codes, v_words, slice(2, 4))
         load_x(0)
-        load_b(0)
-        load_b(1)
-        load_scale_rows(u_scale_in[1], u_scales[:, :, block(1, PASS)])
-        load_u_codes(1, slice(0, 2))
+        load_b(0, slice(0, 2))
         load_e(1)
-        load_b(2)
-        load_b(3)
-        load_u_codes(1, slice(2, 4))
+        load_b(0, slice(2, 4))
         load_x(1)
         load_e(2)
-        load_b(4)
-        load_b(5)
+        load_b(1, slice(0, 2))
         load_x(2)
         load_e(3)
         load_x(3)
         load_e(4)
-        load_b(6)
-        load_b(7)
+        load_b(1, slice(2, 4))
         load_e(5)
         load_e(6)
         load_e(7)
-        order_u_codes(0, slice(0, 2))
-        order_u_scale(0)
-        order_u_codes(0, slice(2, 4))
-        pack_x(0)
-        d_matmul(0, slice(0, 2), 0)
-        d_matmul(1, slice(0, 2), 1)
+        order_u_codes(slice(0, 1))
+        order_u_scale(slice(0, 1))
+        order_u_scale(slice(1, 2))
+        order_u_codes(slice(1, 2))
+        order_u_scale(slice(2, 4))
+        order_u_codes(slice(2, 3))
+        order_u_codes(slice(3, 4))
+        pack_x("vector", 0)
+        split_e("scalar", 0)
+        d_matmul(0, slice(0, 1), 0)
+        d_matmul(1, slice(0, 1), 1)
+        d_matmul(2, slice(0, 1), 2)
+        d_matmul(3, slice(0, 1), 3)
+        d_matmul(4, slice(0, 1), 4)
+        d_matmul(5, slice(0, 1), 5)
+        transpose_e(0, (6, 7), True)
+        d_matmul(0, slice(1, 2), 0)
+        d_matmul(1, slice(1, 2), 1)
+        d_matmul(2, slice(1, 2), 2)
+        d_matmul(3, slice(1, 2), 3)
+        d_matmul(4, slice(1, 2), 4)
+        d_matmul(5, slice(1, 2), 5)
         d_matmul(0, slice(2, 4), 0)
         d_matmul(1, slice(2, 4), 1)
-        transpose_e(0, (6, 7), False)
-        d_matmul(2, slice(0, 4), 2)
-        d_matmul(3, slice(0, 4), 3)
+        d_matmul(2, slice(2, 4), 2)
+        d_matmul(3, slice(2, 4), 3)
+        d_matmul(4, slice(2, 4), 4)
         add_b(0)
-        order_u_scale(1)
-        order_u_codes(1, slice(0, 2))
-        add_b(1)
-        quantize_x(0)
         pack_e("scalar", 0, 0)
         pack_e("scalar", 0, 1)
-        rsqrt_d(0, slice(0, 2))
-        d_matmul(4, slice(0, 2), 4)
-        d_matmul(5, slice(0, 2), 5)
+        rsqrt_d(0, slice(0, 1))
         transpose_e(1, (6, 7), False)
-        quantize_e(0)
-        add_b(2)
-        order_u_codes(1, slice(2, 4))
-        add_b(3)
-        pack_x(1)
-        pack_e("scalar", 1, 0)
-        pack_e("scalar", 1, 1)
-        rsqrt_d(0, slice(2, 4))
-        square("scalar", 0, slice(0, 256))
-        d_matmul(4, slice(2, 4), 4)
         d_matmul(5, slice(2, 4), 5)
         d_matmul(6, slice(0, 4), 0)
-        transpose_e(2, (6, 7), False)
-        d_matmul(7, slice(0, 4), 1)
-        quantize_e(1)
-        quantize_x(1)
-        add_b(4)
-        add_b(5)
-        pack_x(2)
-        pack_e("scalar", 2, 0)
-        pack_e("scalar", 2, 1)
+        quantize_e(0)
+        add_b(1)
+        quantize_x(0)
+        add_b(2)
+        add_b(3)
+        pack_x("vector", 1)
+        rsqrt_d(0, slice(1, 2))
+        pack_e("scalar", 1, 0)
+        pack_e("scalar", 1, 1)
+        split_e("scalar", 2)
+        rsqrt_d(0, slice(2, 4))
         split_e("scalar", 3)
-        square("scalar", 0, slice(256, 512))
+        d_matmul(7, slice(0, 4), 1)
+        transpose_e(2, (6, 7), True)
+        quantize_e(1)
+        add_b(4)
+        quantize_x(1)
+        add_b(5)
+        pack_x("vector", 2)
+        pack_e("vector", 2, 1)
+        quantize_x(2)
+        pack_e("scalar", 2, 0)
+        square("scalar", 0, slice(0, 256))
         r_slot(0, range(0, 2), range(0, 4))
         r_slot(1, range(0, 2), range(0, 4))
         transpose_e(3, (6, 7), True)
-        quantize_e(2)
-        quantize_x(2)
-        pack_x(3)
-        split_e("vector", 4)
-        quantize_x(3)
-        pack_e("scalar", 3, 0)
-        pack_e("scalar", 3, 1)
-        rsqrt_d(1, slice(0, 2))
-        r_slot(2, range(0, 2), range(0, 4))
         r_slot(0, range(2, 3), range(0, 4))
         r_slot(1, range(2, 3), range(0, 4))
-        r_slot(2, range(2, 3), range(0, 4))
+        quantize_e(2)
+        split_e("vector", 4)
+        pack_x("vector", 3)
+        pack_e("scalar", 3, 0)
+        pack_e("scalar", 3, 1)
+        split_e("scalar", 5)
+        square("scalar", 0, slice(256, 512))
+        r_slot(2, range(0, 3), range(0, 4))
         transpose_e(4, (6, 7), True)
-        r_slot(0, range(3, 4), range(0, 4))
-        r_slot(1, range(3, 4), range(0, 4))
-        r_slot(2, range(3, 4), range(0, 4))
         quantize_e(3)
-        split_e("vector", 5)
+        quantize_x(3)
         add_b(6)
         add_b(7)
         split_e("vector", 6)
         pack_e("scalar", 4, 0)
         pack_e("scalar", 4, 1)
-        rsqrt_d(1, slice(2, 3))
-        r_slot(3, range(0, 4), range(0, 2))
+        rsqrt_d(1, slice(0, 2))
+        r_slot(3, range(0, 3), range(0, 4))
+        r_slot(0, range(3, 4), range(0, 2))
+        r_slot(1, range(3, 4), range(0, 2))
+        r_slot(2, range(3, 4), range(0, 2))
+        r_slot(3, range(3, 4), range(0, 2))
         transpose_e(5, (6, 7), True)
-        r_slot(3, range(0, 4), range(2, 4))
+        r_slot(0, range(3, 4), range(2, 4))
+        r_slot(1, range(3, 4), range(2, 4))
+        r_slot(2, range(3, 4), range(2, 4))
+        r_slot(3, range(3, 4), range(2, 4))
         transpose_e(6, (0, 1), True)
         quantize_e(4)
         split_e("vector", 7)
@@ -392,15 +395,15 @@ def tile_cross_backward_error_s12_kernel(tc, e, x, u_words, u_scales, v_words, v
         pack_e("vector", 7, 1)
         quantize_e(6)
         pack_e("scalar", 7, 0)
-        rsqrt_d(1, slice(3, 4))
+        rsqrt_d(1, slice(2, 4))
         square("scalar", 1, slice(256, 512))
         r_slot(5, range(0, 4), range(0, 2))
         r_slot(4, range(0, 4), range(2, 4))
         r_slot(5, range(0, 4), range(2, 4))
         r_slot(6, range(0, 4), range(0, 1))
         quantize_e(7)
-        square("vector", 1, slice(0, 256))
         quantize_r(0, slice(0, 512))
+        square("vector", 1, slice(0, 256))
         quantize_w(1)
         r_slot(7, range(0, 4), range(0, 1))
         r_slot(6, range(0, 4), range(1, 2))

@@ -115,19 +115,19 @@ def tile_cross_backward_error_s12_kernel(tc, e, x, u_words, u_scales, v_words, v
         def zero(tile):
             nc.vector.memset(tile[:].rearrange("p g n -> p (g n)").bitcast(I32), 0)
 
-        def by_slot(dst, src):
+        def by_slot(dst, src, line):
             nc.vector.tensor_copy(
-                out=dst.rearrange("p (a t m) -> p a t m", t=PACK, m=P),
-                in_=src.rearrange("p (a m t) -> p a t m", t=PACK, m=P),
+                out=dst.rearrange("p (a t c i) -> p a c t i", t=PACK, c=P // line, i=line),
+                in_=src.rearrange("p (a c i t) -> p a c t i", t=PACK, c=P // line, i=line),
             )
 
         def order_u_codes(passes):
             cols = slice(passes.start * 2 * M, passes.stop * 2 * M)
-            by_slot(u_codes[:, cols].bitcast(U16), u_codes_in[:, cols].bitcast(U16))
+            by_slot(u_codes[:, cols].bitcast(U16), u_codes_in[:, cols].bitcast(U16), 8)
 
         def order_u_scale(passes):
             cols = slice(passes.start * M, passes.stop * M)
-            by_slot(u_scale[:, cols], u_scale_in[:].rearrange("p g n -> p (g n)")[:, cols])
+            by_slot(u_scale[:, cols], u_scale_in[:].rearrange("p g n -> p (g n)")[:, cols], 16)
 
         d_psum = {}
 
@@ -176,8 +176,8 @@ def tile_cross_backward_error_s12_kernel(tc, e, x, u_words, u_scales, v_words, v
         def split_e(engine, j):
             copy_on(
                 engine,
-                e_split[j % STAGE_BUFS][:].rearrange("p (g u w) -> p g u w", g=K_PASSES, u=2),
-                e_rows[j][:].bitcast(F32).rearrange("p (g w u) -> p g u w", g=K_PASSES, u=2),
+                e_split[j % STAGE_BUFS][:].rearrange("p (g u c i) -> p g c u i", g=K_PASSES, u=2, i=4),
+                e_rows[j][:].bitcast(F32).rearrange("p (g c i u) -> p g c u i", g=K_PASSES, u=2, i=4),
             )
 
         def transpose_e(j, banks, split):

@@ -30,8 +30,8 @@ STAGE_BUFS = 3
 
 FIRST_PAIR, SECOND_PAIR, ALL_PASSES = slice(0, 2), slice(2, 4), slice(0, 4)
 
-R_BANKS = ((2, 3, 4, 5), (6, 7, 4, 5))
-OUT_BANKS = (0, 1, 2, 3)
+R_BANKS = ((4, 5, 6, 7), (2, 3, 0, 1))
+OUT_BANKS = (4, 5, 6, 7)
 
 
 def block(i, width=P):
@@ -264,159 +264,165 @@ def tile_cross_backward_error_s12_kernel(tc, e, x, u_words, u_scales, v_words, v
         zero(u_scale_in)
         zero(v_scale)
         make_identity(nc, ident[:])
-        load_codes(u_codes_in, u_words, slice(0, 1))
+        load_e(0)
+        load_e(1)
         load_scale_rows(u_scale_in, u_scales)
+        load_codes(u_codes_in, u_words, slice(0, 1))
         load_codes(v_codes, v_words, slice(0, 1))
         load_scale_rows(v_scale, v_scales)
-        load_e(0)
         load_codes(u_codes_in, u_words, slice(1, 2))
         load_codes(v_codes, v_words, slice(1, 2))
-        load_codes(u_codes_in, u_words, slice(2, 4))
-        load_codes(v_codes, v_words, slice(2, 4))
+        load_codes(u_codes_in, u_words, slice(2, 3))
+        load_codes(v_codes, v_words, slice(2, 3))
+        load_codes(u_codes_in, u_words, slice(3, 4))
+        load_codes(v_codes, v_words, slice(3, 4))
         load_x(0)
         load_b(0, slice(0, 2))
-        load_e(1)
-        load_b(0, slice(2, 4))
         load_x(1)
+        load_b(0, slice(2, 4))
         load_e(2)
-        load_b(1, slice(0, 2))
-        load_x(2)
         load_e(3)
-        load_x(3)
+        load_b(1, slice(0, 2))
         load_e(4)
-        load_b(1, slice(2, 4))
+        load_x(2)
         load_e(5)
+        load_b(1, slice(2, 4))
+        load_x(3)
         load_e(6)
         load_e(7)
-        order_u_codes(slice(0, 1))
+        transpose_e(0, (0, 1), False)
+        transpose_e(1, (2, 3), False)
         order_u_scale(slice(0, 1))
+        order_u_codes(slice(0, 1))
         order_u_scale(slice(1, 2))
         order_u_codes(slice(1, 2))
-        order_u_scale(slice(2, 4))
+        order_u_scale(slice(2, 3))
         order_u_codes(slice(2, 3))
+        order_u_scale(slice(3, 4))
         order_u_codes(slice(3, 4))
-        pack_x("vector", 0)
-        split_e("scalar", 0)
-        d_matmul(0, slice(0, 1), 0)
-        d_matmul(1, slice(0, 1), 1)
-        d_matmul(2, slice(0, 1), 2)
-        d_matmul(3, slice(0, 1), 3)
-        d_matmul(4, slice(0, 1), 4)
-        d_matmul(5, slice(0, 1), 5)
-        transpose_e(0, (6, 7), True)
-        d_matmul(0, slice(1, 2), 0)
-        d_matmul(1, slice(1, 2), 1)
-        d_matmul(2, slice(1, 2), 2)
-        d_matmul(3, slice(1, 2), 3)
-        d_matmul(4, slice(1, 2), 4)
-        d_matmul(5, slice(1, 2), 5)
-        d_matmul(0, slice(2, 4), 0)
-        d_matmul(1, slice(2, 4), 1)
-        d_matmul(2, slice(2, 4), 2)
-        d_matmul(3, slice(2, 4), 3)
-        d_matmul(4, slice(2, 4), 4)
-        add_b(0)
         pack_e("scalar", 0, 0)
         pack_e("scalar", 0, 1)
-        rsqrt_d(0, slice(0, 1))
-        transpose_e(1, (6, 7), False)
-        d_matmul(5, slice(2, 4), 5)
-        d_matmul(6, slice(0, 4), 0)
-        quantize_e(0)
-        add_b(1)
-        quantize_x(0)
-        add_b(2)
-        add_b(3)
-        pack_x("vector", 1)
-        rsqrt_d(0, slice(1, 2))
         pack_e("scalar", 1, 0)
         pack_e("scalar", 1, 1)
-        split_e("scalar", 2)
-        rsqrt_d(0, slice(2, 4))
-        split_e("scalar", 3)
-        d_matmul(7, slice(0, 4), 1)
-        transpose_e(2, (6, 7), True)
+        pack_x("scalar", 0)
+        d_matmul(0, slice(0, 1), 4)
+        d_matmul(1, slice(0, 1), 5)
+        d_matmul(2, slice(0, 1), 6)
+        d_matmul(3, slice(0, 1), 7)
+        d_matmul(4, slice(0, 1), 0)
+        d_matmul(5, slice(0, 1), 1)
+        d_matmul(6, slice(0, 1), 2)
+        d_matmul(7, slice(0, 1), 3)
+        d_matmul(0, slice(1, 2), 4)
+        d_matmul(1, slice(1, 2), 5)
+        d_matmul(2, slice(1, 2), 6)
+        d_matmul(3, slice(1, 2), 7)
+        d_matmul(4, slice(1, 2), 0)
+        d_matmul(5, slice(1, 2), 1)
+        d_matmul(0, slice(2, 3), 4)
+        d_matmul(1, slice(2, 3), 5)
+        d_matmul(2, slice(2, 3), 6)
+        d_matmul(3, slice(2, 3), 7)
+        d_matmul(0, slice(3, 4), 4)
+        d_matmul(1, slice(3, 4), 5)
+        d_matmul(2, slice(3, 4), 6)
+        d_matmul(3, slice(3, 4), 7)
+        d_matmul(4, slice(2, 4), 0)
+        d_matmul(5, slice(2, 4), 1)
+        d_matmul(6, slice(1, 4), 2)
+        quantize_e(0)
         quantize_e(1)
-        add_b(4)
+        add_b(0)
+        add_b(1)
+        pack_x("vector", 1)
+        add_b(2)
+        add_b(3)
+        quantize_x(0)
         quantize_x(1)
+        add_b(4)
         add_b(5)
-        pack_x("vector", 2)
-        pack_e("vector", 2, 1)
-        quantize_x(2)
+        rsqrt_d(0, slice(0, 2))
+        transpose_e(2, (4, 5), False)
+        transpose_e(3, (6, 7), False)
+        d_matmul(7, slice(1, 4), 3)
+        transpose_e(4, (0, 1), False)
         pack_e("scalar", 2, 0)
-        square("scalar", 0, slice(0, 256))
-        r_slot(0, range(0, 2), range(0, 4))
-        r_slot(1, range(0, 2), range(0, 4))
-        transpose_e(3, (6, 7), True)
-        r_slot(0, range(2, 3), range(0, 4))
-        r_slot(1, range(2, 3), range(0, 4))
-        quantize_e(2)
-        split_e("vector", 4)
-        pack_x("vector", 3)
+        pack_e("scalar", 2, 1)
         pack_e("scalar", 3, 0)
         pack_e("scalar", 3, 1)
-        split_e("scalar", 5)
-        square("scalar", 0, slice(256, 512))
-        r_slot(2, range(0, 3), range(0, 4))
-        transpose_e(4, (6, 7), True)
-        quantize_e(3)
-        quantize_x(3)
-        add_b(6)
-        add_b(7)
-        split_e("vector", 6)
         pack_e("scalar", 4, 0)
         pack_e("scalar", 4, 1)
+        rsqrt_d(0, slice(2, 4))
         rsqrt_d(1, slice(0, 2))
-        r_slot(3, range(0, 3), range(0, 4))
-        r_slot(0, range(3, 4), range(0, 2))
-        r_slot(1, range(3, 4), range(0, 2))
-        r_slot(2, range(3, 4), range(0, 2))
-        r_slot(3, range(3, 4), range(0, 2))
-        transpose_e(5, (6, 7), True)
-        r_slot(0, range(3, 4), range(2, 4))
-        r_slot(1, range(3, 4), range(2, 4))
-        r_slot(2, range(3, 4), range(2, 4))
-        r_slot(3, range(3, 4), range(2, 4))
-        transpose_e(6, (0, 1), True)
+        r_slot(0, range(0, 2), range(0, 2))
+        r_slot(1, range(0, 2), range(0, 2))
+        r_slot(0, range(0, 2), range(2, 4))
+        r_slot(1, range(0, 2), range(2, 4))
+        quantize_e(2)
+        quantize_e(3)
+        pack_x("vector", 2)
         quantize_e(4)
-        split_e("vector", 7)
-        pack_e("vector", 5, 1)
-        quantize_w(0)
-        abs_r(0, 0)
-        abs_r(0, 1)
+        quantize_x(2)
+        add_b(6)
+        add_b(7)
+        pack_x("vector", 3)
+        r_slot(2, range(0, 2), range(0, 4))
+        transpose_e(5, (0, 1), False)
+        r_slot(3, range(0, 2), range(0, 4))
+        r_slot(0, range(2, 3), range(0, 4))
+        r_slot(1, range(2, 3), range(0, 4))
+        r_slot(2, range(2, 3), range(0, 4))
+        r_slot(3, range(2, 3), range(0, 4))
+        transpose_e(6, (2, 3), False)
         pack_e("scalar", 5, 0)
-        abs_r(0, 2)
+        pack_e("scalar", 5, 1)
+        square("scalar", 0, slice(0, 256))
+        square("scalar", 0, slice(256, 512))
         pack_e("scalar", 6, 0)
-        abs_r(0, 3)
-        transpose_e(7, (2, 3), True)
-        r_slot(4, range(0, 4), range(0, 2))
+        transpose_e(7, (0, 1), False)
         quantize_e(5)
+        quantize_x(3)
         pack_e("vector", 6, 1)
+        quantize_w(0)
         pack_e("vector", 7, 1)
         quantize_e(6)
         pack_e("scalar", 7, 0)
         rsqrt_d(1, slice(2, 4))
-        square("scalar", 1, slice(256, 512))
+        r_slot(0, range(3, 4), range(0, 2))
+        r_slot(1, range(3, 4), range(0, 2))
+        r_slot(2, range(3, 4), range(0, 2))
+        r_slot(3, range(3, 4), range(0, 2))
+        r_slot(0, range(3, 4), range(2, 4))
+        r_slot(1, range(3, 4), range(2, 4))
+        r_slot(2, range(3, 4), range(2, 4))
+        r_slot(3, range(3, 4), range(2, 4))
+        r_slot(4, range(0, 4), range(0, 2))
         r_slot(5, range(0, 4), range(0, 2))
-        r_slot(4, range(0, 4), range(2, 4))
-        r_slot(5, range(0, 4), range(2, 4))
-        r_slot(6, range(0, 4), range(0, 1))
+        r_slot(6, range(0, 4), range(0, 2))
         quantize_e(7)
-        quantize_r(0, slice(0, 512))
         square("vector", 1, slice(0, 256))
-        quantize_w(1)
+        square("vector", 1, slice(256, 512))
+        abs_r(0, 0)
+        abs_r(0, 1)
+        abs_r(0, 2)
+        abs_r(0, 3)
         r_slot(7, range(0, 4), range(0, 1))
-        r_slot(6, range(0, 4), range(1, 2))
         r_slot(7, range(0, 4), range(1, 2))
+        r_slot(4, range(0, 4), range(2, 3))
+        r_slot(5, range(0, 4), range(2, 3))
         r_slot(6, range(0, 4), range(2, 3))
         r_slot(7, range(0, 4), range(2, 3))
+        r_slot(4, range(0, 4), range(3, 4))
+        r_slot(5, range(0, 4), range(3, 4))
         r_slot(6, range(0, 4), range(3, 4))
         r_slot(7, range(0, 4), range(3, 4))
-        out_matmul(0, 0)
+        quantize_r(0, slice(0, 512))
+        quantize_w(1)
         abs_r(1, 0)
         abs_r(1, 1)
         abs_r(1, 2)
         abs_r(1, 3)
+        out_matmul(0, 0)
         quantize_r(1, slice(0, 128))
         quantize_r(1, slice(128, 256))
         quantize_r(1, slice(256, 384))

@@ -259,10 +259,34 @@ def tile_cross_backward_error_s12_kernel(tc, e, x, u_words, u_scales, v_words, v
             copy_on(engine, out_rows[c][:], out_psum[c][:])
             nc.sync.dma_start(out=out[block(c), :], in_=out_rows[c][:])
 
+        table_out = sbuf("table_out", [P, 1], F32)
+
+        def load_table():
+            nc.scalar.activation(out=table_out[:], in_=ident[:, 0:1], func=FUNC.Abs_reciprocal_sqrt, bias=1.0)
+
+        warm = sbuf("warm", [P, K], BF16)
+        warm_codes = sbuf("warm_codes", [P, PASS], U32)
+        warm_scale = sbuf("warm_scale", [P, PASS], U8)
+
+        def warm_up(count):
+            bank = psum_bank("warm_psum", 7)
+            for i in range(count):
+                nc.tensor.matmul_mx(
+                    out=bank[:],
+                    lhsT=warm_codes[:, block(0)].bitcast(FP8X4),
+                    lhsT_scale=warm_scale[:, block(0)],
+                    rhs=warm_codes[:].bitcast(FP8X4),
+                    rhs_scale=warm_scale[:],
+                    start=True,
+                    stop=True,
+                )
+
         ctx.enter_context(tc.manual_schedule())
 
         zero(u_scale_in)
         zero(v_scale)
+        nc.vector.memset(warm[:].bitcast(I32), 0)
+        quantize(warm_codes[:], warm_scale[:], warm[:])
         make_identity(nc, ident[:])
         load_e(0)
         load_e(1)
@@ -290,6 +314,7 @@ def tile_cross_backward_error_s12_kernel(tc, e, x, u_words, u_scales, v_words, v
         load_x(3)
         load_e(6)
         load_e(7)
+        warm_up(4)
         transpose_e(0, (0, 1), False)
         transpose_e(1, (2, 3), False)
         order_u_scale(slice(0, 1))
@@ -300,6 +325,7 @@ def tile_cross_backward_error_s12_kernel(tc, e, x, u_words, u_scales, v_words, v
         order_u_codes(slice(2, 3))
         order_u_scale(slice(3, 4))
         order_u_codes(slice(3, 4))
+        load_table()
         pack_e("scalar", 0, 0)
         pack_e("scalar", 0, 1)
         pack_e("scalar", 1, 0)
@@ -317,8 +343,6 @@ def tile_cross_backward_error_s12_kernel(tc, e, x, u_words, u_scales, v_words, v
         d_matmul(1, slice(1, 2), 5)
         d_matmul(2, slice(1, 2), 6)
         d_matmul(3, slice(1, 2), 7)
-        d_matmul(4, slice(1, 2), 0)
-        d_matmul(5, slice(1, 2), 1)
         d_matmul(0, slice(2, 3), 4)
         d_matmul(1, slice(2, 3), 5)
         d_matmul(2, slice(2, 3), 6)
@@ -327,8 +351,8 @@ def tile_cross_backward_error_s12_kernel(tc, e, x, u_words, u_scales, v_words, v
         d_matmul(1, slice(3, 4), 5)
         d_matmul(2, slice(3, 4), 6)
         d_matmul(3, slice(3, 4), 7)
-        d_matmul(4, slice(2, 4), 0)
-        d_matmul(5, slice(2, 4), 1)
+        d_matmul(4, slice(1, 4), 0)
+        d_matmul(5, slice(1, 4), 1)
         d_matmul(6, slice(1, 4), 2)
         quantize_e(0)
         quantize_e(1)
@@ -342,9 +366,10 @@ def tile_cross_backward_error_s12_kernel(tc, e, x, u_words, u_scales, v_words, v
         add_b(4)
         add_b(5)
         rsqrt_d(0, slice(0, 2))
+        rsqrt_d(0, slice(2, 4))
         transpose_e(2, (4, 5), False)
-        transpose_e(3, (6, 7), False)
         d_matmul(7, slice(1, 4), 3)
+        transpose_e(3, (6, 7), False)
         transpose_e(4, (0, 1), False)
         pack_e("scalar", 2, 0)
         pack_e("scalar", 2, 1)
@@ -352,20 +377,21 @@ def tile_cross_backward_error_s12_kernel(tc, e, x, u_words, u_scales, v_words, v
         pack_e("scalar", 3, 1)
         pack_e("scalar", 4, 0)
         pack_e("scalar", 4, 1)
-        rsqrt_d(0, slice(2, 4))
+        square("scalar", 0, slice(0, 256))
         rsqrt_d(1, slice(0, 2))
         r_slot(0, range(0, 2), range(0, 2))
         r_slot(1, range(0, 2), range(0, 2))
         r_slot(0, range(0, 2), range(2, 4))
         r_slot(1, range(0, 2), range(2, 4))
         quantize_e(2)
-        quantize_e(3)
         pack_x("vector", 2)
-        quantize_e(4)
+        quantize_e(3)
         quantize_x(2)
         add_b(6)
         add_b(7)
         pack_x("vector", 3)
+        quantize_e(4)
+        quantize_x(3)
         r_slot(2, range(0, 2), range(0, 4))
         transpose_e(5, (0, 1), False)
         r_slot(3, range(0, 2), range(0, 4))
@@ -376,18 +402,10 @@ def tile_cross_backward_error_s12_kernel(tc, e, x, u_words, u_scales, v_words, v
         transpose_e(6, (2, 3), False)
         pack_e("scalar", 5, 0)
         pack_e("scalar", 5, 1)
-        square("scalar", 0, slice(0, 256))
         square("scalar", 0, slice(256, 512))
+        rsqrt_d(1, slice(2, 4))
         pack_e("scalar", 6, 0)
         transpose_e(7, (0, 1), False)
-        quantize_e(5)
-        quantize_x(3)
-        pack_e("vector", 6, 1)
-        quantize_w(0)
-        pack_e("vector", 7, 1)
-        quantize_e(6)
-        pack_e("scalar", 7, 0)
-        rsqrt_d(1, slice(2, 4))
         r_slot(0, range(3, 4), range(0, 2))
         r_slot(1, range(3, 4), range(0, 2))
         r_slot(2, range(3, 4), range(0, 2))
@@ -396,16 +414,24 @@ def tile_cross_backward_error_s12_kernel(tc, e, x, u_words, u_scales, v_words, v
         r_slot(1, range(3, 4), range(2, 4))
         r_slot(2, range(3, 4), range(2, 4))
         r_slot(3, range(3, 4), range(2, 4))
+        quantize_e(5)
+        pack_e("vector", 6, 1)
+        quantize_w(0)
+        pack_e("vector", 7, 1)
+        quantize_e(6)
+        pack_e("scalar", 7, 0)
+        square("scalar", 1, slice(256, 512))
+        abs_r(0, 0)
+        abs_r(0, 1)
+        abs_r(0, 2)
+        abs_r(0, 3)
         r_slot(4, range(0, 4), range(0, 2))
         r_slot(5, range(0, 4), range(0, 2))
         r_slot(6, range(0, 4), range(0, 2))
         quantize_e(7)
         square("vector", 1, slice(0, 256))
-        square("vector", 1, slice(256, 512))
-        abs_r(0, 0)
-        abs_r(0, 1)
-        abs_r(0, 2)
-        abs_r(0, 3)
+        quantize_r(0, slice(0, 512))
+        quantize_w(1)
         r_slot(7, range(0, 4), range(0, 1))
         r_slot(7, range(0, 4), range(1, 2))
         r_slot(4, range(0, 4), range(2, 3))
@@ -416,13 +442,11 @@ def tile_cross_backward_error_s12_kernel(tc, e, x, u_words, u_scales, v_words, v
         r_slot(5, range(0, 4), range(3, 4))
         r_slot(6, range(0, 4), range(3, 4))
         r_slot(7, range(0, 4), range(3, 4))
-        quantize_r(0, slice(0, 512))
-        quantize_w(1)
+        out_matmul(0, 0)
         abs_r(1, 0)
         abs_r(1, 1)
         abs_r(1, 2)
         abs_r(1, 3)
-        out_matmul(0, 0)
         quantize_r(1, slice(0, 128))
         quantize_r(1, slice(128, 256))
         quantize_r(1, slice(256, 384))

@@ -24,18 +24,28 @@ K_PASSES = K // PASS
 HALVES = M // PASS
 SLOTS = HALVES * PACK
 CHUNKS = N // P
-W_PIECE = N // 2
 BANK = 512
-STAGE_BUFS = 3
+LINE = 16
+ALIGN = 64
+E_STAGES = 3
+WARM_PASSES = 3
 
-FIRST_PAIR, SECOND_PAIR, ALL_PASSES = slice(0, 2), slice(2, 4), slice(0, 4)
+PAIR_A, PAIR_B, PAIR_C, PAIR_D = (0, 1), (2, 3), (4, 5), (6, 7)
+D_BANKS = PAIR_C + PAIR_D + PAIR_A + PAIR_B
+E_BANKS = (PAIR_A, PAIR_B, PAIR_C, PAIR_D, PAIR_A, PAIR_A, PAIR_B, PAIR_A)
+R_BANKS = (PAIR_C + PAIR_D, PAIR_B + PAIR_A)
+OUT_BANKS = PAIR_C + PAIR_D
+WARM_BANK = D_BANKS[PACK - 1]
 
-R_BANKS = ((4, 5, 6, 7), (2, 3, 0, 1))
-OUT_BANKS = (4, 5, 6, 7)
+LOW, HIGH, ALL = range(0, 2), range(2, 4), range(0, 4)
 
 
 def block(i, width=P):
     return slice(width * i, width * (i + 1))
+
+
+def span(indices, width):
+    return slice(width * indices.start, width * indices.stop)
 
 
 def tile_cross_backward_error_s12_kernel(tc, e, x, u_words, u_scales, v_words, v_scales, b_abs, out):
@@ -45,15 +55,18 @@ def tile_cross_backward_error_s12_kernel(tc, e, x, u_words, u_scales, v_words, v
         psum = ctx.enter_context(tc.psum_pool(name="psum", bufs=1))
 
         def sbuf(name, shape, dtype):
-            return keep.tile(shape, dtype, name=name, align_bytes=64)
+            return keep.tile(shape, dtype, name=name, align_bytes=ALIGN)
 
         def sbufs(name, count, shape, dtype):
             return [sbuf("%s%d" % (name, i), shape, dtype) for i in range(count)]
 
         ident = sbuf("ident", [P, P], F32)
+        warm = sbuf("warm", [P, PASS * PACK], BF16)
+        warm_codes = sbuf("warm_codes", [P, PASS], U32)
+        warm_scale = sbuf("warm_scale", [P, PASS], U8)
+        table_out = sbuf("table_out", [P, 1], F32)
         e_rows = sbufs("e_rows", SLOTS, [P, K], BF16)
-        e_split = sbufs("e_split", STAGE_BUFS, [P, K // 2], F32)
-        e_packed = sbufs("e_packed", STAGE_BUFS, [P, K], BF16)
+        e_packed = sbufs("e_packed", E_STAGES, [P, K], BF16)
         e_codes = sbufs("e_codes", SLOTS, [P, K_PASSES * P], U32)
         e_scale = sbufs("e_scale", SLOTS, [P, K_PASSES * P], U8)
         x_rows = sbufs("x_rows", K_PASSES, [P, PACK, N], BF16)
@@ -66,7 +79,7 @@ def tile_cross_backward_error_s12_kernel(tc, e, x, u_words, u_scales, v_words, v
         u_scale = sbuf("u_scale", [P, K_PASSES * M], U8)
         v_codes = sbuf("v_codes", [P, K_PASSES * 2 * N], U8)
         v_scale = sbuf("v_scale", [P, K_PASSES, N], U8)
-        b_slots = sbufs("b_slots", HALVES, [P, PACK * N], BF16)
+        b_rows = sbufs("b_rows", HALVES, [P, PACK * N], BF16)
         d_slots = sbufs("d_slots", HALVES, [P, PACK, N], F32)
         d_rsqrt = sbufs("d_rsqrt", HALVES, [P, PACK, N], F32)
         w_packed = sbufs("w_packed", HALVES, [P, N, PACK], BF16)
@@ -83,17 +96,14 @@ def tile_cross_backward_error_s12_kernel(tc, e, x, u_words, u_scales, v_words, v
         def quantize(codes, scale, packed):
             nc.vector.quantize_mx(out=codes.bitcast(FP8X4), scales=scale, in_=packed)
 
-        def copy_on(engine, dst, src):
-            if engine == "scalar":
-                nc.scalar.copy(out=dst, in_=src)
-            else:
-                nc.vector.tensor_copy(out=dst, in_=src)
+        def scalar_copy(dst, src):
+            nc.scalar.copy(out=dst, in_=src)
 
-        def load_codes(tile, words, passes):
-            width = words.shape[2]
-            dst = tile[:, passes.start * width : passes.stop * width].bitcast(I32)
-            src = words[passes].rearrange("g p n -> p g n").bitcast(I32)
-            nc.sync.dma_start(out=dst.rearrange("p (g w) -> p g w", w=width // 4), in_=src)
+        def vector_copy(dst, src):
+            nc.vector.tensor_copy(out=dst, in_=src)
+
+        def load_codes(tile, words, g):
+            nc.sync.dma_start(out=tile[:, block(g, words.shape[2])].bitcast(I32), in_=words[g].bitcast(I32))
 
         def load_scale_rows(tile, rows):
             for r in range(4):
@@ -102,8 +112,7 @@ def tile_cross_backward_error_s12_kernel(tc, e, x, u_words, u_scales, v_words, v
 
         def load_b(h, slots):
             rows = b_abs[block(h, PASS), :].rearrange("(p t) n -> p (t n)", t=PACK)
-            cols = slice(slots.start * N, slots.stop * N)
-            nc.sync.dma_start(out=b_slots[h][:, cols], in_=rows[:, cols])
+            nc.sync.dma_start(out=b_rows[h][:, span(slots, N)], in_=rows[:, span(slots, N)])
 
         def load_e(j):
             h, t = divmod(j, PACK)
@@ -112,165 +121,12 @@ def tile_cross_backward_error_s12_kernel(tc, e, x, u_words, u_scales, v_words, v
         def load_x(g):
             nc.sync.dma_start(out=x_rows[g][:], in_=x[block(g, PASS), :].rearrange("(p i) n -> p i n", i=PACK))
 
-        def zero(tile):
+        def zero_scale_tile(tile):
             nc.vector.memset(tile[:].rearrange("p g n -> p (g n)").bitcast(I32), 0)
 
-        def by_slot(dst, src, line):
-            nc.vector.tensor_copy(
-                out=dst.rearrange("p (a t c i) -> p a c t i", t=PACK, c=P // line, i=line),
-                in_=src.rearrange("p (a c i t) -> p a c t i", t=PACK, c=P // line, i=line),
-            )
-
-        def order_u_codes(passes):
-            cols = slice(passes.start * 2 * M, passes.stop * 2 * M)
-            by_slot(u_codes[:, cols].bitcast(U16), u_codes_in[:, cols].bitcast(U16), 8)
-
-        def order_u_scale(passes):
-            cols = slice(passes.start * M, passes.stop * M)
-            by_slot(u_scale[:, cols], u_scale_in[:].rearrange("p g n -> p (g n)")[:, cols], 16)
-
-        d_psum = {}
-
-        def d_matmul(j, passes, bank):
-            if passes.start == 0:
-                d_psum[j] = psum_bank("d%d" % j, bank)
-            for g in range(passes.start, passes.stop):
-                nc.tensor.matmul_mx(
-                    out=d_psum[j][:],
-                    lhsT=u_codes[:, block(SLOTS * g + j, 2 * P)].bitcast(FP4X4),
-                    lhsT_scale=u_scale[:, block(SLOTS * g + j)],
-                    rhs=v_codes[:, block(g, 2 * N)].bitcast(FP4X4),
-                    rhs_scale=v_scale[:, g, :],
-                    start=(g == 0),
-                    stop=(g == K_PASSES - 1),
-                )
-
-        def add_b(j):
-            h, t = divmod(j, PACK)
-            nc.vector.tensor_tensor(out=d_slots[h][:, t, :], in0=d_psum[j][:], in1=b_slots[h][:, block(t, N)], op=ALU.add)
-
-        def empty_d(j):
-            h, t = divmod(j, PACK)
-            nc.scalar.copy(out=d_slots[h][:, t, :], in_=d_psum[j][:])
-
-        def add_b_sbuf(j):
-            h, t = divmod(j, PACK)
-            nc.vector.tensor_tensor(out=d_slots[h][:, t, :], in0=d_slots[h][:, t, :], in1=b_slots[h][:, block(t, N)], op=ALU.add)
-
-        def rsqrt_d(h, slots):
-            nc.scalar.activation(out=d_rsqrt[h][:, slots, :], in_=d_slots[h][:, slots, :], func=FUNC.Abs_reciprocal_sqrt)
-
-        def square(engine, h, cols):
-            src = d_rsqrt[h][:, :, cols].rearrange("p t (c i) -> p c t i", i=2)
-            dst = w_packed[h][:, cols, :].rearrange("p (c i) t -> p c t i", i=2)
-            if engine == "scalar":
-                nc.scalar.activation(out=dst, in_=src, func=FUNC.Square)
-            else:
-                nc.vector.tensor_tensor(out=dst, in0=src, in1=src, op=ALU.mult)
-
-        def quantize_w(h):
-            quantize(w_codes[h][:], w_scale[h][:], w_packed[h][:].rearrange("p n t -> p (n t)"))
-
-        e_psum = {}
-
-        def split_e(engine, j):
-            copy_on(
-                engine,
-                e_split[j % STAGE_BUFS][:].rearrange("p (g u c i) -> p g c u i", g=K_PASSES, u=2, i=4),
-                e_rows[j][:].bitcast(F32).rearrange("p (g c i u) -> p g c u i", g=K_PASSES, u=2, i=4),
-            )
-
-        def transpose_e(j, banks, split):
-            if split:
-                words = e_split[j % STAGE_BUFS][:].rearrange("p (g u w) -> p g u w", g=K_PASSES, u=2)
-            else:
-                words = e_rows[j][:].bitcast(F32).rearrange("p (g w u) -> p g u w", g=K_PASSES, u=2)
-            for pair in range(K_PASSES // 2):
-                bank = psum_bank("e%d%d" % (j, pair), banks[pair])
-                e_psum[j, pair] = bank
-                for gg in range(2):
-                    for u in range(2):
-                        nc.tensor.transpose(bank[:, block(2 * gg + u)], words[:, 2 * pair + gg, u, :], ident[:])
-
-        def pack_e(engine, j, pair):
-            dst = e_packed[j % STAGE_BUFS][:, block(pair, K // 2)].bitcast(F32).rearrange("p (g r u) -> p g r u", g=2, u=2)
-            copy_on(engine, dst, e_psum[j, pair][:].rearrange("p (g u r) -> p g r u", g=2, u=2))
-
-        def quantize_e(j):
-            quantize(e_codes[j][:], e_scale[j][:], e_packed[j % STAGE_BUFS][:])
-
-        def pack_x(engine, g):
-            copy_on(
-                engine,
-                x_packed[g][:].rearrange("p (c a) i -> p c i a", a=4),
-                x_rows[g][:].rearrange("p i (c a) -> p c i a", a=4),
-            )
-
-        def quantize_x(g):
-            quantize(x_codes[g][:], x_scale[g][:], x_packed[g][:].rearrange("p n i -> p (n i)"))
-
-        r_psum = {}
-        r_count = {}
-
-        def r_matmul(j, g, c, bank):
-            h, t = divmod(j, PACK)
-            if (h, c) not in r_psum:
-                r_psum[h, c] = psum_bank("r%d%d" % (h, c), bank)
-            done = r_count.get((h, c), 0)
-            r_count[h, c] = done + 1
-            nc.tensor.matmul_mx(
-                out=r_psum[h, c][:, block(t)],
-                lhsT=e_codes[j][:, block(g)].bitcast(FP8X4),
-                lhsT_scale=e_scale[j][:, block(g)],
-                rhs=x_codes[g][:, block(c)].bitcast(FP8X4),
-                rhs_scale=x_scale[g][:, block(c)],
-                start=(done == 0),
-                stop=(done == PACK * K_PASSES - 1),
-            )
-
-        def r_slot(j, passes, chunks=range(CHUNKS)):
-            for g in passes:
-                for c in chunks:
-                    r_matmul(j, g, c, R_BANKS[j // PACK][c])
-
-        def abs_r(h, c):
-            src = r_psum[h, c][:].rearrange("p (t n) -> p n t", t=PACK)
-            nc.scalar.activation(out=r_packed[h][:, block(c), :], in_=src, func=FUNC.Abs)
-
-        def quantize_r(h, cols):
-            quantize(r_codes[h][:, cols], r_scale[h][:, cols], r_packed[h][:, cols, :].rearrange("p n t -> p (n t)"))
-
-        out_psum = {}
-
-        def out_matmul(h, c):
-            if h == 0:
-                out_psum[c] = psum_bank("out%d" % c, OUT_BANKS[c])
-            nc.tensor.matmul_mx(
-                out=out_psum[c][:],
-                lhsT=r_codes[h][:, block(c)].bitcast(FP8X4),
-                lhsT_scale=r_scale[h][:, block(c)],
-                rhs=w_codes[h][:].bitcast(FP8X4),
-                rhs_scale=w_scale[h][:],
-                start=(h == 0),
-                stop=(h == HALVES - 1),
-            )
-
-        def store(engine, c):
-            copy_on(engine, out_rows[c][:], out_psum[c][:])
-            nc.sync.dma_start(out=out[block(c), :], in_=out_rows[c][:])
-
-        table_out = sbuf("table_out", [P, 1], F32)
-
-        def load_table():
-            nc.scalar.activation(out=table_out[:], in_=ident[:, 0:1], func=FUNC.Abs_reciprocal_sqrt, bias=1.0)
-
-        warm = sbuf("warm", [P, K], BF16)
-        warm_codes = sbuf("warm_codes", [P, PASS], U32)
-        warm_scale = sbuf("warm_scale", [P, PASS], U8)
-
-        def warm_up(count):
-            bank = psum_bank("warm_psum", 7)
-            for i in range(count):
+        def warm_tensor_engine():
+            bank = psum_bank("warm_psum", WARM_BANK)
+            for i in range(WARM_PASSES):
                 nc.tensor.matmul_mx(
                     out=bank[:],
                     lhsT=warm_codes[:, block(0)].bitcast(FP8X4),
@@ -281,184 +137,243 @@ def tile_cross_backward_error_s12_kernel(tc, e, x, u_words, u_scales, v_words, v
                     stop=True,
                 )
 
+        def load_activation_table():
+            nc.scalar.activation(out=table_out[:], in_=ident[:, 0:1], func=FUNC.Abs_reciprocal_sqrt, bias=1.0)
+
+        def by_slot(dst, src, per_line):
+            vector_copy(
+                dst.rearrange("p (h t c i) -> p h c t i", t=PACK, c=P // per_line, i=per_line),
+                src.rearrange("p (h c i t) -> p h c t i", t=PACK, c=P // per_line, i=per_line),
+            )
+
+        def order_u(g):
+            by_slot(u_scale[:, block(g, M)], u_scale_in[:].rearrange("p g n -> p (g n)")[:, block(g, M)], LINE)
+            by_slot(u_codes[:, block(g, 2 * M)].bitcast(U16), u_codes_in[:, block(g, 2 * M)].bitcast(U16), LINE // 2)
+
+        d_psum = {}
+
+        def d_matmul(j, passes):
+            for g in passes:
+                if g == 0:
+                    d_psum[j] = psum_bank("d%d" % j, D_BANKS[j])
+                nc.tensor.matmul_mx(
+                    out=d_psum[j][:],
+                    lhsT=u_codes[:, block(SLOTS * g + j, 2 * P)].bitcast(FP4X4),
+                    lhsT_scale=u_scale[:, block(SLOTS * g + j)],
+                    rhs=v_codes[:, block(g, 2 * N)].bitcast(FP4X4),
+                    rhs_scale=v_scale[:, g, :],
+                    start=(g == 0),
+                    stop=(g == K_PASSES - 1),
+                )
+
+        def add_b(h, slots):
+            for t in slots:
+                nc.vector.tensor_tensor(
+                    out=d_slots[h][:, t, :], in0=d_psum[PACK * h + t][:], in1=b_rows[h][:, block(t, N)], op=ALU.add
+                )
+
+        def rsqrt_d(h, slots):
+            nc.scalar.activation(
+                out=d_rsqrt[h][:, span(slots, 1), :], in_=d_slots[h][:, span(slots, 1), :], func=FUNC.Abs_reciprocal_sqrt
+            )
+
+        def square_operands(h, chunks):
+            src = d_rsqrt[h][:, :, span(chunks, P)].rearrange("p t (c i) -> p c t i", i=2)
+            dst = w_packed[h][:, span(chunks, P), :].rearrange("p (c i) t -> p c t i", i=2)
+            return dst, src
+
+        def square_on_scalar(h, chunks):
+            dst, src = square_operands(h, chunks)
+            nc.scalar.activation(out=dst, in_=src, func=FUNC.Square)
+
+        def square_on_vector(h, chunks):
+            dst, src = square_operands(h, chunks)
+            nc.vector.tensor_tensor(out=dst, in0=src, in1=src, op=ALU.mult)
+
+        def quantize_w(h):
+            quantize(w_codes[h][:], w_scale[h][:], w_packed[h][:].rearrange("p n t -> p (n t)"))
+
+        e_psum = {}
+
+        def transpose_e(j):
+            words = e_rows[j][:].bitcast(F32).rearrange("p (g w u) -> p g u w", g=K_PASSES, u=2)
+            for pair in range(2):
+                bank = psum_bank("e%d%d" % (j, pair), E_BANKS[j][pair])
+                e_psum[j, pair] = bank
+                for gg in range(2):
+                    for u in range(2):
+                        nc.tensor.transpose(bank[:, block(2 * gg + u)], words[:, 2 * pair + gg, u, :], ident[:])
+
+        def pack_e(copy, j, pairs=range(2)):
+            for pair in pairs:
+                dst = e_packed[j % E_STAGES][:, block(pair, K // 2)].bitcast(F32)
+                src = e_psum[j, pair][:].rearrange("p (g u r) -> p g r u", g=2, u=2)
+                copy(dst.rearrange("p (g r u) -> p g r u", g=2, u=2), src)
+
+        def quantize_e(j):
+            quantize(e_codes[j][:], e_scale[j][:], e_packed[j % E_STAGES][:])
+
+        def pack_x(copy, g):
+            copy(
+                x_packed[g][:].rearrange("p (c a) i -> p c i a", a=4),
+                x_rows[g][:].rearrange("p i (c a) -> p c i a", a=4),
+            )
+
+        def quantize_x(g):
+            quantize(x_codes[g][:], x_scale[g][:], x_packed[g][:].rearrange("p n i -> p (n i)"))
+
+        r_psum = {}
+        r_done = {}
+
+        def r_matmul(h, slots, passes, chunks):
+            for t in slots:
+                for g in passes:
+                    for c in chunks:
+                        done = r_done.get((h, c), 0)
+                        r_done[h, c] = done + 1
+                        if done == 0:
+                            r_psum[h, c] = psum_bank("r%d%d" % (h, c), R_BANKS[h][c])
+                        nc.tensor.matmul_mx(
+                            out=r_psum[h, c][:, block(t)],
+                            lhsT=e_codes[PACK * h + t][:, block(g)].bitcast(FP8X4),
+                            lhsT_scale=e_scale[PACK * h + t][:, block(g)],
+                            rhs=x_codes[g][:, block(c)].bitcast(FP8X4),
+                            rhs_scale=x_scale[g][:, block(c)],
+                            start=(done == 0),
+                            stop=(done == PACK * K_PASSES - 1),
+                        )
+
+        def abs_r(h, c):
+            src = r_psum[h, c][:].rearrange("p (t n) -> p n t", t=PACK)
+            nc.scalar.activation(out=r_packed[h][:, block(c), :], in_=src, func=FUNC.Abs)
+
+        def quantize_r(h, chunks):
+            cols = span(chunks, P)
+            quantize(r_codes[h][:, cols], r_scale[h][:, cols], r_packed[h][:, cols, :].rearrange("p n t -> p (n t)"))
+
+        def out_matmul(c):
+            bank = psum_bank("out%d" % c, OUT_BANKS[c])
+            for h in range(HALVES):
+                nc.tensor.matmul_mx(
+                    out=bank[:],
+                    lhsT=r_codes[h][:, block(c)].bitcast(FP8X4),
+                    lhsT_scale=r_scale[h][:, block(c)],
+                    rhs=w_codes[h][:].bitcast(FP8X4),
+                    rhs_scale=w_scale[h][:],
+                    start=(h == 0),
+                    stop=(h == HALVES - 1),
+                )
+            return bank
+
         ctx.enter_context(tc.manual_schedule())
 
-        zero(u_scale_in)
-        zero(v_scale)
-        nc.vector.memset(warm[:].bitcast(I32), 0)
+        nc.gpsimd.memset(warm[:].bitcast(I32), 0)
+        zero_scale_tile(u_scale_in)
         quantize(warm_codes[:], warm_scale[:], warm[:])
+        zero_scale_tile(v_scale)
         make_identity(nc, ident[:])
+        load_activation_table()
+
         load_e(0)
         load_e(1)
         load_scale_rows(u_scale_in, u_scales)
-        load_codes(u_codes_in, u_words, slice(0, 1))
-        load_codes(v_codes, v_words, slice(0, 1))
-        load_scale_rows(v_scale, v_scales)
-        load_codes(u_codes_in, u_words, slice(1, 2))
-        load_codes(v_codes, v_words, slice(1, 2))
-        load_codes(u_codes_in, u_words, slice(2, 3))
-        load_codes(v_codes, v_words, slice(2, 3))
-        load_codes(u_codes_in, u_words, slice(3, 4))
-        load_codes(v_codes, v_words, slice(3, 4))
-        load_x(0)
-        load_b(0, slice(0, 2))
-        load_x(1)
-        load_b(0, slice(2, 4))
+        for g in ALL:
+            load_codes(u_codes_in, u_words, g)
+            load_codes(v_codes, v_words, g)
+            if g == 0:
+                load_scale_rows(v_scale, v_scales)
+        for g, slots in enumerate((LOW, HIGH)):
+            load_x(g)
+            load_b(0, slots)
         load_e(2)
         load_e(3)
-        load_b(1, slice(0, 2))
+        load_b(1, LOW)
         load_e(4)
         load_x(2)
         load_e(5)
-        load_b(1, slice(2, 4))
+        load_b(1, HIGH)
         load_x(3)
         load_e(6)
         load_e(7)
-        warm_up(4)
-        transpose_e(0, (0, 1), False)
-        transpose_e(1, (2, 3), False)
-        order_u_scale(slice(0, 1))
-        order_u_codes(slice(0, 1))
-        order_u_scale(slice(1, 2))
-        order_u_codes(slice(1, 2))
-        order_u_scale(slice(2, 3))
-        order_u_codes(slice(2, 3))
-        order_u_scale(slice(3, 4))
-        order_u_codes(slice(3, 4))
-        load_table()
-        pack_e("scalar", 0, 0)
-        pack_e("scalar", 0, 1)
-        pack_e("scalar", 1, 0)
-        pack_e("scalar", 1, 1)
-        pack_x("scalar", 0)
-        d_matmul(0, slice(0, 1), 4)
-        d_matmul(1, slice(0, 1), 5)
-        d_matmul(2, slice(0, 1), 6)
-        d_matmul(3, slice(0, 1), 7)
-        d_matmul(4, slice(0, 1), 0)
-        d_matmul(5, slice(0, 1), 1)
-        d_matmul(6, slice(0, 1), 2)
-        d_matmul(7, slice(0, 1), 3)
-        d_matmul(0, slice(1, 2), 4)
-        d_matmul(1, slice(1, 2), 5)
-        d_matmul(2, slice(1, 2), 6)
-        d_matmul(3, slice(1, 2), 7)
-        d_matmul(0, slice(2, 3), 4)
-        d_matmul(1, slice(2, 3), 5)
-        d_matmul(2, slice(2, 3), 6)
-        d_matmul(3, slice(2, 3), 7)
-        d_matmul(0, slice(3, 4), 4)
-        d_matmul(1, slice(3, 4), 5)
-        d_matmul(2, slice(3, 4), 6)
-        d_matmul(3, slice(3, 4), 7)
-        d_matmul(4, slice(1, 4), 0)
-        d_matmul(5, slice(1, 4), 1)
-        d_matmul(6, slice(1, 4), 2)
-        quantize_e(0)
-        quantize_e(1)
-        add_b(0)
-        add_b(1)
-        pack_x("vector", 1)
-        add_b(2)
-        add_b(3)
-        quantize_x(0)
-        quantize_x(1)
-        add_b(4)
-        add_b(5)
-        rsqrt_d(0, slice(0, 2))
-        rsqrt_d(0, slice(2, 4))
-        transpose_e(2, (4, 5), False)
-        d_matmul(7, slice(1, 4), 3)
-        transpose_e(3, (6, 7), False)
-        transpose_e(4, (0, 1), False)
-        pack_e("scalar", 2, 0)
-        pack_e("scalar", 2, 1)
-        pack_e("scalar", 3, 0)
-        pack_e("scalar", 3, 1)
-        pack_e("scalar", 4, 0)
-        pack_e("scalar", 4, 1)
-        square("scalar", 0, slice(0, 256))
-        rsqrt_d(1, slice(0, 2))
-        r_slot(0, range(0, 2), range(0, 2))
-        r_slot(1, range(0, 2), range(0, 2))
-        r_slot(0, range(0, 2), range(2, 4))
-        r_slot(1, range(0, 2), range(2, 4))
+
+        warm_tensor_engine()
+        for j in LOW:
+            transpose_e(j)
+            pack_e(scalar_copy, j)
+        warm_tensor_engine()
+
+        for g in ALL:
+            order_u(g)
+            for j in range(SLOTS if g == 0 else PACK):
+                d_matmul(j, [g])
+        later_passes = range(1, K_PASSES)
+        for j in range(PACK, SLOTS - 1):
+            d_matmul(j, later_passes)
+
+        pack_x(scalar_copy, 0)
+        for j in LOW:
+            quantize_e(j)
+        add_b(0, LOW)
+        pack_x(vector_copy, 1)
+        add_b(0, HIGH)
+        for g in LOW:
+            quantize_x(g)
+        add_b(1, LOW)
+        rsqrt_d(0, LOW)
+        rsqrt_d(0, HIGH)
+
+        transpose_e(2)
+        d_matmul(SLOTS - 1, later_passes)
+        transpose_e(3)
+        transpose_e(4)
+        for j in (2, 3, 4):
+            pack_e(scalar_copy, j)
+        r_matmul(0, LOW, LOW, LOW)
+        r_matmul(0, LOW, LOW, HIGH)
         quantize_e(2)
-        pack_x("vector", 2)
+        pack_x(vector_copy, 2)
         quantize_e(3)
         quantize_x(2)
-        add_b(6)
-        add_b(7)
-        pack_x("vector", 3)
+        add_b(1, HIGH)
+        pack_x(vector_copy, 3)
         quantize_e(4)
         quantize_x(3)
-        r_slot(2, range(0, 2), range(0, 4))
-        transpose_e(5, (0, 1), False)
-        r_slot(3, range(0, 2), range(0, 4))
-        r_slot(0, range(2, 3), range(0, 4))
-        r_slot(1, range(2, 3), range(0, 4))
-        r_slot(2, range(2, 3), range(0, 4))
-        r_slot(3, range(2, 3), range(0, 4))
-        transpose_e(6, (2, 3), False)
-        pack_e("scalar", 5, 0)
-        pack_e("scalar", 5, 1)
-        square("scalar", 0, slice(256, 512))
-        rsqrt_d(1, slice(2, 4))
-        pack_e("scalar", 6, 0)
-        transpose_e(7, (0, 1), False)
-        r_slot(0, range(3, 4), range(0, 2))
-        r_slot(1, range(3, 4), range(0, 2))
-        r_slot(2, range(3, 4), range(0, 2))
-        r_slot(3, range(3, 4), range(0, 2))
-        r_slot(0, range(3, 4), range(2, 4))
-        r_slot(1, range(3, 4), range(2, 4))
-        r_slot(2, range(3, 4), range(2, 4))
-        r_slot(3, range(3, 4), range(2, 4))
+        r_matmul(0, [2], LOW, ALL)
+        transpose_e(5)
+        square_on_scalar(0, LOW)
+        rsqrt_d(1, LOW)
+        pack_e(scalar_copy, 5)
+        square_on_scalar(0, HIGH)
+        rsqrt_d(1, HIGH)
+        r_matmul(0, [3], LOW, ALL)
+        r_matmul(0, ALL, [2], ALL)
         quantize_e(5)
-        pack_e("vector", 6, 1)
+
+        transpose_e(6)
+        pack_e(scalar_copy, 6, [0])
+        pack_e(vector_copy, 6, [1])
+        transpose_e(7)
         quantize_w(0)
-        pack_e("vector", 7, 1)
+        pack_e(scalar_copy, 7, [0])
+        pack_e(vector_copy, 7, [1])
         quantize_e(6)
-        pack_e("scalar", 7, 0)
-        square("scalar", 1, slice(256, 512))
-        abs_r(0, 0)
-        abs_r(0, 1)
-        abs_r(0, 2)
-        abs_r(0, 3)
-        r_slot(4, range(0, 4), range(0, 2))
-        r_slot(5, range(0, 4), range(0, 2))
-        r_slot(6, range(0, 4), range(0, 2))
         quantize_e(7)
-        square("vector", 1, slice(0, 256))
-        quantize_r(0, slice(0, 512))
+        square_on_vector(1, LOW)
+        square_on_scalar(1, HIGH)
+        r_matmul(0, ALL, [3], LOW)
+        r_matmul(0, ALL, [3], HIGH)
+        for c in ALL:
+            abs_r(0, c)
+        quantize_r(0, ALL)
         quantize_w(1)
-        r_slot(7, range(0, 4), range(0, 1))
-        r_slot(7, range(0, 4), range(1, 2))
-        r_slot(4, range(0, 4), range(2, 3))
-        r_slot(5, range(0, 4), range(2, 3))
-        r_slot(6, range(0, 4), range(2, 3))
-        r_slot(7, range(0, 4), range(2, 3))
-        r_slot(4, range(0, 4), range(3, 4))
-        r_slot(5, range(0, 4), range(3, 4))
-        r_slot(6, range(0, 4), range(3, 4))
-        r_slot(7, range(0, 4), range(3, 4))
-        out_matmul(0, 0)
-        abs_r(1, 0)
-        abs_r(1, 1)
-        abs_r(1, 2)
-        abs_r(1, 3)
-        quantize_r(1, slice(0, 128))
-        quantize_r(1, slice(128, 256))
-        quantize_r(1, slice(256, 384))
-        quantize_r(1, slice(384, 512))
-        out_matmul(1, 0)
-        out_matmul(0, 1)
-        out_matmul(1, 1)
-        out_matmul(0, 2)
-        out_matmul(1, 2)
-        out_matmul(0, 3)
-        out_matmul(1, 3)
-        store("scalar", 0)
-        store("vector", 1)
-        store("scalar", 2)
-        store("vector", 3)
+
+        r_matmul(1, range(PACK - 1), ALL, LOW)
+        for c in ALL:
+            r_matmul(1, [PACK - 1] if c in LOW else ALL, ALL, [c])
+            abs_r(1, c)
+            quantize_r(1, range(c, c + 1))
+
+        for c in ALL:
+            copy = vector_copy if c % 2 else scalar_copy
+            copy(out_rows[c][:], out_matmul(c)[:])
+            nc.sync.dma_start(out=out[block(c), :], in_=out_rows[c][:])

@@ -32,12 +32,15 @@ WARM_PASSES = 3
 
 PAIR_A, PAIR_B, PAIR_C, PAIR_D = (0, 1), (2, 3), (4, 5), (6, 7)
 D_BANKS = PAIR_C + PAIR_D + PAIR_A + PAIR_B
-E_BANKS = (PAIR_A, PAIR_B, PAIR_C, PAIR_D, PAIR_A, PAIR_A, PAIR_B, PAIR_A)
-R_BANKS = (PAIR_C + PAIR_D, PAIR_B + PAIR_A)
+E_BANKS = (PAIR_A, PAIR_B, PAIR_C, PAIR_D) + (PAIR_A, PAIR_B) * 2
+R_BANKS = (PAIR_C + PAIR_D, PAIR_A + PAIR_B)
 OUT_BANKS = PAIR_C + PAIR_D
 WARM_BANK = D_BANKS[PACK - 1]
 
 LOW, HIGH, ALL = range(0, 2), range(2, 4), range(0, 4)
+PRELOADED = 2
+ROUNDS = ((0, LOW), (0, HIGH), (1, LOW), (1, HIGH))
+LAST_SLOTS = range(PRELOADED + len(ROUNDS), SLOTS)
 
 
 def block(i, width=P):
@@ -61,7 +64,6 @@ def tile_cross_backward_error_s12_kernel(tc, e, x, u_words, u_scales, v_words, v
             return [sbuf("%s%d" % (name, i), shape, dtype) for i in range(count)]
 
         ident = sbuf("ident", [P, P], F32)
-        warm = sbuf("warm", [P, PASS * PACK], BF16)
         warm_codes = sbuf("warm_codes", [P, PASS], U32)
         warm_scale = sbuf("warm_scale", [P, PASS], U8)
         table_out = sbuf("table_out", [P, 1], F32)
@@ -123,6 +125,9 @@ def tile_cross_backward_error_s12_kernel(tc, e, x, u_words, u_scales, v_words, v
 
         def zero_scale_tile(tile):
             nc.vector.memset(tile[:].rearrange("p g n -> p (g n)").bitcast(I32), 0)
+
+        def make_warm_up_operand():
+            quantize(warm_codes[:], warm_scale[:], u_scale_in[:].rearrange("p g n -> p (g n)").bitcast(BF16))
 
         def warm_tensor_engine():
             bank = psum_bank("warm_psum", WARM_BANK)
@@ -267,9 +272,8 @@ def tile_cross_backward_error_s12_kernel(tc, e, x, u_words, u_scales, v_words, v
 
         ctx.enter_context(tc.manual_schedule())
 
-        nc.gpsimd.memset(warm[:].bitcast(I32), 0)
         zero_scale_tile(u_scale_in)
-        quantize(warm_codes[:], warm_scale[:], warm[:])
+        make_warm_up_operand()
         zero_scale_tile(v_scale)
         make_identity(nc, ident[:])
         load_activation_table()
@@ -282,22 +286,15 @@ def tile_cross_backward_error_s12_kernel(tc, e, x, u_words, u_scales, v_words, v
             load_codes(v_codes, v_words, g)
             if g == 0:
                 load_scale_rows(v_scale, v_scales)
-        for g, slots in enumerate((LOW, HIGH)):
-            load_x(g)
-            load_b(0, slots)
-        load_e(2)
-        load_e(3)
-        load_b(1, LOW)
-        load_e(4)
-        load_x(2)
-        load_e(5)
-        load_b(1, HIGH)
-        load_x(3)
-        load_e(6)
-        load_e(7)
+        for i, (h, slots) in enumerate(ROUNDS):
+            load_x(i)
+            load_b(h, slots)
+            load_e(PRELOADED + i)
+        for j in LAST_SLOTS:
+            load_e(j)
 
         warm_tensor_engine()
-        for j in LOW:
+        for j in range(PRELOADED):
             transpose_e(j)
             pack_e(scalar_copy, j)
         warm_tensor_engine()
@@ -306,66 +303,53 @@ def tile_cross_backward_error_s12_kernel(tc, e, x, u_words, u_scales, v_words, v
             order_u(g)
             for j in range(SLOTS if g == 0 else PACK):
                 d_matmul(j, [g])
-        later_passes = range(1, K_PASSES)
-        for j in range(PACK, SLOTS - 1):
-            d_matmul(j, later_passes)
-
-        pack_x(scalar_copy, 0)
-        for j in LOW:
+        for j in range(PRELOADED):
             quantize_e(j)
-        add_b(0, LOW)
-        pack_x(vector_copy, 1)
-        add_b(0, HIGH)
-        for g in LOW:
-            quantize_x(g)
-        add_b(1, LOW)
-        rsqrt_d(0, LOW)
-        rsqrt_d(0, HIGH)
 
-        transpose_e(2)
-        d_matmul(SLOTS - 1, later_passes)
-        transpose_e(3)
-        transpose_e(4)
-        for j in (2, 3, 4):
-            pack_e(scalar_copy, j)
-        r_matmul(0, LOW, LOW, LOW)
-        r_matmul(0, LOW, LOW, HIGH)
+        later_passes = range(1, K_PASSES)
+        for i, slots in enumerate((LOW, HIGH)):
+            for t in slots:
+                d_matmul(PACK + t, later_passes)
+            pack_x(vector_copy if i else scalar_copy, i)
+            add_b(0, slots)
+            quantize_x(i)
+            rsqrt_d(0, slots)
+            transpose_e(PRELOADED + i)
+            pack_e(scalar_copy, PRELOADED + i)
         quantize_e(2)
-        pack_x(vector_copy, 2)
-        quantize_e(3)
-        quantize_x(2)
-        add_b(1, HIGH)
-        pack_x(vector_copy, 3)
-        quantize_e(4)
-        quantize_x(3)
-        r_matmul(0, [2], LOW, ALL)
-        transpose_e(5)
-        square_on_scalar(0, LOW)
-        rsqrt_d(1, LOW)
-        pack_e(scalar_copy, 5)
-        square_on_scalar(0, HIGH)
-        rsqrt_d(1, HIGH)
-        r_matmul(0, [3], LOW, ALL)
-        r_matmul(0, ALL, [2], ALL)
+
+        for c in ALL:
+            r_matmul(0, range(3), LOW, [c])
+        for i, slots in enumerate((LOW, HIGH)):
+            g, j = 2 + i, PACK + i
+            add_b(1, slots)
+            square_on_scalar(0, slots)
+            rsqrt_d(1, slots)
+            transpose_e(j)
+            pack_e(scalar_copy, j)
+            pack_x(vector_copy, g)
+            quantize_e(j - 1)
+            quantize_x(g)
+            if g == 2:
+                r_matmul(0, [3], LOW, ALL)
+                r_matmul(0, ALL, [g], ALL)
+        quantize_w(0)
         quantize_e(5)
 
-        transpose_e(6)
-        pack_e(scalar_copy, 6, [0])
-        pack_e(vector_copy, 6, [1])
-        transpose_e(7)
-        quantize_w(0)
-        pack_e(scalar_copy, 7, [0])
-        pack_e(vector_copy, 7, [1])
-        quantize_e(6)
-        quantize_e(7)
+        for j, chunks in zip(LAST_SLOTS, (LOW, HIGH)):
+            transpose_e(j)
+            pack_e(scalar_copy, j, [0])
+            pack_e(vector_copy, j, [1])
+            r_matmul(0, ALL, [3], chunks)
+            if chunks == LOW:
+                square_on_scalar(1, HIGH)
+        for j in LAST_SLOTS:
+            quantize_e(j)
         square_on_vector(1, LOW)
-        square_on_scalar(1, HIGH)
-        r_matmul(0, ALL, [3], LOW)
-        r_matmul(0, ALL, [3], HIGH)
+        quantize_w(1)
         for c in ALL:
             abs_r(0, c)
         quantize_r(0, ALL)
-        quantize_w(1)
 
         r_matmul(1, range(PACK - 1), ALL, LOW)
         for c in ALL:

@@ -28,7 +28,7 @@ BANK = 512
 LINE = 16
 ALIGN = 64
 E_STAGES = 3
-WARM_PASSES = 3
+WARM_PASSES = 2
 
 PAIR_A, PAIR_B, PAIR_C, PAIR_D = (0, 1), (2, 3), (4, 5), (6, 7)
 D_BANKS = PAIR_C + PAIR_D + PAIR_A + PAIR_B
@@ -297,7 +297,7 @@ def tile_cross_backward_error_s12_kernel(tc, e, x, u_words, u_scales, v_words, v
         for j in range(PRELOADED):
             transpose_e(j)
             pack_e(scalar_copy, j)
-        warm_tensor_engine()
+            warm_tensor_engine()
 
         for g in ALL:
             order_u(g)
@@ -332,7 +332,8 @@ def tile_cross_backward_error_s12_kernel(tc, e, x, u_words, u_scales, v_words, v
             quantize_x(g)
             if g == 2:
                 r_matmul(0, [3], LOW, ALL)
-                r_matmul(0, ALL, [g], ALL)
+                r_matmul(0, range(3), [g], ALL)
+        r_matmul(0, [3], [2], ALL)
         quantize_w(0)
         quantize_e(5)
 

@@ -32,14 +32,15 @@ WARM_PASSES = 2
 
 PAIR_A, PAIR_B, PAIR_C, PAIR_D = (0, 1), (2, 3), (4, 5), (6, 7)
 D_BANKS = PAIR_C + PAIR_D + PAIR_A + PAIR_B
-E_BANKS = (PAIR_A, PAIR_B, PAIR_C, PAIR_D) + (PAIR_A, PAIR_B) * 2
-R_BANKS = (PAIR_C + PAIR_D, PAIR_A + PAIR_B)
+E_BANKS = (PAIR_A, PAIR_B, PAIR_C, PAIR_D, PAIR_A, PAIR_A, PAIR_B, PAIR_A)
+R_BANKS = (PAIR_C + PAIR_D, PAIR_B + PAIR_A)
 OUT_BANKS = PAIR_C + PAIR_D
 WARM_BANK = D_BANKS[PACK - 1]
 
 LOW, HIGH, ALL = range(0, 2), range(2, 4), range(0, 4)
 PRELOADED = 2
 ROUNDS = ((0, LOW), (0, HIGH), (1, LOW), (1, HIGH))
+BANKS_FIRST = 2
 LAST_SLOTS = range(PRELOADED + len(ROUNDS), SLOTS)
 
 
@@ -287,8 +288,11 @@ def tile_cross_backward_error_s12_kernel(tc, e, x, u_words, u_scales, v_words, v
             if g == 0:
                 load_scale_rows(v_scale, v_scales)
         for i, (h, slots) in enumerate(ROUNDS):
+            if i == BANKS_FIRST:
+                load_b(h, slots)
             load_x(i)
-            load_b(h, slots)
+            if i != BANKS_FIRST:
+                load_b(h, slots)
             load_e(PRELOADED + i)
         for j in LAST_SLOTS:
             load_e(j)
@@ -320,41 +324,47 @@ def tile_cross_backward_error_s12_kernel(tc, e, x, u_words, u_scales, v_words, v
 
         for c in ALL:
             r_matmul(0, range(3), LOW, [c])
-        for i, slots in enumerate((LOW, HIGH)):
-            g, j = 2 + i, PACK + i
-            add_b(1, slots)
-            square_on_scalar(0, slots)
-            rsqrt_d(1, slots)
-            transpose_e(j)
-            pack_e(scalar_copy, j)
-            pack_x(vector_copy, g)
-            quantize_e(j - 1)
-            quantize_x(g)
-            if g == 2:
-                r_matmul(0, [3], LOW, ALL)
-                r_matmul(0, range(3), [g], ALL)
-        r_matmul(0, [3], [2], ALL)
-        quantize_w(0)
-        quantize_e(5)
+        add_b(1, LOW)
+        square_on_scalar(0, LOW)
+        rsqrt_d(1, LOW)
+        transpose_e(4)
+        pack_e(scalar_copy, 4)
+        pack_x(vector_copy, 2)
+        quantize_e(3)
+        quantize_x(2)
+        r_matmul(0, [3], LOW, ALL)
+        r_matmul(0, ALL, [2], ALL)
 
-        for j, chunks in zip(LAST_SLOTS, (LOW, HIGH)):
+        pack_x(vector_copy, 3)
+        quantize_x(3)
+        add_b(1, HIGH)
+        quantize_e(4)
+        square_on_scalar(0, HIGH)
+        transpose_e(5)
+        pack_e(scalar_copy, 5)
+        rsqrt_d(1, HIGH)
+        r_matmul(0, ALL, [3], ALL)
+        quantize_e(5)
+        quantize_w(0)
+
+        for j in LAST_SLOTS:
             transpose_e(j)
             pack_e(scalar_copy, j, [0])
             pack_e(vector_copy, j, [1])
-            r_matmul(0, ALL, [3], chunks)
-            if chunks == LOW:
-                square_on_scalar(1, HIGH)
+            abs_r(0, j - LAST_SLOTS.start)
         for j in LAST_SLOTS:
             quantize_e(j)
-        square_on_vector(1, LOW)
-        quantize_w(1)
-        for c in ALL:
+        for c in HIGH:
             abs_r(0, c)
+        square_on_vector(1, LOW)
+        square_on_scalar(1, HIGH)
         quantize_r(0, ALL)
+        quantize_w(1)
 
-        r_matmul(1, range(PACK - 1), ALL, LOW)
+        r_matmul(1, LOW, ALL, LOW)
+        r_matmul(1, LOW, ALL, HIGH)
         for c in ALL:
-            r_matmul(1, [PACK - 1] if c in LOW else ALL, ALL, [c])
+            r_matmul(1, HIGH, ALL, [c])
             abs_r(1, c)
             quantize_r(1, range(c, c + 1))
 

@@ -32,16 +32,13 @@ WARM_PASSES = 2
 
 PAIR_A, PAIR_B, PAIR_C, PAIR_D = (0, 1), (2, 3), (4, 5), (6, 7)
 D_BANKS = PAIR_C + PAIR_D + PAIR_A + PAIR_B
-E_BANKS = (PAIR_A, PAIR_B, PAIR_C, PAIR_D, PAIR_A, PAIR_A, PAIR_B, PAIR_A)
-R_BANKS = (PAIR_C + PAIR_D, PAIR_B + PAIR_A)
-OUT_BANKS = PAIR_C + PAIR_D
+E_BANKS = (PAIR_A, PAIR_B, PAIR_C, PAIR_C, PAIR_C, PAIR_C, PAIR_B, PAIR_C)
+R_BANKS = PAIR_D + PAIR_A
+OUT_BANKS = PAIR_B + PAIR_C
 WARM_BANK = D_BANKS[PACK - 1]
 
 LOW, HIGH, ALL = range(0, 2), range(2, 4), range(0, 4)
-PRELOADED = 2
-ROUNDS = ((0, LOW), (0, HIGH), (1, LOW), (1, HIGH))
-BANKS_FIRST = 2
-LAST_SLOTS = range(PRELOADED + len(ROUNDS), SLOTS)
+SCALE_BATCHES = (LOW, HIGH)
 
 
 def block(i, width=P):
@@ -77,11 +74,11 @@ def tile_cross_backward_error_s12_kernel(tc, e, x, u_words, u_scales, v_words, v
         x_codes = sbufs("x_codes", K_PASSES, [P, N], U32)
         x_scale = sbufs("x_scale", K_PASSES, [P, N], U8)
         u_codes_in = sbuf("u_codes_in", [P, K_PASSES * 2 * M], U8)
-        u_scale_in = sbuf("u_scale_in", [P, K_PASSES, M], U8)
+        u_scale_in = sbufs("u_scale_in", len(SCALE_BATCHES), [P, len(LOW) * M], U8)
+        v_scale = sbufs("v_scale", len(SCALE_BATCHES), [P, len(LOW) * N], U8)
         u_codes = sbuf("u_codes", [P, K_PASSES * 2 * M], U8)
         u_scale = sbuf("u_scale", [P, K_PASSES * M], U8)
         v_codes = sbuf("v_codes", [P, K_PASSES * 2 * N], U8)
-        v_scale = sbuf("v_scale", [P, K_PASSES, N], U8)
         b_rows = sbufs("b_rows", HALVES, [P, PACK * N], BF16)
         d_slots = sbufs("d_slots", HALVES, [P, PACK, N], F32)
         d_rsqrt = sbufs("d_rsqrt", HALVES, [P, PACK, N], F32)
@@ -108,10 +105,19 @@ def tile_cross_backward_error_s12_kernel(tc, e, x, u_words, u_scales, v_words, v
         def load_codes(tile, words, g):
             nc.sync.dma_start(out=tile[:, block(g, words.shape[2])].bitcast(I32), in_=words[g].bitcast(I32))
 
-        def load_scale_rows(tile, rows):
+        def load_uv(g):
+            load_codes(u_codes_in, u_words, g)
+            load_codes(v_codes, v_words, g)
+
+        def scale_plane(tiles, g, width):
+            batch, i = divmod(g, len(LOW))
+            return tiles[batch][:, block(i, width)]
+
+        def load_scale_rows(tiles, rows, batch):
             for r in range(4):
-                src = rows[:, r:16:4, :].rearrange("g b n -> b g n")
-                nc.sync.dma_start(out=tile[r:P:32].bitcast(I32), in_=src.bitcast(I32))
+                src = rows[span(SCALE_BATCHES[batch], 1), r:16:4, :].rearrange("g b n -> b g n")
+                dst = tiles[batch][r:P:32, :].rearrange("b (g n) -> b g n", g=len(LOW))
+                nc.sync.dma_start(out=dst.bitcast(I32), in_=src.bitcast(I32))
 
         def load_b(h, slots):
             rows = b_abs[block(h, PASS), :].rearrange("(p t) n -> p (t n)", t=PACK)
@@ -125,10 +131,12 @@ def tile_cross_backward_error_s12_kernel(tc, e, x, u_words, u_scales, v_words, v
             nc.sync.dma_start(out=x_rows[g][:], in_=x[block(g, PASS), :].rearrange("(p i) n -> p i n", i=PACK))
 
         def zero_scale_tile(tile):
-            nc.vector.memset(tile[:].rearrange("p g n -> p (g n)").bitcast(I32), 0)
+            nc.vector.memset(tile[:].bitcast(I32), 0)
 
         def make_warm_up_operand():
-            quantize(warm_codes[:], warm_scale[:], u_scale_in[:].rearrange("p g n -> p (g n)").bitcast(BF16))
+            for batch, tile in enumerate(u_scale_in):
+                cols = block(batch, PASS // 2)
+                quantize(warm_codes[:, cols], warm_scale[:, cols], tile[:].bitcast(BF16))
 
         def warm_tensor_engine():
             bank = psum_bank("warm_psum", WARM_BANK)
@@ -146,15 +154,18 @@ def tile_cross_backward_error_s12_kernel(tc, e, x, u_words, u_scales, v_words, v
         def load_activation_table():
             nc.scalar.activation(out=table_out[:], in_=ident[:, 0:1], func=FUNC.Abs_reciprocal_sqrt, bias=1.0)
 
-        def by_slot(dst, src, per_line):
-            vector_copy(
+        def by_slot(copy, dst, src, per_line):
+            copy(
                 dst.rearrange("p (h t c i) -> p h c t i", t=PACK, c=P // per_line, i=per_line),
                 src.rearrange("p (h c i t) -> p h c t i", t=PACK, c=P // per_line, i=per_line),
             )
 
-        def order_u(g):
-            by_slot(u_scale[:, block(g, M)], u_scale_in[:].rearrange("p g n -> p (g n)")[:, block(g, M)], LINE)
-            by_slot(u_codes[:, block(g, 2 * M)].bitcast(U16), u_codes_in[:, block(g, 2 * M)].bitcast(U16), LINE // 2)
+        def order_u_scale(g):
+            by_slot(vector_copy, u_scale[:, block(g, M)], scale_plane(u_scale_in, g, M), LINE)
+
+        def order_u_codes(copy, g, halves=range(HALVES)):
+            cols = span(range(HALVES * g + halves.start, HALVES * g + halves.stop), 2 * PASS)
+            by_slot(copy, u_codes[:, cols].bitcast(U16), u_codes_in[:, cols].bitcast(U16), LINE // 2)
 
         d_psum = {}
 
@@ -167,7 +178,7 @@ def tile_cross_backward_error_s12_kernel(tc, e, x, u_words, u_scales, v_words, v
                     lhsT=u_codes[:, block(SLOTS * g + j, 2 * P)].bitcast(FP4X4),
                     lhsT_scale=u_scale[:, block(SLOTS * g + j)],
                     rhs=v_codes[:, block(g, 2 * N)].bitcast(FP4X4),
-                    rhs_scale=v_scale[:, g, :],
+                    rhs_scale=scale_plane(v_scale, g, N),
                     start=(g == 0),
                     stop=(g == K_PASSES - 1),
                 )
@@ -219,10 +230,10 @@ def tile_cross_backward_error_s12_kernel(tc, e, x, u_words, u_scales, v_words, v
         def quantize_e(j):
             quantize(e_codes[j][:], e_scale[j][:], e_packed[j % E_STAGES][:])
 
-        def pack_x(copy, g):
+        def pack_x(copy, g, cols=slice(0, N)):
             copy(
-                x_packed[g][:].rearrange("p (c a) i -> p c i a", a=4),
-                x_rows[g][:].rearrange("p i (c a) -> p c i a", a=4),
+                x_packed[g][:, cols, :].rearrange("p (c a) i -> p c i a", a=4),
+                x_rows[g][:, :, cols].rearrange("p i (c a) -> p c i a", a=4),
             )
 
         def quantize_x(g):
@@ -238,7 +249,7 @@ def tile_cross_backward_error_s12_kernel(tc, e, x, u_words, u_scales, v_words, v
                         done = r_done.get((h, c), 0)
                         r_done[h, c] = done + 1
                         if done == 0:
-                            r_psum[h, c] = psum_bank("r%d%d" % (h, c), R_BANKS[h][c])
+                            r_psum[h, c] = psum_bank("r%d%d" % (h, c), R_BANKS[c])
                         nc.tensor.matmul_mx(
                             out=r_psum[h, c][:, block(t)],
                             lhsT=e_codes[PACK * h + t][:, block(g)].bitcast(FP8X4),
@@ -273,98 +284,130 @@ def tile_cross_backward_error_s12_kernel(tc, e, x, u_words, u_scales, v_words, v
 
         ctx.enter_context(tc.manual_schedule())
 
-        zero_scale_tile(u_scale_in)
+        for tile in u_scale_in:
+            zero_scale_tile(tile)
         make_warm_up_operand()
-        zero_scale_tile(v_scale)
+        for tile in v_scale:
+            zero_scale_tile(tile)
         make_identity(nc, ident[:])
         load_activation_table()
 
         load_e(0)
         load_e(1)
-        load_scale_rows(u_scale_in, u_scales)
-        for g in ALL:
-            load_codes(u_codes_in, u_words, g)
-            load_codes(v_codes, v_words, g)
-            if g == 0:
-                load_scale_rows(v_scale, v_scales)
-        for i, (h, slots) in enumerate(ROUNDS):
-            if i == BANKS_FIRST:
-                load_b(h, slots)
-            load_x(i)
-            if i != BANKS_FIRST:
-                load_b(h, slots)
-            load_e(PRELOADED + i)
-        for j in LAST_SLOTS:
+        for batch, passes in enumerate(SCALE_BATCHES):
+            load_scale_rows(u_scale_in, u_scales, batch)
+            load_uv(passes[0])
+            load_scale_rows(v_scale, v_scales, batch)
+            if batch == 1:
+                load_x(0)
+            load_uv(passes[1])
+        load_b(0, LOW)
+        load_x(1)
+        load_b(0, HIGH)
+        load_e(2)
+        load_b(1, LOW)
+        load_e(3)
+        load_x(2)
+        load_e(4)
+        load_x(3)
+        load_b(1, HIGH)
+        for j in range(5, SLOTS):
             load_e(j)
 
-        warm_tensor_engine()
-        for j in range(PRELOADED):
+        for j in LOW:
+            warm_tensor_engine()
             transpose_e(j)
             pack_e(scalar_copy, j)
-            warm_tensor_engine()
 
-        for g in ALL:
-            order_u(g)
-            for j in range(SLOTS if g == 0 else PACK):
+        order_u_scale(0)
+        order_u_codes(vector_copy, 0, range(0, 1))
+        order_u_codes(vector_copy, 0, range(1, 2))
+        order_u_scale(1)
+        order_u_codes(scalar_copy, 1)
+        quantize_e(0)
+        order_u_scale(2)
+        order_u_codes(scalar_copy, 2)
+        order_u_scale(3)
+        quantize_e(1)
+        pack_x(vector_copy, 0)
+        order_u_codes(scalar_copy, 3, range(0, 1))
+        order_u_codes(scalar_copy, 3, range(1, 2))
+        quantize_x(0)
+
+        for g in LOW:
+            for j in range(SLOTS):
                 d_matmul(j, [g])
-        for j in range(PRELOADED):
-            quantize_e(j)
+        for j in range(PACK + 1):
+            d_matmul(j, [2])
+        for j in ALL:
+            d_matmul(j, [3])
+        d_matmul(PACK, [3])
+        for j in range(PACK + 1, SLOTS):
+            d_matmul(j, HIGH)
 
-        later_passes = range(1, K_PASSES)
-        for i, slots in enumerate((LOW, HIGH)):
-            for t in slots:
-                d_matmul(PACK + t, later_passes)
-            pack_x(vector_copy if i else scalar_copy, i)
-            add_b(0, slots)
-            quantize_x(i)
-            rsqrt_d(0, slots)
-            transpose_e(PRELOADED + i)
-            pack_e(scalar_copy, PRELOADED + i)
-        quantize_e(2)
+        add_b(0, LOW)
+        pack_x(scalar_copy, 1, block(0, N // 2))
+        pack_x(vector_copy, 1, block(1, N // 2))
+        add_b(0, HIGH)
+        quantize_x(1)
+        rsqrt_d(0, LOW)
 
-        for c in ALL:
-            r_matmul(0, range(3), LOW, [c])
+        transpose_e(2)
+        pack_e(scalar_copy, 2)
+        r_matmul(0, LOW, LOW, LOW)
         add_b(1, LOW)
-        square_on_scalar(0, LOW)
-        rsqrt_d(1, LOW)
-        transpose_e(4)
-        pack_e(scalar_copy, 4)
+        quantize_e(2)
+        rsqrt_d(0, HIGH)
+
+        transpose_e(3)
+        pack_e(scalar_copy, 3)
+        r_matmul(0, LOW, LOW, HIGH)
+        r_matmul(0, [2], LOW, ALL)
         pack_x(vector_copy, 2)
         quantize_e(3)
         quantize_x(2)
+        square_on_scalar(0, LOW)
+
+        transpose_e(4)
+        pack_e(scalar_copy, 4)
         r_matmul(0, [3], LOW, ALL)
         r_matmul(0, ALL, [2], ALL)
-
         pack_x(vector_copy, 3)
+        quantize_e(4)
         quantize_x(3)
         add_b(1, HIGH)
-        quantize_e(4)
         square_on_scalar(0, HIGH)
+        rsqrt_d(1, LOW)
+
         transpose_e(5)
         pack_e(scalar_copy, 5)
-        rsqrt_d(1, HIGH)
-        r_matmul(0, ALL, [3], ALL)
-        quantize_e(5)
+        for c in ALL:
+            r_matmul(0, ALL, [3], [c])
         quantize_w(0)
+        quantize_e(5)
 
-        for j in LAST_SLOTS:
-            transpose_e(j)
-            pack_e(scalar_copy, j, [0])
-            pack_e(vector_copy, j, [1])
-            abs_r(0, j - LAST_SLOTS.start)
-        for j in LAST_SLOTS:
-            quantize_e(j)
-        for c in HIGH:
+        transpose_e(6)
+        for c in ALL:
             abs_r(0, c)
-        square_on_vector(1, LOW)
-        square_on_scalar(1, HIGH)
+        pack_e(vector_copy, 6)
+        for c in LOW:
+            r_matmul(1, LOW, ALL, [c])
+
+        transpose_e(7)
+        rsqrt_d(1, HIGH)
+        quantize_e(6)
         quantize_r(0, ALL)
+        pack_e(scalar_copy, 7, [0])
+        pack_e(vector_copy, 7, [1])
+        square_on_scalar(1, LOW)
+        r_matmul(1, LOW, ALL, HIGH)
+        quantize_e(7)
+        square_on_vector(1, HIGH)
         quantize_w(1)
 
-        r_matmul(1, LOW, ALL, LOW)
-        r_matmul(1, LOW, ALL, HIGH)
+        r_matmul(1, [2], ALL, LOW)
         for c in ALL:
-            r_matmul(1, HIGH, ALL, [c])
+            r_matmul(1, [3] if c in LOW else HIGH, ALL, [c])
             abs_r(1, c)
             quantize_r(1, range(c, c + 1))
 

@@ -38,7 +38,7 @@ OUT_BANKS = PAIR_B + PAIR_C
 WARM_BANK = D_BANKS[PACK - 1]
 
 LOW, HIGH, ALL = range(0, 2), range(2, 4), range(0, 4)
-SCALE_BATCHES = (LOW, HIGH)
+SCALE_BATCHES = (ALL,)
 
 
 def block(i, width=P):
@@ -74,8 +74,8 @@ def tile_cross_backward_error_s12_kernel(tc, e, x, u_words, u_scales, v_words, v
         x_codes = sbufs("x_codes", K_PASSES, [P, N], U32)
         x_scale = sbufs("x_scale", K_PASSES, [P, N], U8)
         u_codes_in = sbuf("u_codes_in", [P, K_PASSES * 2 * M], U8)
-        u_scale_in = sbufs("u_scale_in", len(SCALE_BATCHES), [P, len(LOW) * M], U8)
-        v_scale = sbufs("v_scale", len(SCALE_BATCHES), [P, len(LOW) * N], U8)
+        u_scale_in = sbufs("u_scale_in", len(SCALE_BATCHES), [P, len(ALL) * M], U8)
+        v_scale = sbufs("v_scale", len(SCALE_BATCHES), [P, len(ALL) * N], U8)
         u_codes = sbuf("u_codes", [P, K_PASSES * 2 * M], U8)
         u_scale = sbuf("u_scale", [P, K_PASSES * M], U8)
         v_codes = sbuf("v_codes", [P, K_PASSES * 2 * N], U8)
@@ -110,13 +110,13 @@ def tile_cross_backward_error_s12_kernel(tc, e, x, u_words, u_scales, v_words, v
             load_codes(v_codes, v_words, g)
 
         def scale_plane(tiles, g, width):
-            batch, i = divmod(g, len(LOW))
+            batch, i = divmod(g, len(ALL))
             return tiles[batch][:, block(i, width)]
 
         def load_scale_rows(tiles, rows, batch):
             for r in range(4):
                 src = rows[span(SCALE_BATCHES[batch], 1), r:16:4, :].rearrange("g b n -> b g n")
-                dst = tiles[batch][r:P:32, :].rearrange("b (g n) -> b g n", g=len(LOW))
+                dst = tiles[batch][r:P:32, :].rearrange("b (g n) -> b g n", g=len(ALL))
                 nc.sync.dma_start(out=dst.bitcast(I32), in_=src.bitcast(I32))
 
         def load_b(h, slots):
@@ -134,9 +134,7 @@ def tile_cross_backward_error_s12_kernel(tc, e, x, u_words, u_scales, v_words, v
             nc.vector.memset(tile[:].bitcast(I32), 0)
 
         def make_warm_up_operand():
-            for batch, tile in enumerate(u_scale_in):
-                cols = block(batch, PASS // 2)
-                quantize(warm_codes[:, cols], warm_scale[:, cols], tile[:].bitcast(BF16))
+            quantize(warm_codes[:], warm_scale[:], u_scale_in[0][:].bitcast(BF16))
 
         def warm_tensor_engine():
             bank = psum_bank("warm_psum", WARM_BANK)
@@ -284,8 +282,7 @@ def tile_cross_backward_error_s12_kernel(tc, e, x, u_words, u_scales, v_words, v
 
         ctx.enter_context(tc.manual_schedule())
 
-        for tile in u_scale_in:
-            zero_scale_tile(tile)
+        zero_scale_tile(u_scale_in[0])
         make_warm_up_operand()
         for tile in v_scale:
             zero_scale_tile(tile)
@@ -294,13 +291,13 @@ def tile_cross_backward_error_s12_kernel(tc, e, x, u_words, u_scales, v_words, v
 
         load_e(0)
         load_e(1)
-        for batch, passes in enumerate(SCALE_BATCHES):
-            load_scale_rows(u_scale_in, u_scales, batch)
-            load_uv(passes[0])
-            load_scale_rows(v_scale, v_scales, batch)
-            if batch == 1:
-                load_x(0)
-            load_uv(passes[1])
+        load_scale_rows(u_scale_in, u_scales, 0)
+        load_uv(0)
+        load_scale_rows(v_scale, v_scales, 0)
+        load_uv(1)
+        load_uv(2)
+        load_x(0)
+        load_uv(3)
         load_b(0, LOW)
         load_x(1)
         load_b(0, HIGH)

@@ -28,17 +28,17 @@ BANK = 512
 LINE = 16
 ALIGN = 64
 E_STAGES = 3
-WARM_PASSES = 2
+WARM_RUNS = (2, 3)
 
 PAIR_A, PAIR_B, PAIR_C, PAIR_D = (0, 1), (2, 3), (4, 5), (6, 7)
 D_BANKS = PAIR_C + PAIR_D + PAIR_A + PAIR_B
-E_BANKS = (PAIR_A, PAIR_B, PAIR_C, PAIR_C, PAIR_C, PAIR_C, PAIR_B, PAIR_C)
-R_BANKS = PAIR_D + PAIR_A
-OUT_BANKS = PAIR_B + PAIR_C
+E_BANKS = (PAIR_A, PAIR_B, PAIR_C, PAIR_D, PAIR_A, PAIR_A, PAIR_B, PAIR_A)
+R_BANKS = (PAIR_C + PAIR_D, PAIR_B + PAIR_A)
+OUT_BANKS = PAIR_C + PAIR_D
+LAST_SLOTS = range(6, 8)
 WARM_BANK = D_BANKS[PACK - 1]
 
 LOW, HIGH, ALL = range(0, 2), range(2, 4), range(0, 4)
-SCALE_BATCHES = (ALL,)
 
 
 def block(i, width=P):
@@ -73,12 +73,12 @@ def tile_cross_backward_error_s12_kernel(tc, e, x, u_words, u_scales, v_words, v
         x_packed = sbufs("x_packed", K_PASSES, [P, N, PACK], BF16)
         x_codes = sbufs("x_codes", K_PASSES, [P, N], U32)
         x_scale = sbufs("x_scale", K_PASSES, [P, N], U8)
-        u_codes_in = sbuf("u_codes_in", [P, K_PASSES * 2 * M], U8)
-        u_scale_in = sbufs("u_scale_in", len(SCALE_BATCHES), [P, len(ALL) * M], U8)
-        v_scale = sbufs("v_scale", len(SCALE_BATCHES), [P, len(ALL) * N], U8)
-        u_codes = sbuf("u_codes", [P, K_PASSES * 2 * M], U8)
-        u_scale = sbuf("u_scale", [P, K_PASSES * M], U8)
+        u_codes_in = sbufs("u_codes_in", HALVES, [P, K_PASSES * 2 * PASS], U8)
+        u_scale_in = sbufs("u_scale_in", HALVES, [P, K_PASSES * PASS], U8)
+        u_codes = sbufs("u_codes", HALVES, [P, K_PASSES * 2 * PASS], U8)
+        u_scale = sbufs("u_scale", HALVES, [P, K_PASSES * PASS], U8)
         v_codes = sbuf("v_codes", [P, K_PASSES * 2 * N], U8)
+        v_scale = sbuf("v_scale", [P, K_PASSES * N], U8)
         b_rows = sbufs("b_rows", HALVES, [P, PACK * N], BF16)
         d_slots = sbufs("d_slots", HALVES, [P, PACK, N], F32)
         d_rsqrt = sbufs("d_rsqrt", HALVES, [P, PACK, N], F32)
@@ -102,21 +102,22 @@ def tile_cross_backward_error_s12_kernel(tc, e, x, u_words, u_scales, v_words, v
         def vector_copy(dst, src):
             nc.vector.tensor_copy(out=dst, in_=src)
 
-        def load_codes(tile, words, g):
-            nc.sync.dma_start(out=tile[:, block(g, words.shape[2])].bitcast(I32), in_=words[g].bitcast(I32))
+        def load_codes(tile, words, passes):
+            width = words.shape[2]
+            dst = tile[:, span(passes, width)].rearrange("p (g n) -> p g n", n=width)
+            src = words[span(passes, 1)].rearrange("g p n -> p g n")
+            nc.sync.dma_start(out=dst.bitcast(I32), in_=src.bitcast(I32))
 
-        def load_uv(g):
-            load_codes(u_codes_in, u_words, g)
-            load_codes(v_codes, v_words, g)
+        def load_u(h, passes):
+            load_codes(u_codes_in[h], u_words[:, :, block(h, 2 * PASS)], passes)
 
-        def scale_plane(tiles, g, width):
-            batch, i = divmod(g, len(ALL))
-            return tiles[batch][:, block(i, width)]
+        def load_v(passes):
+            load_codes(v_codes, v_words, passes)
 
-        def load_scale_rows(tiles, rows, batch):
+        def load_scale_rows(tile, rows):
             for r in range(4):
-                src = rows[span(SCALE_BATCHES[batch], 1), r:16:4, :].rearrange("g b n -> b g n")
-                dst = tiles[batch][r:P:32, :].rearrange("b (g n) -> b g n", g=len(ALL))
+                src = rows[:, r:16:4, :].rearrange("g b n -> b g n")
+                dst = tile[r:P:32].rearrange("b (g n) -> b g n", g=K_PASSES)
                 nc.sync.dma_start(out=dst.bitcast(I32), in_=src.bitcast(I32))
 
         def load_b(h, slots):
@@ -134,11 +135,13 @@ def tile_cross_backward_error_s12_kernel(tc, e, x, u_words, u_scales, v_words, v
             nc.vector.memset(tile[:].bitcast(I32), 0)
 
         def make_warm_up_operand():
-            quantize(warm_codes[:], warm_scale[:], u_scale_in[0][:].bitcast(BF16))
+            for i, tile in enumerate((v_scale, u_scale_in[1])):
+                cols = block(i, PASS // 2)
+                quantize(warm_codes[:, cols], warm_scale[:, cols], tile[:].bitcast(BF16))
 
-        def warm_tensor_engine():
+        def warm_tensor_engine(passes):
             bank = psum_bank("warm_psum", WARM_BANK)
-            for i in range(WARM_PASSES):
+            for i in range(passes):
                 nc.tensor.matmul_mx(
                     out=bank[:],
                     lhsT=warm_codes[:, block(0)].bitcast(FP8X4),
@@ -158,25 +161,27 @@ def tile_cross_backward_error_s12_kernel(tc, e, x, u_words, u_scales, v_words, v
                 src.rearrange("p (h c i t) -> p h c t i", t=PACK, c=P // per_line, i=per_line),
             )
 
-        def order_u_scale(g):
-            by_slot(vector_copy, u_scale[:, block(g, M)], scale_plane(u_scale_in, g, M), LINE)
+        def order_u_scale(h, passes):
+            cols = span(passes, PASS)
+            by_slot(vector_copy, u_scale[h][:, cols], u_scale_in[h][:, cols], LINE)
 
-        def order_u_codes(copy, g, halves=range(HALVES)):
-            cols = span(range(HALVES * g + halves.start, HALVES * g + halves.stop), 2 * PASS)
-            by_slot(copy, u_codes[:, cols].bitcast(U16), u_codes_in[:, cols].bitcast(U16), LINE // 2)
+        def order_u_codes(copy, h, passes):
+            cols = span(passes, 2 * PASS)
+            by_slot(copy, u_codes[h][:, cols].bitcast(U16), u_codes_in[h][:, cols].bitcast(U16), LINE // 2)
 
         d_psum = {}
 
         def d_matmul(j, passes):
+            h, t = divmod(j, PACK)
             for g in passes:
                 if g == 0:
                     d_psum[j] = psum_bank("d%d" % j, D_BANKS[j])
                 nc.tensor.matmul_mx(
                     out=d_psum[j][:],
-                    lhsT=u_codes[:, block(SLOTS * g + j, 2 * P)].bitcast(FP4X4),
-                    lhsT_scale=u_scale[:, block(SLOTS * g + j)],
+                    lhsT=u_codes[h][:, block(PACK * g + t, 2 * P)].bitcast(FP4X4),
+                    lhsT_scale=u_scale[h][:, block(PACK * g + t)],
                     rhs=v_codes[:, block(g, 2 * N)].bitcast(FP4X4),
-                    rhs_scale=scale_plane(v_scale, g, N),
+                    rhs_scale=v_scale[:, block(g, N)],
                     start=(g == 0),
                     stop=(g == K_PASSES - 1),
                 )
@@ -225,8 +230,9 @@ def tile_cross_backward_error_s12_kernel(tc, e, x, u_words, u_scales, v_words, v
                 src = e_psum[j, pair][:].rearrange("p (g u r) -> p g r u", g=2, u=2)
                 copy(dst.rearrange("p (g r u) -> p g r u", g=2, u=2), src)
 
-        def quantize_e(j):
-            quantize(e_codes[j][:], e_scale[j][:], e_packed[j % E_STAGES][:])
+        def quantize_e(j, passes=ALL):
+            cols = span(passes, P)
+            quantize(e_codes[j][:, cols], e_scale[j][:, cols], e_packed[j % E_STAGES][:, span(passes, PASS)])
 
         def pack_x(copy, g, cols=slice(0, N)):
             copy(
@@ -247,7 +253,7 @@ def tile_cross_backward_error_s12_kernel(tc, e, x, u_words, u_scales, v_words, v
                         done = r_done.get((h, c), 0)
                         r_done[h, c] = done + 1
                         if done == 0:
-                            r_psum[h, c] = psum_bank("r%d%d" % (h, c), R_BANKS[c])
+                            r_psum[h, c] = psum_bank("r%d%d" % (h, c), R_BANKS[h][c])
                         nc.tensor.matmul_mx(
                             out=r_psum[h, c][:, block(t)],
                             lhsT=e_codes[PACK * h + t][:, block(g)].bitcast(FP8X4),
@@ -280,131 +286,130 @@ def tile_cross_backward_error_s12_kernel(tc, e, x, u_words, u_scales, v_words, v
                 )
             return bank
 
+        def store_out(copy, c, bank):
+            copy(out_rows[c][:], bank[:])
+            nc.sync.dma_start(out=out[block(c), :], in_=out_rows[c][:])
+
         ctx.enter_context(tc.manual_schedule())
 
+        def one(i):
+            return range(i, i + 1)
+
         zero_scale_tile(u_scale_in[0])
+        zero_scale_tile(v_scale)
+        zero_scale_tile(u_scale_in[1])
         make_warm_up_operand()
-        for tile in v_scale:
-            zero_scale_tile(tile)
         make_identity(nc, ident[:])
         load_activation_table()
 
         load_e(0)
+        load_scale_rows(u_scale_in[0], u_scales[:, :, block(0, PASS)])
+        load_u(0, one(0))
         load_e(1)
-        load_scale_rows(u_scale_in, u_scales, 0)
-        load_uv(0)
-        load_scale_rows(v_scale, v_scales, 0)
-        load_uv(1)
-        load_uv(2)
+        load_v(one(0))
+        load_scale_rows(v_scale, v_scales)
+        load_u(0, range(1, 4))
+        load_v(one(1))
+        load_v(HIGH)
+        load_scale_rows(u_scale_in[1], u_scales[:, :, block(1, PASS)])
+        load_u(1, LOW)
         load_x(0)
-        load_uv(3)
         load_b(0, LOW)
+        load_u(1, HIGH)
+        load_e(2)
         load_x(1)
         load_b(0, HIGH)
-        load_e(2)
-        load_b(1, LOW)
         load_e(3)
+        load_b(1, LOW)
         load_x(2)
         load_e(4)
         load_x(3)
         load_b(1, HIGH)
-        for j in range(5, SLOTS):
+        for j in range(5, 8):
             load_e(j)
 
-        for j in LOW:
-            warm_tensor_engine()
-            transpose_e(j)
-            pack_e(scalar_copy, j)
-
-        order_u_scale(0)
-        order_u_codes(vector_copy, 0, range(0, 1))
-        order_u_codes(vector_copy, 0, range(1, 2))
-        order_u_scale(1)
-        order_u_codes(scalar_copy, 1)
+        warm_tensor_engine(WARM_RUNS[0])
+        transpose_e(0)
+        pack_e(scalar_copy, 0)
+        warm_tensor_engine(WARM_RUNS[1])
+        transpose_e(1)
+        pack_e(scalar_copy, 1)
+        order_u_scale(0, ALL)
+        order_u_codes(vector_copy, 0, one(0))
         quantize_e(0)
-        order_u_scale(2)
-        order_u_codes(scalar_copy, 2)
-        order_u_scale(3)
+        order_u_codes(vector_copy, 0, one(1))
+        order_u_codes(scalar_copy, 0, HIGH)
         quantize_e(1)
+        for g in ALL:
+            for t in ALL:
+                d_matmul(t, [g])
+        order_u_scale(1, ALL)
+        order_u_codes(scalar_copy, 1, LOW)
         pack_x(vector_copy, 0)
-        order_u_codes(scalar_copy, 3, range(0, 1))
-        order_u_codes(scalar_copy, 3, range(1, 2))
-        quantize_x(0)
-
-        for g in LOW:
-            for j in range(SLOTS):
-                d_matmul(j, [g])
-        for j in range(PACK + 1):
-            d_matmul(j, [2])
-        for j in ALL:
-            d_matmul(j, [3])
-        d_matmul(PACK, [3])
-        for j in range(PACK + 1, SLOTS):
-            d_matmul(j, HIGH)
-
+        order_u_codes(scalar_copy, 1, one(2))
+        order_u_codes(scalar_copy, 1, one(3))
         add_b(0, LOW)
+        quantize_x(0)
+        rsqrt_d(0, LOW)
+        for g in LOW:
+            for t in ALL:
+                d_matmul(PACK + t, [g])
+        transpose_e(2)
         pack_x(scalar_copy, 1, block(0, N // 2))
+        pack_e(scalar_copy, 2)
+        for t in ALL:
+            d_matmul(PACK + t, HIGH)
         pack_x(vector_copy, 1, block(1, N // 2))
         add_b(0, HIGH)
         quantize_x(1)
-        rsqrt_d(0, LOW)
-
-        transpose_e(2)
-        pack_e(scalar_copy, 2)
-        r_matmul(0, LOW, LOW, LOW)
-        add_b(1, LOW)
-        quantize_e(2)
         rsqrt_d(0, HIGH)
-
         transpose_e(3)
         pack_e(scalar_copy, 3)
-        r_matmul(0, LOW, LOW, HIGH)
-        r_matmul(0, [2], LOW, ALL)
+        quantize_e(2)
+
+        for c in ALL:
+            r_matmul(0, range(3), LOW, [c])
+        add_b(1, LOW)
+        square_on_scalar(0, LOW)
+        rsqrt_d(1, LOW)
+        transpose_e(4)
+        pack_e(scalar_copy, 4)
         pack_x(vector_copy, 2)
         quantize_e(3)
         quantize_x(2)
-        square_on_scalar(0, LOW)
-
-        transpose_e(4)
-        pack_e(scalar_copy, 4)
         r_matmul(0, [3], LOW, ALL)
         r_matmul(0, ALL, [2], ALL)
+
         pack_x(vector_copy, 3)
-        quantize_e(4)
         quantize_x(3)
         add_b(1, HIGH)
+        quantize_e(4)
         square_on_scalar(0, HIGH)
-        rsqrt_d(1, LOW)
-
         transpose_e(5)
         pack_e(scalar_copy, 5)
-        for c in ALL:
-            r_matmul(0, ALL, [3], [c])
-        quantize_w(0)
-        quantize_e(5)
-
-        transpose_e(6)
-        for c in ALL:
-            abs_r(0, c)
-        pack_e(vector_copy, 6)
-        for c in LOW:
-            r_matmul(1, LOW, ALL, [c])
-
-        transpose_e(7)
         rsqrt_d(1, HIGH)
-        quantize_e(6)
+        r_matmul(0, ALL, [3], ALL)
+        quantize_e(5)
+        quantize_w(0)
+
+        for j in LAST_SLOTS:
+            transpose_e(j)
+            pack_e(scalar_copy, j, [0])
+            pack_e(vector_copy, j, [1])
+            abs_r(0, j - LAST_SLOTS.start)
+        for j in LAST_SLOTS:
+            quantize_e(j)
+        for c in HIGH:
+            abs_r(0, c)
+        square_on_vector(1, LOW)
+        square_on_scalar(1, HIGH)
         quantize_r(0, ALL)
-        pack_e(scalar_copy, 7, [0])
-        pack_e(vector_copy, 7, [1])
-        square_on_scalar(1, LOW)
-        r_matmul(1, LOW, ALL, HIGH)
-        quantize_e(7)
-        square_on_vector(1, HIGH)
         quantize_w(1)
 
-        r_matmul(1, [2], ALL, LOW)
+        r_matmul(1, LOW, ALL, LOW)
+        r_matmul(1, LOW, ALL, HIGH)
         for c in ALL:
-            r_matmul(1, [3] if c in LOW else HIGH, ALL, [c])
+            r_matmul(1, HIGH, ALL, [c])
             abs_r(1, c)
             quantize_r(1, range(c, c + 1))
 

from contextlib import ExitStack

import concourse.mybir as mybir
from concourse.masks import make_identity

M, K, N = 1024, 2048, 512
FLOPS = 2 * (2 * M * K * N) + 2 * M * N * N

F32 = mybir.dt.float32
BF16 = mybir.dt.bfloat16
I32 = mybir.dt.int32
U32 = mybir.dt.uint32
U16 = mybir.dt.uint16
U8 = mybir.dt.uint8
FP8X4 = mybir.dt.float8_e4m3fn_x4
FP4X4 = mybir.dt.float4_e2m1fn_x4
FUNC = mybir.ActivationFunctionType
ALU = mybir.AluOpType

P = 128
PACK = 4
PASS = P * PACK
K_PASSES = K // PASS
HALVES = M // PASS
SLOTS = HALVES * PACK
CHUNKS = N // P
BANK = 512
LINE = 16
ALIGN = 64
E_STAGES = 3
WARM_RUNS = (2, 3)

PAIR_A, PAIR_B, PAIR_C, PAIR_D = (0, 1), (2, 3), (4, 5), (6, 7)
D_BANKS = PAIR_C + PAIR_D + PAIR_A + PAIR_B
E_BANKS = (PAIR_A, PAIR_B, PAIR_C, PAIR_D, PAIR_A, PAIR_A, PAIR_B, PAIR_A)
R_BANKS = (PAIR_C + PAIR_D, PAIR_B + PAIR_A)
OUT_BANKS = PAIR_C + PAIR_D
LAST_SLOTS = range(6, 8)
WARM_BANK = D_BANKS[PACK - 1]

LOW, HIGH, ALL = range(0, 2), range(2, 4), range(0, 4)


def block(i, width=P):
    return slice(width * i, width * (i + 1))


def span(indices, width):
    return slice(width * indices.start, width * indices.stop)


def tile_cross_backward_error_s12_kernel(tc, e, x, u_words, u_scales, v_words, v_scales, b_abs, out):
    nc = tc.nc
    with ExitStack() as ctx:
        keep = ctx.enter_context(tc.tile_pool(name="keep", bufs=1))
        psum = ctx.enter_context(tc.psum_pool(name="psum", bufs=1))

        def sbuf(name, shape, dtype):
            return keep.tile(shape, dtype, name=name, align_bytes=ALIGN)

        def sbufs(name, count, shape, dtype):
            return [sbuf("%s%d" % (name, i), shape, dtype) for i in range(count)]

        ident = sbuf("ident", [P, P], F32)
        warm_codes = sbuf("warm_codes", [P, PASS], U32)
        warm_scale = sbuf("warm_scale", [P, PASS], U8)
        table_out = sbuf("table_out", [P, 1], F32)
        e_rows = sbufs("e_rows", SLOTS, [P, K], BF16)
        e_packed = sbufs("e_packed", E_STAGES, [P, K], BF16)
        e_codes = sbufs("e_codes", SLOTS, [P, K_PASSES * P], U32)
        e_scale = sbufs("e_scale", SLOTS, [P, K_PASSES * P], U8)
        x_rows = sbufs("x_rows", K_PASSES, [P, PACK, N], BF16)
        x_packed = sbufs("x_packed", K_PASSES, [P, N, PACK], BF16)
        x_codes = sbufs("x_codes", K_PASSES, [P, N], U32)
        x_scale = sbufs("x_scale", K_PASSES, [P, N], U8)
        u_codes_in = sbufs("u_codes_in", HALVES, [P, K_PASSES * 2 * PASS], U8)
        u_scale_in = sbufs("u_scale_in", HALVES, [P, K_PASSES * PASS], U8)
        u_codes = sbufs("u_codes", HALVES, [P, K_PASSES * 2 * PASS], U8)
        u_scale = sbufs("u_scale", HALVES, [P, K_PASSES * PASS], U8)
        v_codes = sbuf("v_codes", [P, K_PASSES * 2 * N], U8)
        v_scale = sbuf("v_scale", [P, K_PASSES * N], U8)
        b_rows = sbufs("b_rows", HALVES, [P, PACK * N], BF16)
        d_slots = sbufs("d_slots", HALVES, [P, PACK, N], F32)
        d_rsqrt = sbufs("d_rsqrt", HALVES, [P, PACK, N], F32)
        w_packed = sbufs("w_packed", HALVES, [P, N, PACK], BF16)
        w_codes = sbufs("w_codes", HALVES, [P, N], U32)
        w_scale = sbufs("w_scale", HALVES, [P, N], U8)
        r_packed = sbufs("r_packed", HALVES, [P, N, PACK], BF16)
        r_codes = sbufs("r_codes", HALVES, [P, N], U32)
        r_scale = sbufs("r_scale", HALVES, [P, N], U8)
        out_rows = sbufs("out_rows", CHUNKS, [P, N], F32)

        def psum_bank(name, index):
            return psum.tile([P, BANK], F32, name=name, tag="bank%d" % index)

        def quantize(codes, scale, packed):
            nc.vector.quantize_mx(out=codes.bitcast(FP8X4), scales=scale, in_=packed)

        def scalar_copy(dst, src):
            nc.scalar.copy(out=dst, in_=src)

        def vector_copy(dst, src):
            nc.vector.tensor_copy(out=dst, in_=src)

        def load_codes(tile, words, passes):
            width = words.shape[2]
            dst = tile[:, span(passes, width)].rearrange("p (g n) -> p g n", n=width)
            src = words[span(passes, 1)].rearrange("g p n -> p g n")
            nc.sync.dma_start(out=dst.bitcast(I32), in_=src.bitcast(I32))

        def load_u(h, passes):
            load_codes(u_codes_in[h], u_words[:, :, block(h, 2 * PASS)], passes)

        def load_v(passes):
            load_codes(v_codes, v_words, passes)

        def load_scale_rows(tile, rows):
            for r in range(4):
                src = rows[:, r:16:4, :].rearrange("g b n -> b g n")
                dst = tile[r:P:32].rearrange("b (g n) -> b g n", g=K_PASSES)
                nc.sync.dma_start(out=dst.bitcast(I32), in_=src.bitcast(I32))

        def load_b(h, slots):
            rows = b_abs[block(h, PASS), :].rearrange("(p t) n -> p (t n)", t=PACK)
            nc.sync.dma_start(out=b_rows[h][:, span(slots, N)], in_=rows[:, span(slots, N)])

        def load_e(j):
            h, t = divmod(j, PACK)
            nc.sync.dma_start(out=e_rows[j][:], in_=e[h * PASS + t : (h + 1) * PASS : PACK, :])

        def load_x(g):
            nc.sync.dma_start(out=x_rows[g][:], in_=x[block(g, PASS), :].rearrange("(p i) n -> p i n", i=PACK))

        def zero_scale_tile(tile):
            nc.vector.memset(tile[:].bitcast(I32), 0)

        def make_warm_up_operand():
            for i, tile in enumerate((v_scale, u_scale_in[1])):
                cols = block(i, PASS // 2)
                quantize(warm_codes[:, cols], warm_scale[:, cols], tile[:].bitcast(BF16))

        def warm_tensor_engine(passes):
            bank = psum_bank("warm_psum", WARM_BANK)
            for i in range(passes):
                nc.tensor.matmul_mx(
                    out=bank[:],
                    lhsT=warm_codes[:, block(0)].bitcast(FP8X4),
                    lhsT_scale=warm_scale[:, block(0)],
                    rhs=warm_codes[:].bitcast(FP8X4),
                    rhs_scale=warm_scale[:],
                    start=True,
                    stop=True,
                )

        def load_activation_table():
            nc.scalar.activation(out=table_out[:], in_=ident[:, 0:1], func=FUNC.Abs_reciprocal_sqrt, bias=1.0)

        def by_slot(copy, dst, src, per_line):
            copy(
                dst.rearrange("p (h t c i) -> p h c t i", t=PACK, c=P // per_line, i=per_line),
                src.rearrange("p (h c i t) -> p h c t i", t=PACK, c=P // per_line, i=per_line),
            )

        def order_u_scale(h, passes):
            cols = span(passes, PASS)
            by_slot(vector_copy, u_scale[h][:, cols], u_scale_in[h][:, cols], LINE)

        def order_u_codes(copy, h, passes):
            cols = span(passes, 2 * PASS)
            by_slot(copy, u_codes[h][:, cols].bitcast(U16), u_codes_in[h][:, cols].bitcast(U16), LINE // 2)

        d_psum = {}

        def d_matmul(j, passes):
            h, t = divmod(j, PACK)
            for g in passes:
                if g == 0:
                    d_psum[j] = psum_bank("d%d" % j, D_BANKS[j])
                nc.tensor.matmul_mx(
                    out=d_psum[j][:],
                    lhsT=u_codes[h][:, block(PACK * g + t, 2 * P)].bitcast(FP4X4),
                    lhsT_scale=u_scale[h][:, block(PACK * g + t)],
                    rhs=v_codes[:, block(g, 2 * N)].bitcast(FP4X4),
                    rhs_scale=v_scale[:, block(g, N)],
                    start=(g == 0),
                    stop=(g == K_PASSES - 1),
                )

        def add_b(h, slots):
            for t in slots:
                nc.vector.tensor_tensor(
                    out=d_slots[h][:, t, :], in0=d_psum[PACK * h + t][:], in1=b_rows[h][:, block(t, N)], op=ALU.add
                )

        def rsqrt_d(h, slots):
            nc.scalar.activation(
                out=d_rsqrt[h][:, span(slots, 1), :], in_=d_slots[h][:, span(slots, 1), :], func=FUNC.Abs_reciprocal_sqrt
            )

        def square_operands(h, chunks):
            src = d_rsqrt[h][:, :, span(chunks, P)].rearrange("p t (c i) -> p c t i", i=2)
            dst = w_packed[h][:, span(chunks, P), :].rearrange("p (c i) t -> p c t i", i=2)
            return dst, src

        def square_on_scalar(h, chunks):
            dst, src = square_operands(h, chunks)
            nc.scalar.activation(out=dst, in_=src, func=FUNC.Square)

        def square_on_vector(h, chunks):
            dst, src = square_operands(h, chunks)
            nc.vector.tensor_tensor(out=dst, in0=src, in1=src, op=ALU.mult)

        def quantize_w(h):
            quantize(w_codes[h][:], w_scale[h][:], w_packed[h][:].rearrange("p n t -> p (n t)"))

        e_psum = {}

        def transpose_e(j):
            words = e_rows[j][:].bitcast(F32).rearrange("p (g w u) -> p g u w", g=K_PASSES, u=2)
            for pair in range(2):
                bank = psum_bank("e%d%d" % (j, pair), E_BANKS[j][pair])
                e_psum[j, pair] = bank
                for gg in range(2):
                    for u in range(2):
                        nc.tensor.transpose(bank[:, block(2 * gg + u)], words[:, 2 * pair + gg, u, :], ident[:])

        def pack_e(copy, j, pairs=range(2)):
            for pair in pairs:
                dst = e_packed[j % E_STAGES][:, block(pair, K // 2)].bitcast(F32)
                src = e_psum[j, pair][:].rearrange("p (g u r) -> p g r u", g=2, u=2)
                copy(dst.rearrange("p (g r u) -> p g r u", g=2, u=2), src)

        def quantize_e(j, passes=ALL):
            cols = span(passes, P)
            quantize(e_codes[j][:, cols], e_scale[j][:, cols], e_packed[j % E_STAGES][:, span(passes, PASS)])

        def pack_x(copy, g, cols=slice(0, N)):
            copy(
                x_packed[g][:, cols, :].rearrange("p (c a) i -> p c i a", a=4),
                x_rows[g][:, :, cols].rearrange("p i (c a) -> p c i a", a=4),
            )

        def quantize_x(g):
            quantize(x_codes[g][:], x_scale[g][:], x_packed[g][:].rearrange("p n i -> p (n i)"))

        r_psum = {}
        r_done = {}

        def r_matmul(h, slots, passes, chunks):
            for t in slots:
                for g in passes:
                    for c in chunks:
                        done = r_done.get((h, c), 0)
                        r_done[h, c] = done + 1
                        if done == 0:
                            r_psum[h, c] = psum_bank("r%d%d" % (h, c), R_BANKS[h][c])
                        nc.tensor.matmul_mx(
                            out=r_psum[h, c][:, block(t)],
                            lhsT=e_codes[PACK * h + t][:, block(g)].bitcast(FP8X4),
                            lhsT_scale=e_scale[PACK * h + t][:, block(g)],
                            rhs=x_codes[g][:, block(c)].bitcast(FP8X4),
                            rhs_scale=x_scale[g][:, block(c)],
                            start=(done == 0),
                            stop=(done == PACK * K_PASSES - 1),
                        )

        def abs_r(h, c):
            src = r_psum[h, c][:].rearrange("p (t n) -> p n t", t=PACK)
            nc.scalar.activation(out=r_packed[h][:, block(c), :], in_=src, func=FUNC.Abs)

        def quantize_r(h, chunks):
            cols = span(chunks, P)
            quantize(r_codes[h][:, cols], r_scale[h][:, cols], r_packed[h][:, cols, :].rearrange("p n t -> p (n t)"))

        def out_matmul(c):
            bank = psum_bank("out%d" % c, OUT_BANKS[c])
            for h in range(HALVES):
                nc.tensor.matmul_mx(
                    out=bank[:],
                    lhsT=r_codes[h][:, block(c)].bitcast(FP8X4),
                    lhsT_scale=r_scale[h][:, block(c)],
                    rhs=w_codes[h][:].bitcast(FP8X4),
                    rhs_scale=w_scale[h][:],
                    start=(h == 0),
                    stop=(h == HALVES - 1),
                )
            return bank

        def store_out(copy, c, bank):
            copy(out_rows[c][:], bank[:])
            nc.sync.dma_start(out=out[block(c), :], in_=out_rows[c][:])

        ctx.enter_context(tc.manual_schedule())

        def one(i):
            return range(i, i + 1)

        zero_scale_tile(u_scale_in[0])
        zero_scale_tile(v_scale)
        zero_scale_tile(u_scale_in[1])
        make_warm_up_operand()
        make_identity(nc, ident[:])
        load_activation_table()

        load_e(0)
        load_scale_rows(u_scale_in[0], u_scales[:, :, block(0, PASS)])
        load_u(0, one(0))
        load_e(1)
        load_v(one(0))
        load_scale_rows(v_scale, v_scales)
        load_u(0, range(1, 4))
        load_v(one(1))
        load_v(HIGH)
        load_scale_rows(u_scale_in[1], u_scales[:, :, block(1, PASS)])
        load_u(1, LOW)
        load_x(0)
        load_b(0, LOW)
        load_u(1, HIGH)
        load_e(2)
        load_x(1)
        load_b(0, HIGH)
        load_e(3)
        load_b(1, LOW)
        load_x(2)
        load_e(4)
        load_x(3)
        load_b(1, HIGH)
        for j in range(5, 8):
            load_e(j)

        warm_tensor_engine(WARM_RUNS[0])
        transpose_e(0)
        pack_e(scalar_copy, 0)
        warm_tensor_engine(WARM_RUNS[1])
        transpose_e(1)
        pack_e(scalar_copy, 1)
        order_u_scale(0, ALL)
        order_u_codes(vector_copy, 0, one(0))
        quantize_e(0)
        order_u_codes(vector_copy, 0, one(1))
        order_u_codes(scalar_copy, 0, HIGH)
        quantize_e(1)
        for g in ALL:
            for t in ALL:
                d_matmul(t, [g])
        order_u_scale(1, ALL)
        order_u_codes(scalar_copy, 1, LOW)
        pack_x(vector_copy, 0)
        order_u_codes(scalar_copy, 1, one(2))
        order_u_codes(scalar_copy, 1, one(3))
        add_b(0, LOW)
        quantize_x(0)
        rsqrt_d(0, LOW)
        for g in LOW:
            for t in ALL:
                d_matmul(PACK + t, [g])
        transpose_e(2)
        pack_x(scalar_copy, 1, block(0, N // 2))
        pack_e(scalar_copy, 2)
        for t in ALL:
            d_matmul(PACK + t, HIGH)
        pack_x(vector_copy, 1, block(1, N // 2))
        add_b(0, HIGH)
        quantize_x(1)
        rsqrt_d(0, HIGH)
        transpose_e(3)
        pack_e(scalar_copy, 3)
        quantize_e(2)

        for c in ALL:
            r_matmul(0, range(3), LOW, [c])
        add_b(1, LOW)
        square_on_scalar(0, LOW)
        rsqrt_d(1, LOW)
        transpose_e(4)
        pack_e(scalar_copy, 4)
        pack_x(vector_copy, 2)
        quantize_e(3)
        quantize_x(2)
        r_matmul(0, [3], LOW, ALL)
        r_matmul(0, ALL, [2], ALL)

        pack_x(vector_copy, 3)
        quantize_x(3)
        add_b(1, HIGH)
        quantize_e(4)
        square_on_scalar(0, HIGH)
        transpose_e(5)
        pack_e(scalar_copy, 5)
        rsqrt_d(1, HIGH)
        r_matmul(0, ALL, [3], ALL)
        quantize_e(5)
        quantize_w(0)

        for j in LAST_SLOTS:
            transpose_e(j)
            pack_e(scalar_copy, j, [0])
            pack_e(vector_copy, j, [1])
            abs_r(0, j - LAST_SLOTS.start)
        for j in LAST_SLOTS:
            quantize_e(j)
        for c in HIGH:
            abs_r(0, c)
        square_on_vector(1, LOW)
        square_on_scalar(1, HIGH)
        quantize_r(0, ALL)
        quantize_w(1)

        r_matmul(1, LOW, ALL, LOW)
        r_matmul(1, LOW, ALL, HIGH)
        for c in ALL:
            r_matmul(1, HIGH, ALL, [c])
            abs_r(1, c)
            quantize_r(1, range(c, c + 1))

        for c in ALL:
            copy = vector_copy if c % 2 else scalar_copy
            copy(out_rows[c][:], out_matmul(c)[:])
            nc.sync.dma_start(out=out[block(c), :], in_=out_rows[c][:])
